import numpy as np, ml_dtypes
CORES = [8,136,40,168]
N = 4
BF = ml_dtypes.bfloat16
def gentries(a):
    return np.ascontiguousarray(a.reshape(8, 16, -1).transpose(0, 2, 1)).reshape(8, -1)
def gtable(e):
    e = np.asarray(e); return np.ascontiguousarray(e.reshape(8, -1, 16).transpose(0, 2, 1)).reshape(128, -1).astype(np.int32)
V, K, B, CAP, E0, EC, RO = 768, 8, 96, 96, 1536, 384, 3
E = E0 + RO * EC
JJ, KK = np.triu_indices(K, 1)
def turn(ends):
    f = ends.reshape(-1); o = np.argsort(f, kind="stable"); s = f[o]; r = np.empty(len(f), np.int64); r[o] = np.arange(len(f)) - np.searchsorted(s, s)
    return r.reshape(-1, 2)
def place(rng, a, b):
    a = np.concatenate(a); b = np.concatenate(b); lo = np.minimum(a, b); hi = np.maximum(a, b)
    first = np.sort(np.unique(lo * V + hi, return_index=True)[1]); first = first[lo[first] != hi[first]]
    ends = np.stack([lo[first], hi[first]], 1); ends = ends[np.all(turn(ends) < K, axis=1)][:E0]
    slot = np.argsort(rng.random((V, K)), axis=1)[ends, turn(ends)]
    name = rng.permutation(np.concatenate([np.array([0, E0 - 1]), rng.permutation(np.arange(1, E0 - 1))[:len(ends) - 2]]))
    nb = np.full((V, K), -1); en = np.full((V, K), -1); nb[ends, slot] = ends[:, ::-1]; en[ends, slot] = name[:, None]
    return nb, en
def world(rng, make):
    pl = np.argsort(rng.random((N, 8, B)), axis=-1)
    got = [[place(rng, *make(q, g, pl[q - 1, g], pl[q, g])) for g in range(8)] for q in range(N)]
    return np.array([[h[0] for h in r] for r in got]), np.array([[h[1] for h in r] for r in got])
def seam(first, last, lo, hi):
    i = np.arange(lo, hi - 1)
    return np.concatenate([first[i], last[i] + V - B]), np.concatenate([first[i + 1], last[i + 1] + V - B])
def roads(rng, share, first, last):
    n = V - 2 * B; p = B + rng.permutation(n); t = rng.permutation(n); h = 3 * B // 4; i = 4 * np.arange(8); j = i + 33
    a = [last[i] + V - B, first[i], first[j], last[j] + V - B]; b = [last[i + 2], first[i + 2], first[j + 2] + V - B, last[j + 2] + V - B]
    for w in (first, last + V - B):
        for d, c in ((1, 0.85), (3, 0.5)):
            i = np.flatnonzero(rng.random(B - d) < c); a.append(w[i]); b.append(w[i + d])
    for s, w in enumerate((first, last + V - B)):
        c = p[t[s * h:(s + 1) * h]]; i = rng.permutation(B - 1)[:h]; a += [c, c]; b += [w[i], w[i + 1]]
    m = int(share * 1.3 * (E0 - len(np.concatenate(a)))); i = (n * rng.random(m) ** 1.5).astype(np.int64)
    a.append(p[i]); b.append(p[(i + rng.integers(1, 7, m)) % n])
    return a, b
def shares(rng):
    return np.stack([rng.permutation(np.repeat(np.array([0.25, 0.5, 0.75, 1.0]), 2)) for q in range(N)])
def tri(t):
    out = []; c = K
    while t > 0:
        while c * (c - 1) // 2 > t: c -= 1
        out.append(c); t -= c * (c - 1) // 2
    return out
def hubs(rng, iso, t, first, last):
    a, b = [], []; v = B + iso; use = [0, 0]
    for i, c in enumerate(tri(t)):
        s = i % 2
        if use[s] + c > B: s = 1 - s
        w = (first, last + V - B)[s][use[s]:use[s] + c]; use[s] += c
        a.append(np.full(len(w), v)); b.append(w); v += 1
    for i in range(CAP // 4):
        m = v + np.arange(5); a.append(m); b.append(np.roll(m, 1)); v += 5
    r = rng.permutation(np.arange(v, V - B)); r = r[:len(r) // 5 * 5].reshape(-1, 5); i, j = np.triu_indices(5, 1)
    a.append(r[:, i].reshape(-1)); b.append(r[:, j].reshape(-1)); x, y = seam(first, last, B - 8, B); a.append(x); b.append(y)
    return a, b
def fives(rng, n, first, last):
    a, b = [], []
    for i, c in enumerate(np.array_split(B + rng.permutation(V - 2 * B), n)):
        m = len(c)
        if i % 3 == 0: x, y = np.triu_indices(m, 1); a.append(c[x]); b.append(c[y])
        elif i % 3 == 1: a.append(np.full(m - 1, c[0])); b.append(c[1:])
        else: a.append(np.repeat(c[:2], m - 2)); b.append(np.tile(c[2:], 2))
        w = (first, last + V - B)[i % 2][i // 2 * 2:i // 2 * 2 + 2]; a.append(np.full(len(w), c[0])); b.append(w)
    x, y = seam(first, last, 0, B); a.append(x); b.append(y)
    return a, b
def full(rng, first, last):
    n = min((E0 - 2 * B) // (K * K), (V - 2 * B) // (2 * K)); p = (B + rng.permutation(n * 2 * K)).reshape(n, 2, K); x, y = seam(first, last, 0, B)
    return [np.repeat(p[:, 0], K, axis=1).reshape(-1), x], [np.tile(p[:, 1], (1, K)).reshape(-1), y]
def knots(rng):
    n = min(E0 // (K * (K + 1) // 2), (V - 2 * B) // (K + 1)); p = (B + rng.permutation(n * (K + 1))).reshape(n, K + 1); x, y = np.triu_indices(K + 1, 1)
    return [p[:, x].reshape(-1)], [p[:, y].reshape(-1)]
def stuffed(rng, first, last):
    h = B // K; n = min((E0 - 2 * h * K) // (K * (K + 1) // 2), (V - 2 * B - 2 * h) // (K + 1)); z = n * K; i = np.arange(z)
    c = B + rng.permutation(n); v = B + n + rng.permutation(2 * h); p = B + n + 2 * h + rng.permutation(z); w = np.concatenate([first[:h * K], last[:h * K] + V - B])
    a = [np.repeat(v, K), c[i % n], p[::2]]; b = [w, p, p[(i[::2] + K - 1) % z]]
    for d in range(1, K // 2): a.append(p); b.append(p[(i + d) % z])
    return a, b
def around(w):
    d = np.arange(1, K // 2 + 1)[:, None]; i = np.arange(B)[None, :]
    return np.tile(w, K // 2), w[(i + d) % B].reshape(-1)
def rims(rng, shift, first, last):
    r = B + rng.permutation(V - 2 * B); r = r[:len(r) // 5 * 5].reshape(-1, 5)
    x, y = around((first + shift) % B); s, t = around(last + V - B)
    return [x, s, r.reshape(-1)], [y, t, np.roll(r, 1, axis=1).reshape(-1)]
def small(rng, start, first, last):
    n = V - 2 * B; p = B + rng.permutation(n); i = np.arange(1, n); far = np.maximum(i - rng.integers(1, 4, n - 1), 0); on = rng.random(n - 1) >= start
    a, b = [p[i][on]], [p[far][on]]; x, y = seam(first, last, 0, B); a.append(x); b.append(y); h = B // 4; t = rng.permutation(n)
    for s, w in enumerate((first, last + V - B)):
        c = p[t[s * h:(s + 1) * h]]; a += [c, c]; b += [w[0:2 * h:2], w[1:2 * h:2]]
    return a, b
def which(nb, en):
    bl = np.full(V + 1, 2); bl[:B] = 0; bl[V - B:V] = 1; bl[V] = 3; own = bl[:V][None, None, :, None]
    q, g, v, k = np.nonzero((bl[nb] == own) & (own < 2)); m = np.full((N, 8, E0), -1); m[q, g, en[q, g, v, k]] = bl[v]
    return m[:, :, None, :]
def usual(rng, nb, en):
    v = np.clip(np.exp2(2 + 5.5 * rng.random((N, 8, 1, E0))) * (0.5 + rng.random((N, 8, 16, E0))), 1, 255).astype(np.int64)
    near = np.where(rng.random((1, 8, 1, 1)) < 0.5, rng.integers(15, 60, v.shape), 20 + 10 * rng.integers(0, 3, v.shape))
    return np.where(which(nb, en) >= 0, near, v)
def pack(v, nb, en):
    return {"lens": np.ascontiguousarray(v.reshape(N, 128, E0)).astype(np.float32).astype(BF), "en": np.stack([gtable(a.transpose(0, 2, 1).reshape(8, -1)) for a in en]),
            "nb": np.stack([gtable(a.transpose(0, 2, 1).reshape(8, -1)) for a in nb])}
def setup_inputs(rng):
    sh = shares(rng); nb, en = world(rng, lambda q, g, first, last: roads(rng, sh[q, g], first, last))
    return pack(usual(rng, nb, en), nb, en)
def setup_inputs_spread(rng):
    sh = shares(rng); nb, en = world(rng, lambda q, g, first, last: roads(rng, sh[q, g], first, last))
    return pack(np.clip(np.exp2(8 * rng.random((N, 8, 1, E0))) * rng.random((N, 8, 16, E0)), 1, 255).astype(np.int64), nb, en)
def setup_inputs_ends(rng):
    sh = shares(rng)
    def make(q, g, first, last):
        if g % 2:
            a, b = hubs(rng, CAP * (1 + (g // 2 + q + 1) % (RO - 1)), EC - CAP // 4 + 3 * len(JJ), first, last); far = [[0, V - 1]]
        else:
            a, b = roads(rng, sh[q, g], first, last); far = [[0, V - 1], [B, V - B - 1], [0, B], [V - 1, V - B - 1], [0, V - B - 1], [V - 1, B]]
        far = np.array(far); return [far[:, 0]] + a, [far[:, 1]] + b
    nb, en = world(rng, make); pr = rng.choice(np.array([0.0, 0.25, 0.75, 0.75, 0.9, 1.0]), (N, 8, 1, E0))
    return pack(np.where(rng.random((N, 8, 16, E0)) < pr, 1, 255), nb, en)
def setup_inputs_corners(rng):
    c4 = CAP // 4
    def make(q, g, first, last):
        c = (q + g) % 8
        if c < 4: return hubs(rng, 0, EC - c4 + (0, -1, 1, 3 * len(JJ))[c], first, last)
        if c == 4: return hubs(rng, CAP * (RO - 1), EC - c4, first, last)
        return fives(rng, CAP + (0, -1, 1)[c - 5], first, last)
    nb, en = world(rng, make)
    return pack(usual(rng, nb, en), nb, en)
def setup_inputs_crowd(rng):
    def make(q, g, first, last):
        if g >= 6: return rims(rng, g - 6, first, last)
        if g == 3: return stuffed(rng, first, last)
        if g == 4: return knots(rng)
        if g % 3 == 0: return full(rng, first, last)
        if g % 3 == 1: return fives(rng, CAP, first, last)
        return hubs(rng, 0, EC - CAP // 4 + 3 * len(JJ), first, last)
    nb, en = world(rng, make); w = which(nb, en); r = np.argsort(rng.random((1, 8, 16, 1)), axis=2)
    c = rng.choice(np.array([0, 1, 7, 8, 9, 10, 15, 16]), (N, 8, 1, E0))
    for q in range(0, N, 2):
        for s, k in ((q, 1), ((q + 1) % N, 0)):
            c[s, 6] = np.where(w[s, 6] == k, rng.integers(0, 2, (1, E0)) + 7 * int(k == 1 - q // 2 % 2), c[s, 6])
    side = 20 + (r < c)
    return pack(np.where((rng.random((N, 8, 1, E0)) < 0.5) & (w < 0), 10, side), nb, en)
def setup_inputs_calm(rng):
    st = np.stack([rng.permutation(np.array([0.05, 0.1, 0.15, 0.2, 0.25, 0.35, 0.5, 0.7])) for q in range(N)])
    nb, en = world(rng, lambda q, g, first, last: small(rng, st[q, g], first, last))
    return pack(rng.integers(1, 5, (N, 8, 16, E0)), nb, en)
def check_inputs(d):
    bad = []
    for k, lo, hi in (("lens", 1, 255), ("en", -1, E0 - 1), ("nb", -1, V - 1)):
        a = np.asarray(d[k]).astype(np.float64)
        if not (np.all(a >= lo) and np.all(a <= hi)): bad.append("range of " + k)
        elif not np.all(a == np.floor(a)): bad.append("whole numbers of " + k)
    if bad: return bad
    for q in range(N):
        nl = gentries(np.asarray(d["nb"][q])).astype(np.int64); el = gentries(np.asarray(d["en"][q])).astype(np.int64)
        for g in range(8):
            n, e = nl[g], el[g]; f = np.flatnonzero(e >= 0)
            if np.any((n >= 0) != (e >= 0)): bad.append("empty slots alike in en and nb"); continue
            v = f % V; u = n[f]; o = np.argsort(e[f], kind="stable"); s = e[f][o]
            if len(s) % 2 or np.any(s[0::2] != s[1::2]) or np.any(s[2::2] == s[1:-1:2]): bad.append("every edge in two slots"); continue
            a, b = o[0::2], o[1::2]
            if np.any(v[a] != u[b]) or np.any(v[b] != u[a]): bad.append("ends of an edge name each other")
            if np.any(v[a] == v[b]): bad.append("two different ends")
            if len(np.unique(np.minimum(v[a], v[b]) * V + np.maximum(v[a], v[b]))) != len(a): bad.append("no two edges between the same vertices")
    return sorted(set(bad))
def contract(nb, en, x, mid, live, t):
    me = np.arange(V); big = (K + 1) * V; deg = np.add.reduce((nb >= 0).astype(np.int64), axis=1)
    key = np.where(live & (me >= B) & (me < V - B), deg * V + me, big); m = key
    for hop in range(2): m = np.minimum(m, np.min(np.append(m, big)[nb], axis=1))
    go = np.flatnonzero((m == key) & (key < big))[:CAP]
    un, ue = nb[go], en[go]; u, w = un[:, JJ], un[:, KK]; ok = (u >= 0) & (w >= 0)
    z = np.minimum(x[:, ue[:, JJ]] + x[:, ue[:, KK]], 255)
    same = (nb[u] == w[..., None]) & ok[..., None]; has = np.any(same, axis=2); side = np.max(np.where(same, en[u], -1), axis=2)
    a, p = np.nonzero(has); zz = z[:, a, p]; e = side[a, p]; old = x[:, e]
    win = np.add.reduce((zz < old).astype(np.int64), axis=0) >= 9
    x[:, e] = np.minimum(zz, old); mid[e[win]] = go[a[win]]
    live[go] = False; dead = np.zeros(V + 1, bool); dead[go] = True; hit = dead[nb]
    nb[hit] = -1; en[hit] = -1; nb[go] = -1; en[go] = -1
    new = ok & ~has; s = np.zeros((len(go), K, K), np.int64); s[:, JJ, KK] = new; s[:, KK, JJ] = new
    before = np.add.accumulate(s, axis=2) - s; free = nb[un] < 0
    fits = before < np.add.reduce(free.astype(np.int64), axis=2)[..., None]
    given = np.take_along_axis(np.argsort(~free, axis=2, kind="stable"), before, 2)
    a, p = np.nonzero(new & fits[:, JJ, KK] & fits[:, KK, JJ]); a, p = a[:EC], p[:EC]; j, k = JJ[p], KK[p]; e = E0 + EC * t + np.arange(len(a))
    x[:, e] = z[:, a, p]; mid[e] = go[a]
    u, w = un[a, j], un[a, k]; nb[u, given[a, j, k]] = w; en[u, given[a, j, k]] = e; nb[w, given[a, k, j]] = u; en[w, given[a, k, j]] = e
def meet(nr, er, xr, ns, es, xs):
    far = nr[V - B:] - (V - B); same = (far[:, :, None] == ns[:B][:, None, :]) & (far >= 0)[:, :, None]
    a, l, m = np.nonzero(same); e = er[V - B + a, l]; f = es[a, m]; p = xr[:, e]; o = xs[:, f]
    xr[:, e] = np.minimum(p, o); xs[:, f] = np.minimum(p, o)
    c = np.add.reduce((p > o).astype(np.int64), axis=0) >= 9; nr[V - B + a[c], l[c]] = -1; er[V - B + a[c], l[c]] = -1
    c = np.add.reduce((o > p).astype(np.int64), axis=0) >= 9; ns[a[c], m[c]] = -1; es[a[c], m[c]] = -1
def reference(lens, en, nb):
    fn = np.ascontiguousarray(np.stack([gentries(a) for a in nb]).astype(np.int64).reshape(N, 8, K, V).transpose(0, 1, 3, 2))
    fe = np.ascontiguousarray(np.stack([gentries(a) for a in en]).astype(np.int64).reshape(N, 8, K, V).transpose(0, 1, 3, 2))
    x = np.zeros((N, 8, 16, E), np.int64); x[..., :E0] = lens.astype(np.float32).astype(np.int64).reshape(N, 8, 16, E0)
    mid = np.full((N, 8, E), -1, np.int64); live = np.ones((N, 8, V), bool)
    for t in range(RO):
        for q in range(N):
            for g in range(8): contract(fn[q, g], fe[q, g], x[q, g], mid[q, g], live[q, g], t)
        for q in range(N):
            s = (q + 1) % N
            for g in range(8): meet(fn[q, g], fe[q, g], x[q, g], fn[s, g], fe[s, g], x[s, g])
    return {"ylen": x.reshape(N, 128, E).astype(np.float32).astype(BF), "ymid": mid.astype(np.float32),
            "yen": fe.transpose(0, 1, 3, 2).reshape(N, 8, K * V).astype(np.float32), "ynb": fn.transpose(0, 1, 3, 2).reshape(N, 8, K * V).astype(np.float32)}

@@ -1,0 +1,668 @@
+import numpy as np
+from concourse.bass import DstId, RemoteDMATransfer
+from concourse.mybir import AluOpType as A, AxisListType as AX, ActivationFunctionType as F
+
+F32, BF, I32, U16 = "float32", "bfloat16", "int32", "uint16"
+RK = F32
+SOFT_SAME = True
+SB = dict(
+    xw=(3488, BF), RR=(2400, BF), Rs=(768, I32), nbw=(384, I32), enw=(384, I32), i1=(864, I32), i2=(384, I32), i3=(384, I32),
+    EO=(384, U16), EW=(3840, BF), LA=(168, U16), LB=(168, U16), W=(384, U16), SL=(48, U16), XL=(8, U16),
+    lo8=(800, BF), hi8=(800, BF), Tc=(800, F32), NM=(1152, BF), b1=(800, BF), b2=(800, BF), b3=(800, BF),
+    PC=(128, F32), PI=(64, I32), CMx=(144, BF), CH=(128, BF), CO=(192, F32), MZ=(144 * 20, BF), M=(128 * 56, BF), ZO=(192, BF),
+    MF=(128, F32), MR=(128, RK), PAT=(224, BF), cod=(64, BF), pu=(192, BF), jk=(64, I32),
+    fil=(576, BF), dead=(576, BF), ind=(576, BF), cumd=(576, F32), f1=(576, F32), rk=(576, RK), val=(800, BF), G1=(6144, BF), S1=(800, BF),
+    sg=(576, BF), cho=(576, BF), cumc=(592, BF), c96=(576, BF), ctr=(576, BF), junk=(576, BF), junk2=(576, BF), vc=(16, F32), vd=(16, F32), VL=(18, U16),
+    Rv=(288, BF), fv=(96, BF), UL=(144, U16), Us=(48, U16), s1=(96, F32), s2=(96, F32), s3=(96, F32), pos=(48, F32), pk=(192, F32),
+    Lf=(768, F32), tg=(768, F32), Aw=(1568, F32), Ac=(800, F32), Tt=(800, F32), T2=(800, F32), Bw=(800, F32), keep=(768, BF), Kn=(768, BF), Ke=(768, BF),
+    G=(768, BF), EQ=(2304, BF), wish=(192, BF), nf=(96, BF), Nw=(400, BF), fw=(384, BF), ok=(192, BF), cumb=(208, F32), c884=(192, F32),
+    num=(208, F32), big=(384, BF), ws=(192, F32), we=(192, F32), ZL=(12, U16), Z=(1728, BF), ids=(192, BF), mx=(384, BF), wr=(384, BF), CL=(24, U16),
+    im=(384, F32), oh=(384, BF), pr=(768, BF), j1=(48, I32), j2=(48, I32), j3=(48, I32), IL=(48, U16), W2=(1600, BF), J8=(768, BF), G2=(768, BF), e2=(768, BF),
+    AL=(48, U16), Aux=(6912 * 3, BF), ga=(2688, F32), zf=(2304, F32), zn=(384, F32), zb=(2304, BF), ix=(2688, BF), own=(168, F32), mid=(168, F32),
+    m1=(168, I32), m2=(168, F32), m3=(168, F32),
+    snd=(432 * 6, U16), lnd=(432 * 6, U16), Eb=(96, U16), nbs=(96, F32), Ebf=(96, F32), slf=(96, F32), dum=(96, F32), thr=(96, F32), can=(96, F32), q1=(96, F32),
+    SS=(96, U16), PL=(96, U16), pc8=(96, F32), Go=(1536, BF), Pw=(1552, I32), par=(96, BF), eqs=(768, BF), si=(1536, BF), mn=(1536, BF), sn=(1536, BF),
+    ks=(192, BF), O=(768, F32),
+)
+SB.update(Aux=(6912, BF), EW=(3840, F32), gz=(4224, F32), zf=(1536, F32), zb=(1536, BF), nbK=(768, F32), Zr=(1536, BF), Zf=(384, F32), ZE=(144, F32),
+          Vf=(768, F32), ab=(768, BF), rl=(768, BF), QL=(6, U16), junk=(288, BF), junk2=(160, BF), id1=(96, BF))
+for _k in ("T2", "keep", "ctr"):
+    SB.pop(_k)
+ALIAS = dict(ga=("gz", 0), zf=("gz", 2688), EW=("gz", 0), Vf=("O", 0), b1=("si", 0), b2=("sn", 0), b3=("mn", 0), lo8=("Go", 0), hi8=("G1", 4608),
+             Rs=("Pw", 0), nbw=("Pw", 768), enw=("Pw", 1152), CO=("tg", 0), Zf=("zn", 0))
+LOC, SCRATCH = {}, {}
+for _d in (F32, BF, I32, U16):
+    _n, _o = 0, 0
+    for _k, (_w, _e) in SB.items():
+        if _e != _d or _k in ALIAS: continue
+        if _o + _w > 16384: _n, _o = _n + 1, 0
+        LOC[_k] = ("%s%d" % (_d[0], _n), _o); _o += (_w + 31) // 32 * 32
+        SCRATCH[LOC[_k][0]] = ("sbuf", [128, _o], _d)
+for _k, (_b, _o) in ALIAS.items():
+    LOC[_k] = (LOC[_b][0], LOC[_b][1] + _o)
+
+
+def S(T, n, a, b, rows=slice(None)):
+    return T[LOC[n][0]][rows, LOC[n][1] + a:LOC[n][1] + b]
+
+
+ACT_EQ = (1,)
+SPL = [2, 4]
+XACT = [0, 0, 0]
+HV = [8, 6, 8, 6, 8, 6]
+BIASES, PASSES, JIT = ((300.0, 0), (1000.0, 0), (2500.0, 0)), 5, 3000.0
+for _k in range(4):
+    SCRATCH["P%d" % _k] = ("psum", [128, 1024], F32)
+NDMA = 24
+SEMAPHORES = ["ev", "ea", "ep", "eg", "ax"] + ["d%d" % k for k in range(NDMA)] + ["r0", "r1", "r2", "r3", "l0", "l1", "l2", "l3"]
+CYC = 1.04
+GAT, SCA, PEC = 1.56, 3.8, 0.6
+
+
+def V(n, a, b, s=1):
+    return (n, a, b, s, None)
+
+
+def IND(n, a, b, off):
+    return (n, a, b, 1, off)
+
+
+def wid(v):
+    return 16 * wid(v[4]) if v[4] else len(range(v[1], v[2], v[3]))
+
+
+def two(v):
+    return v[0] in SB and SB[v[0]][1] in (BF, U16)
+
+
+def program():
+    ops = []
+
+    def add(engs, fn, rd, wr, cost, kind="c", lat=0.0):
+        r = []
+        for v in rd:
+            if isinstance(v, tuple):
+                r.append(v)
+                if v[4]: r.append(v[4])
+        w = []
+        for v in wr:
+            w.append(v)
+            if v[4]: r.append(v[4])
+        ops.append(dict(engs=engs, fn=fn, rd=r, wr=w, cost=cost, kind=kind, lat=lat))
+
+    def el(o, i, base):
+        if o[4]: return SCA * wid(o)
+        if i[4]: return GAT * wid(o)
+        return base * wid(o)
+
+    def ts(o, i, s1, s2, op0, op1=None):
+        def fn(q, e, ap):
+            if op1 is None: return q.tensor_scalar(ap(o), ap(i), ap(s1), None, op0)
+            return q.tensor_scalar(ap(o), ap(i), ap(s1), ap(s2), op0, op1)
+        add("v", fn, [i, s1, s2], [o], 60 + CYC * el(o, i, 0.5 if two(o) and two(i) else 1))
+
+    def tt(o, a, b, op):
+        ps = a[0][0] == "P" and a[0] not in SB or b[0] not in SB
+        base = 1 if ps else (1.5 if two(o) and two(a) and two(b) else 2)
+        add("v", lambda q, e, ap: q.tensor_tensor(ap(o), ap(a), ap(b), op), [a, b], [o], 60 + CYC * el(o, a, base))
+
+    def cp(o, i, engs="v"):
+        def fn(q, e, ap):
+            if e == "v": return q.tensor_copy(ap(o), ap(i))
+            return q.activation(ap(o), ap(i), F.Copy)
+        add(engs, fn, [i], [o], 60 + CYC * el(o, i, 0.5 if two(o) and two(i) and engs == "v" else 1))
+
+    def act(o, i, f, bias=0.0, scale=1.0, acc=None, alt=None):
+        def fn(q, e, ap):
+            if e == "v": return alt(q, ap)
+            if acc: return q.activation(ap(o), ap(i), f, bias=ap(bias), scale=ap(scale), accum_out=ap(acc))
+            return q.activation(ap(o), ap(i), f, bias=ap(bias), scale=ap(scale))
+        add("av" if alt else "a", fn, [i, bias, scale], [o] + ([acc] if acc else []), 80 + CYC * wid(o))
+
+    def eq(o, i, c, nc):
+        tmp = o
+
+        def fn(q, e, ap):
+            if e == "v": return q.tensor_scalar(ap(o), ap(i), ap(c), None, A.is_equal)
+            ap("step")(q.activation(ap(tmp), ap(i), F.Abs, bias=ap(nc)))
+            return q.activation(ap(o), ap(tmp), F.Relu, bias=ap(pc("one")), scale=-1.0)
+        add("av", fn, [i, c, nc, pc("one")], [o], 60 + CYC * wid(o)); ops[-1]["ca"] = 270 + 2 * CYC * wid(o)
+
+    def parts(f, k, *vs):
+        def cut(v, j):
+            if v[4]: return (v[0], v[1], v[2], 1, cut(v[4], j))
+            w = (v[2] - v[1]) // k
+            return V(v[0], v[1] + j * w, v[1] + j * w + w)
+        for j in range(k): f(*[cut(v, j) if isinstance(v, tuple) else v for v in vs])
+
+    def scan(o, d0, d1, init, op0, op1):
+        add("v", lambda q, e, ap: q.tensor_tensor_scan(ap(o), ap(d0), ap(d1), init, op0, op1), [d0, d1], [o],
+            60 + CYC * wid(o) * (0.5 if two(o) and two(d0) and two(d1) else 1))
+
+    def mset(o, c):
+        add("v", lambda q, e, ap: q.memset(ap(o), c), [], [o], 60 + CYC * wid(o) * (0.5 if two(o) else 1))
+
+    def iota(o, pat, base=0, cm=0):
+        def fn(q, e, ap):
+            if SB[o[0]][1] == I32: return q.iota(ap(o), pat, base, cm)
+            return q.iota(ap(o), pat, base, cm, allow_small_or_imprecise_dtypes=True)
+        add("g", fn, [], [o], 130 + 2 * CYC * wid(o))
+
+    def mm(*groups):
+        def fn(q, e, ap):
+            for gr in groups:
+                for n, (o, l, r) in enumerate(gr):
+                    last = q.matmul(ap(o), ap(l), ap(r), n == 0, n == len(gr) - 1)
+            return last
+        al = [x for gr in groups for x in gr]
+        add("p", fn, [x[1] for x in al] + [x[2] for x in al], [x[0] for x in al],
+            60 + sum(PEC * max(64, wid(o)) * (4 if SB[r[0]][1] == F32 else 1) for o, l, r in al))
+
+    def dma(eng, pairs, rd, wr, lat=2200.0):
+        add(eng, pairs, rd, wr, 60.0 * len(pairs), kind="d", lat=lat)
+
+    P0, P1, P2, P3 = "P0", "P1", "P2", "P3"
+    for q, ks in (("s", range(0, 4)), ("a", range(4, 8))):
+        dma(q, [(lambda T, k=k, n=n, u=u: (S(T, "Rs", 0, 768, slice(k + u, 128, 16)), T[n][:, 48 * k:48 * k + 48])) for k in ks for n, u in (("nb", 0), ("en", 8))],
+            [], [V("Rs", 0, 768)] if q == "s" else [V("Rs2", 0, 768)])
+    dma("s", [lambda T: (S(T, "nbw", 0, 384), T.nb[:, :]), lambda T: (S(T, "enw", 0, 384), T.en[:, :])], [], [V("nbw", 0, 384), V("enw", 0, 384)])
+    dma("s", [lambda T: (S(T, "xw", 32, 1568), T.lens[:, :])], [], [V("xw", 32, 1568)], 3500.0)
+
+    def zero(z, zw, parts, lat):
+        ps = [(n, c, min(b, c + zw)) for n, a, b in parts for c in range(a, b, zw)]
+        dma("s", [(lambda T, n=n, a=a, b=b: (S(T, n, a, b), S(T, z, 0, b - a))) for n, a, b in ps], [V(z, 0, zw)], [V(*p) for p in parts], lat)
+    mset(V("Zf", 0, 384), 0); zero("Zf", 384, [("EW", 0, 3072)], 6000.0)
+    iota(V("Zr", 0, 1536), [[0, 1536]]); zero("Zr", 1536, [("xw", 1568, 2720), ("Z", 0, 1728), ("ix", 1920, 2688)], 5000.0)
+    pcn = {}
+
+    def pc(n, w=1):
+        if n not in pcn:
+            a = sum(x[2] - x[1] for x in pcn.values()); pcn[n] = V("PC", a, a + w)
+        return pcn[n]
+
+    def col(v, j):
+        return V(v[0], v[1] + j, v[1] + j + 1)
+    iota(V("PI", 0, 1), [[0, 1]], 0, 1)
+    iota(V("CMx", 0, 144), [[1, 144]], -15)
+    iota(V("CH", 0, 128), [[1, 16], [0, 8]])
+    iota(V("PI", 8, 24), [[1, 16]])
+    iota(V("PI", 32, 40), [[1, 4], [4, 2]])
+    iota(V("pos", 0, 48), [[1, 48]])
+    iota(V("lo8", 0, 800), [[0, 25], [1, 32]])
+    iota(V("hi8", 0, 800), [[1, 25], [0, 32]])
+    ts(V("PI", 1, 2), V("PI", 0, 1), 15, None, A.bitwise_and)
+    ts(V("PI", 2, 3), V("PI", 0, 1), 7, None, A.bitwise_and)
+    ts(V("PI", 3, 4), V("PI", 0, 1), 4, None, A.arith_shift_right)
+    cp(pc("rlg", 3), V("PI", 1, 4))
+    r, l, gr = col(pc("rlg"), 0), col(pc("rlg"), 1), col(pc("rlg"), 2)
+    h, nh, wlh = pc("h"), pc("nh"), pc("wlh")
+    ts(h, r, 8, None, A.is_ge); ts(nh, r, 8, None, A.is_lt); ts(wlh, h, 31, 1, A.mult, A.add)
+    ts(pc("g16"), gr, 16, None, A.mult); ts(pc("g2"), gr, 2, None, A.mult)
+    ts(pc("E", 16), V("PI", 8, 24), r, None, A.is_equal)
+    E = lambda j: col(pc("E"), j)
+    ts(pc("r48"), r, 48, None, A.mult)
+    ts(V("SL", 0, 48), V("pos", 0, 48), pc("r48"), None, A.add)
+    ts(V("pos", 0, 48), V("pos", 0, 48), 16, r, A.mult, A.add)
+    ts(V("CMx", 0, 144), V("CMx", 0, 144), pc("g16"), None, A.subtract)
+    CM0 = V("CMx", 15, 143)
+    zn_, mn_ = {}, {}
+
+    def Z(n, c=None):
+        if n not in zn_: zn_[n] = 144 * len(zn_)
+        a = zn_[n]
+        return V("MZ", a, a + 144) if c is None else V("MZ", a + 15 - c, a + 143 - c)
+
+    def M(n):
+        if n not in mn_: mn_[n] = 128 * len(mn_)
+        return V("M", mn_[n], mn_[n] + 128)
+
+    def zm(n, tg_, w):
+        ts(Z(n), V("CMx", 0, 144), tg_, w, A.is_equal, A.mult)
+    zm("lo", l, nh); zm("hi", l, h); zm("W", l, wlh)
+    ts(M("I"), CM0, r, None, A.is_equal)
+    ts(V("CH", 0, 128), V("CH", 0, 128), pc("g2"), None, A.subtract)
+    ts(M("t1"), V("CH", 0, 128), 0, None, A.is_ge); ts(M("t2"), V("CH", 0, 128), 2, None, A.is_lt); tt(M("Blk"), M("t1"), M("t2"), A.mult)
+    ts(M("Hi"), M("Blk"), h, None, A.mult); ts(M("D"), M("Blk"), E(0), 1000, A.mult, A.mult)
+    ts(M("t1"), CM0, r, None, A.is_gt); tt(M("Tri"), M("t1"), M("Blk"), A.mult)
+    cp(V("MF", 0, 128), M("Tri")); cp(V("MR", 0, 128), M("Blk"))
+    ts(pc("n128"), h, -128, None, A.mult); ts(pc("nr"), r, -1, None, A.mult)
+    ts(pc("c0"), r, 36, None, A.mult); ts(pc("c1"), r, 36, 37, A.mult, A.add); ts(pc("cb"), r, 36 * 4.6, 84.0, A.mult, A.add)
+    ts(M("N92"), M("I"), -92, None, A.mult)
+    mset(V("dead", 0, 576), 0); mset(V("val", 0, 128), 0); mset(V("val", 704, 800), 0); mset(V("S1", 0, 32), 0); iota(V("c96", 0, 576), [[0, 576]], 96); mset(V("cumc", 0, 16), 0)
+    mset(V("RR", 0, 32), 0); mset(V("RR", 800, 832), 0)
+    SLv = V("SL", 0, 48); Rsw = IND("Rs", 0, 768, SLv)
+    ts(V("b1", 0, 768), Rsw, 1.0 / 32, 128.515625, A.mult, A.add); ops[-1]["rd"].append(V("Rs2", 0, 768))
+    ts(pc("b4128"), r, 0, -4128, A.mult, A.add)
+    act(V("b2", 0, 768), V("b1", 0, 768), F.Relu, pc("b4128"), 32.0)
+    tt(V("b3", 0, 768), Rsw, V("b2", 0, 768), A.subtract)
+    for Pn, za, zb, o in ((P0, Z("lo", 0), Z("lo", 8), 32), (P1, Z("hi", 0), Z("hi", 8), 832)):
+        mm(*[[(V(Pn, a, b), za, V("b3", a, b)), (V(Pn, a, b), zb, V("b1", a, b))] for a, b in ((0, 512), (512, 768))])
+        act(V("RR", o, o + 768), V(Pn, 0, 768), F.Relu, pc("n128"),
+            alt=lambda q, ap, o=o, Pn=Pn: q.tensor_scalar(ap(V("RR", o, o + 768)), ap(V(Pn, 0, 768)), ap(pc("n128")), 0.0, A.add, A.max))
+
+    def wrap(o, n, a, b):
+        return [(o, Z("W", 0), V(n, a, b, 2)), (o, Z("W", 8), V(n, a + 1, b, 2))]
+    mm(wrap(V(P2, 512, 896), "RR", 32, 800)); cp(V("W", 0, 384), V(P2, 512, 896))
+    mm(*[[(V(P3, a, b), Z("lo", 0), V("lo8", a, b)), (V(P3, a, b), Z("hi", 8), V("hi8", a, b))] for a, b in ((0, 512), (512, 800))])
+    cp(V("RR", 1600, 2400), V(P3, 0, 800), "av")
+    tt(M("Wc"), Z("W", 0), Z("W", 8), A.add); ts(M("Wk"), M("Wc"), -4096, None, A.mult); tt(M("W2"), Z("hi", 0), Z("W", 8), A.add)
+    ts(M("I256"), M("I"), 256, None, A.mult); ts(Z("F"), Z("hi"), 2000, None, A.mult)
+    ts(pc("h8"), h, 8, None, A.mult); ts(pc("l8"), l, 8, None, A.mult); ts(pc("l8b"), l, 8, -16, A.mult, A.add); ts(pc("l64"), l, 8, -64, A.mult, A.add)
+    ts(pc("El", 8), V("PI", 8, 16), l, None, A.is_equal)
+    tt(pc("we"), col(pc("El"), 0), wlh, A.mult); tt(pc("ws"), l, nh, A.mult)
+    ts(pc("wu"), E(9), 32, E(8), A.mult, A.add); ts(pc("wu"), pc("wu"), 8, None, A.mult)
+    tt(pc("wa"), E(8), E(9), A.add); tt(pc("wb"), E(10), E(11), A.add)
+    zm("all", 0, 1); zm("Y2", pc("h8"), -4); zm("e", 0, pc("we")); zm("s", 0, pc("ws")); zm("u", 0, pc("wu")); zm("A", pc("l8"), pc("wa")); zm("B", pc("l8b"), pc("wb"))
+    zm("0", 0, E(0)); mset(V("junk2", 36, 37), 200)
+    zm("2", 8, 1); tt(Z("2"), Z("2"), Z("all"), A.add)
+    for m_ in range(4):
+        ts(pc("sp%d" % m_), h, 2 * m_ + 1, None, A.add); zm("sp%d" % m_, l, pc("sp%d" % m_))
+    ts(M("t1"), V("CH", 0, 128), -99, None, A.add); tt(M("t2"), M("t1"), M("Blk"), A.mult); ts(V("CH", 0, 128), M("t2"), 99, None, A.add)
+    CH = V("CH", 0, 128)
+    ts(V("PI", 24, 32), V("PI", 8, 16), -1, l, A.mult, A.add); ts(V("PI", 24, 32), V("PI", 24, 32), 7, None, A.bitwise_and); cp(pc("dd", 8), V("PI", 24, 32))
+    ts(pc("nw"), wlh, -1, None, A.mult); ts(pc("nwe"), pc("we"), -1, None, A.mult)
+    for k in range(8): ts(M("N%d" % k), CH, col(pc("dd"), k), pc("nw"), A.is_equal, A.mult)
+    ts(M("NV"), CH, 1, pc("nwe"), A.is_equal, A.mult); ts(M("NLo"), CH, 0, -1, A.is_equal, A.mult); ts(M("R0"), CH, 0, E(0), A.is_equal, A.mult)
+    ts(pc("de", 8), V("PI", 32, 40), -2, r, A.mult, A.add)
+    for k in range(8): ts(M("R%d%d" % (k // 2, k % 2)), CH, col(pc("de"), k), -1, A.is_equal, A.mult)
+    ts(M("t1"), M("I"), -500, None, A.mult); tt(M("TriM"), M("t1"), M("Tri"), A.add)
+    ts(M("t1"), CM0, l, -1, A.is_gt, A.mult); tt(M("t2"), M("t1"), M("NLo"), A.mult); ts(M("t1"), CM0, l, -100, A.is_equal, A.mult); tt(M("CF"), M("t1"), M("t2"), A.add)
+    ts(pc("t8"), h, 8, None, A.add)
+    for j in range(8): ts(M("U%d" % j), CM0, pc("t8"), col(pc("El"), j), A.is_equal, A.mult)
+    iota(V("CO", 0, 192), [[1, 192]], -64)
+    ts(pc("to"), gr, 8, l, A.mult, A.add); ts(V("ZO", 0, 192), V("CO", 0, 192), pc("to"), wlh, A.is_equal, A.mult)
+    iota(V("jk", 0, 32), [[0, 4], [1, 8]]); iota(V("jk", 32, 64), [[1, 4], [1, 8]], 1)
+    ts(V("jk", 32, 64), V("jk", 32, 64), 7, None, A.bitwise_and)
+    ts(V("pu", 0, 64), V("jk", 0, 64), l, h, A.is_equal, A.mult); tt(V("PAT", 0, 32), V("pu", 0, 32), V("pu", 32, 64), A.add)
+    o_ = 0
+    for j in range(7):
+        iota(V("cod", o_, o_ + 7 - j), [[1, 7 - j]], 17 * j + 1); iota(V("cod", 32 + o_, 32 + o_ + 7 - j), [[16, 7 - j]], 17 * j + 16); o_ += 7 - j
+    iota(V("cod", 28, 32), [[0, 4]], -512); iota(V("cod", 60, 64), [[0, 4]], -512)
+    cod = V("cod", 0, 64)
+    ts(pc("r16"), r, 16, None, A.mult); ts(pc("p12"), r, 12, 1000, A.is_ge, A.mult)
+    ts(V("pu", 0, 64), cod, pc("r16"), 0, A.subtract, A.is_ge); ts(V("pu", 64, 128), cod, pc("r16"), 8, A.subtract, A.is_ge)
+    tt(V("PAT", 160, 224), V("pu", 0, 64), V("pu", 64, 128), A.subtract)
+    tt(pc("lh"), l, h, A.add)
+    for sb in range(2):
+        y = pc("y%d" % sb); ts(V("PI", 40, 41), pc("lh"), 2 * sb + 1, None, A.add); ts(V("PI", 41, 42), V("PI", 40, 41), 7, None, A.bitwise_and); cp(y, V("PI", 41, 42))
+        dst = V("PAT", 32 + 64 * sb, 96 + 64 * sb)
+        for z, (a_, b_) in enumerate(((l, y), (y, l))):
+            c0, w0 = pc("k%d%d" % (sb, z)), pc("w%d%d" % (sb, z))
+            ts(c0, a_, 16, b_, A.mult, A.add)
+            if sb: tt(c0, c0, pc("p12"), A.add)
+            ts(w0, a_, 8, -64, A.mult, A.add)
+            ts(V("pu", 0, 64), cod, c0, 1, A.subtract, A.is_ge); ts(V("pu", 64, 128), cod, c0, 8, A.subtract, A.is_ge); ts(V("pu", 128, 192), cod, c0, w0, A.is_equal, A.mult)
+            tt(V("pu", 0, 64), V("pu", 0, 64), V("pu", 64, 128), A.subtract)
+            if z: tt(V("pu", 0, 64), V("pu", 0, 64), dst, A.add)
+            tt(dst, V("pu", 0, 64), V("pu", 128, 192), A.add)
+    ts(V("XL", 0, 8), V("PI", 8, 16), 0, r, A.mult, A.add)
+    for n in range(14): tt(M("X%d" % n), IND("PAT", 16 * n, 16 * n + 16, V("XL", 0, 8)), M("Blk"), A.mult)
+    iota(V("Vf", 0, 768), [[1, 768]], 32); ts(V("ZE", 0, 144), V("CMx", 0, 144), 0, E(0), A.is_equal, A.mult); iota(V("i2", 0, 384), [[0, 8], [16, 48]])
+    iota(V("Tc", 0, 800), [[2048, 800]]); iota(V("Ac", 0, 800), [[0, 800]], 600); iota(V("Ac", 0, 1), [[0, 1]])
+    iota(V("J8", 0, 768), [[0, 96], [8, 8]], 36); iota(V("ids", 0, 192), [[1, 192]], 2); iota(V("im", 0, 384), [[1, 384]]); iota(V("id1", 0, 96), [[1, 96]], 1)
+    iota(V("big", 0, 384), [[0, 24], [1, 16]]); ts(V("big", 0, 384), V("big", 0, 384), r, 4096, A.is_equal, A.mult)
+    iota(V("W2", 768, 1600), [[0, 832]], -8); ts(V("W2", 768, 1600), V("W2", 768, 1600), E(9), None, A.mult)
+    iota(V("c884", 0, 192), [[0, 192]], 884); iota(V("cumb", 0, 1), [[0, 1]], 500); iota(V("num", 0, 2), [[0, 2]], 999); iota(V("Nw", 0, 2), [[0, 2]])
+    iota(V("xw", 0, 32), [[0, 32]]); iota(V("mid", 0, 168), [[0, 168]], 31)
+    ts(M("nI"), M("I"), -1, None, A.mult)
+    iota(V("thr", 0, 48), [[0, 48]])
+    iota(V("slf", 0, 96), [[672, 2], [2, 48]], 32); ts(V("slf", 0, 96), V("slf", 0, 96), h, None, A.add)
+    iota(V("pc8", 0, 96), [[768, 2], [16, 48]], 15); ts(V("pc8", 0, 96), V("pc8", 0, 96), pc("h8"), None, A.add)
+    for s in range(2): ts(V("dum", 48 * s, 48 * s + 48), V("pos", 0, 48), 2720, None, A.add)
+    ts(V("pk", 0, 48), V("pos", 0, 48), 1232, None, A.add); ts(V("pk", 48, 96), V("pos", 0, 48), -512, None, A.add); ts(V("pk", 96, 108), V("pos", 0, 12), 308, None, A.add)
+    ts(V("pk", 112, 118), V("pos", 0, 6), 0.5, None, A.add)
+    ts(M("t1"), M("I"), E(10), None, A.mult); ts(M("t2"), M("I"), E(11), None, A.mult)
+    mm([(V(P3, 0, 384), M("t1"), V("lo8", 0, 384)), (V(P3, 0, 384), M("t2"), V("hi8", 0, 384))])
+    for t in range(3):
+        ts(pc("nm%d" % t), E(11), 49 + 12 * t, None, A.mult); act(V("NM", 384 * t, 384 * t + 384), V(P3, 0, 384), F.Identity, pc("nm%d" % t))
+    a384 = lambda n: V(n, 0, 384)
+    ts(a384("i2"), a384("i2"), r, None, A.add)
+    tt(a384("i3"), a384("i2"), a384("nbw"), A.is_gt); ts(a384("i3"), a384("i3"), 1536, None, A.mult); tt(a384("i3"), a384("i3"), a384("enw"), A.add)
+    ts(a384("i2"), a384("i2"), 1537, None, A.add); ts(a384("i1"), a384("enw"), 0, None, A.is_lt); tt(a384("i1"), a384("i1"), a384("i2"), A.mult)
+    tt(a384("i3"), a384("i3"), a384("i1"), A.add); cp(a384("EO"), a384("i3"))
+    for k in range(16):
+        eo = IND("EW", 0, 3840, V("EO", 24 * k, 24 * k + 24)); vf = V("Vf", 384 * (k % 2), 384 * (k % 2) + 384)
+        add("a", lambda q, e, ap, eo=eo, vf=vf: q.activation(ap(eo), ap(vf), F.Silu), [vf], [eo], 80 + CYC * SCA * 384)
+    mm([(V(P3, 0, 192), V("ZE", 15 - i, 143 - i), V("EW", i, 3072, 16)) for i in range(16)])
+    ts(V("i2", 0, 192), V(P3, 0, 192), 1, None, A.max); cp(V("LA", 0, 96), V("i2", 0, 96)); cp(V("LB", 0, 96), V("i2", 96, 192))
+    iota(V("ga", 1920, 2688), [[0, 768]]); iota(V("Pw", 0, 16), [[0, 16]], 300)
+
+    sp = ((0, 512), (512, 576)); sq = ((0, 512), (512, 768)); late = ([], [])
+    for t in range(3):
+        Et = 1536 + 384 * t; last = t == 2
+        dma("s", [lambda T: (S(T, "Aw", 768, 1568), S(T, "Ac", 0, 800))], [V("Ac", 0, 800)], [V("Aw", 768, 1568)])
+        zero("Zr", 1536, [("Aux", 768, 6912)], 8000.0)
+        n576 = lambda n: V(n, 0, 576)
+        act(n576("fil"), V("RR", 128, 704), F.Sign, alt=lambda q, ap: q.tensor_scalar(ap(n576("fil")), ap(V("RR", 128, 704)), 1, None, A.is_ge))
+        ops[-1]["ca"] = ops[-1]["cost"]; ops[-1]["cost"] = 360.0
+        mm(*[[(V(P2, a, b), M("Hi"), V("fil", a, b)), (V(P2, a, b), M("D"), V("dead", a, b))] for a, b in sp])
+        eq(n576("ind"), V(P2, 0, 576), r, pc("nr"))
+        scan(n576("cumd"), n576("ind"), n576("ind"), 0.0, A.add, A.max)
+        mm([(V(P1, 0, 1), V("MF", 0, 128), V("cumd", 575, 576))]); cp(pc("off"), V(P1, 0, 1), "av")
+        act(V(P0, 0, 576), n576("cumd"), F.Identity, pc("off"), alt=lambda q, ap: q.tensor_scalar(ap(V(P0, 0, 576)), ap(n576("cumd")), ap(pc("off")), None, A.add)); tt(n576("rk"), V(P0, 0, 576), n576("ind"), A.mult)
+        mm(*[[(V(P2, a, b), V("MR", 0, 128), V("rk", a, b)), (V(P2, a, b), M("D"), V("dead", a, b))] for a, b in sp])
+        ts(n576("f1"), V(P2, 0, 576), pc("c0"), pc("c1"), A.max, A.min)
+        act(V("val", 128, 704), n576("f1"), F.Exp, pc("cb"), -4.6)
+        for c in range(8):
+            cp(V("G1", 768 * c, 768 * c + 768), IND("val", 0, 800, V("W", 48 * c, 48 * c + 48)), "av" if c % 4 * 2 + c // 4 >= 8 - HV[2 * t] else "a")
+            o = V(P0, 512 * (c // 4) + 96 * (c % 4), 512 * (c // 4) + 96 * (c % 4) + 96)
+            mm([(o, M("I"), V("val", 32 + 96 * c, 128 + 96 * c))] + [(o, M("I"), V("G1", 768 * c + k, 768 * c + 768, 8)) for k in range(8)])
+        for u in range(2): cp(V("S1", 32 + 384 * u, 416 + 384 * u), V(P0, 512 * u, 512 * u + 384), "av")
+        for c in range(6):
+            cp(V("G1", 768 * c, 768 * c + 768), IND("S1", 0, 800, V("W", 48 * c + 48, 48 * c + 96)), "av" if c % 3 * 2 + c // 3 >= 6 - HV[2 * t + 1] else "a")
+            o = V(P1, 512 * (c // 3) + 96 * (c % 3), 512 * (c // 3) + 96 * (c % 3) + 96)
+            mm([(o, M("I"), V("S1", 128 + 96 * c, 224 + 96 * c)), (o, M("N92"), V("val", 128 + 96 * c, 224 + 96 * c))] +
+               [(o, M("I"), V("G1", 768 * c + k, 768 * c + 768, 8)) for k in range(8)])
+        for u in range(2):
+            so, pi = V("sg", 288 * u, 288 * u + 288), V(P1, 512 * u, 512 * u + 288)
+            act(so, pi, F.Sign)
+            po = V(P2, 512 * u, 512 * u + 288); co = V("cho", 288 * u, 288 * u + 288)
+            mm([(po, M("Blk"), so), (po, M("D"), V("dead", 288 * u, 288 * u + 288))])
+            act(co, po, F.Relu, pc("m15"), -1.0, alt=lambda q, ap, co=co, po=po: q.tensor_scalar(ap(co), ap(po), -15.5, None, A.is_lt))
+        scan(V("cumc", 16, 592), n576("cho"), n576("c96"), 0.0, A.add, A.min)
+        cc = V("cumc", 16, 592)
+        for c in range(6): act(V("junk", 48 * c, 48 * c + 36), V("cumc", 31, 592, 16), F.Sign, V("pk", 112 + c, 113 + c), -1.0, acc=V("vc", c, c + 1))
+        mm([(V(P0, 0, 36), Z("0", i), V("cumc", 16 + i, 592, 16)) for i in range(16)]); cp(V("junk2", 0, 36), V(P0, 0, 36))
+        ts(V("QL", 0, 6), V("vc", 0, 6), 0.5, 18, A.mult, A.add)
+        tt(V("junk2", 64, 160), IND("junk2", 0, 37, V("QL", 0, 6)), V("id1", 0, 96), A.is_lt)
+        ts(V("vd", 0, 6), V("vc", 0, 6), 8, 416, A.mult, A.add); ts(V("vd", 8, 14), V("vc", 0, 6), 35, None, A.is_lt); tt(V("vd", 0, 6), V("vd", 0, 6), V("vd", 8, 14), A.mult)
+        mm([(V(P0, 512, 518), Z("all", i), V("junk2", 64 + i, 160, 16)) for i in range(16)]); tt(V("vd", 8, 14), V(P0, 512, 518), V("vd", 0, 6), A.add)
+        for u in range(3): ts(V("VL", 6 * u, 6 * u + 6), V("vd", 8, 14), 800 * u, None, A.add)
+        mm(*[[(V(P2, a, b), M("I"), V("dead", a, b)), (V(P2, a, b), M("I"), V("cumc", 16 + a, 16 + b)), (V(P2, a, b), M("nI"), V("cumc", 15 + a, 15 + b))] for a, b in sp])
+        cp(n576("dead"), V(P2, 0, 576), "a")
+        cp(V("Rv", 0, 288), IND("RR", 0, 2400, V("VL", 0, 18)))
+        while late[0]: late[0].pop()()
+        mm(wrap(V(P0, 0, 144), "Rv", 0, 288)); cp(V("UL", 0, 144), V(P0, 0, 144))
+        ts(V("fv", 0, 96), V("Rv", 0, 96), 1, None, A.is_ge)
+        o = V(P0, 512, 560)
+        mm(wrap(o, "Rv", 0, 96) + [(o, Z("F", 0), V("fv", 0, 96, 2)), (o, Z("F", 8), V("fv", 1, 96, 2))])
+        tt(V("s1", 0, 48), o, V("pk", 0, 48), A.max); ts(V("Us", 0, 48), V("s1", 0, 48), -1232, None, A.add)
+        for u in range(2): cp(V("G", 384 * u, 384 * u + 384), IND("RR", 0, 800, V("UL", 24 * u, 24 * u + 24)), "av")
+        parts(cp, SPL[0], V("Lf", 0, 768), IND("xw", 0, 2720, V("UL", 48, 96)), "av"); parts(cp, SPL[0], V("tg", 0, 768), IND("Tc", 0, 800, V("UL", 96, 144)), "av")
+        while late[1]: late[1].pop()()
+        parts(tt, SPL[1], IND("Aw", 0, 1568, V("Us", 0, 48)), V("Lf", 0, 768), V("tg", 0, 768), A.add)
+        MG = 1.5 * 2.0 ** 34
+        mm(*[[(V(P3, a, b), M("Wk"), V("RR", 32 + a, 32 + b))] for a, b in sq]); cp(V("nbK", 0, 768), V(P3, 0, 768), "a")
+        act(V("Tt", 0, 800), V("Aw", 768, 1568), F.Identity, pc("mg"))
+        act(V(P3, 0, 800), V("Tt", 0, 800), F.Identity, pc("mg2"), -2.0); tt(V("Bw", 0, 800), V("Aw", 768, 1568), V(P3, 0, 800), A.add)
+        for it, Pn in enumerate((P1, P2, P0)):
+            mm(*[[(V(Pn, a, b), M("W2" if it == 2 else "Wc"), V("G", a, b))] +
+                 [(V(Pn, a + j, b, 8), M("NV") if it == 2 else M("N%d" % ((j + 2 * it + 1) % 8)), V("Rv", a // 8 + (192 if it == 2 else 0), b // 8 + (192 if it == 2 else 0))) for j in range(8)]
+                 for a, b in sq])
+            for a, b in sq: eq(V("EQ", 768 * it + a, 768 * it + b), V(Pn, a, b), 0, 0.0)
+        mm(*[[(V(P1, 96 * b, 96 * b + 96), M("X%d" % b), V("fv", 0, 96))] + [(V(P1, 96 * b, 96 * b + 96), Z("Y2", j), V("EQ", 768 * b + j, 768 * b + 768, 8)) for j in range(8)] for b in range(2)])
+        act(V("wish", 0, 192), V(P1, 0, 192), F.Relu, pc("m1"), alt=lambda q, ap: q.tensor_scalar(ap(V("wish", 0, 192)), ap(V(P1, 0, 192)), 1.5, None, A.is_ge))
+        mm([(V(P1, 512, 608), Z("all", j), V("EQ", 1536 + j, 2304, 8)) for j in range(8)])
+        act(V("nf", 0, 96), V(P1, 512, 608), F.Identity, pc("l64"))
+        mm(*[[(V(P2, 192 * e + b, 192 * e + 192, 2), M("X%d" % (2 + 4 * sb + 2 * e + b)), V("wish", 96 * sb, 96 * sb + 96)) for sb in range(2)] for e in range(2) for b in range(2)])
+        mm(*[[(V(P2, 512 + 192 * e + b, 704 + 192 * e, 2), M("X%d" % (10 + 2 * e + b)), V("nf", 0, 96))] for e in range(2) for b in range(2)])
+        cp(V("Nw", 2, 386), V(P2, 0, 384), "av")
+        tt(V("fw", 0, 384), V("Nw", 2, 386), V(P2, 512, 896), A.is_lt); tt(V("ok", 0, 192), V("fw", 0, 192), V("fw", 192, 384), A.mult)
+        mm([(V(P1, 512, 704), M("Blk"), V("ok", 0, 192))]); mm([(V(P1, 0, 192), M("TriM"), V("ok", 0, 192))])
+        scan(V("cumb", 1, 193), V(P1, 512, 704), V("c884", 0, 192), 500.0, A.add, A.min)
+        scan(V("ws", 0, 192), V("big", 0, 192), V("cumb", 0, 192), 0.0, A.add, A.min); scan(V("we", 0, 192), V("big", 0, 192), V("cumb", 1, 193), 0.0, A.add, A.min)
+        tt(V("s2", 0, 12), V("we", 15, 192, 16), V("ws", 15, 192, 16), A.is_gt); tt(V("s2", 16, 28), V("s2", 0, 12), V("ws", 15, 192, 16), A.mult)
+        tt(V("s2", 32, 44), V("s2", 16, 28), V("pk", 96, 108), A.max); ts(V("ZL", 0, 12), V("s2", 32, 44), -308, None, A.add)
+        cp(IND("Z", 576 * t, 576 * t + 576, V("ZL", 0, 12)), V("ids", 0, 192))
+        zr = V("Z", 576 * t + 192, 576 * t + 576)
+        scan(a384("mx"), zr, zr, 0.0, A.max, A.max); scan(a384("wr"), a384("big"), a384("mx"), 0.0, A.add, A.min)
+        cp(V("CL", 0, 24), V("wr", 15, 384, 16)); CL = V("CL", 0, 24)
+        tt(V("num", 2, 194), V(P1, 0, 192), V("cumb", 0, 192), A.add)
+        tt(a384("oh"), IND("num", 0, 194, CL), a384("im"), A.is_equal)
+        for e in range(2): tt(V("pr", 384 * e, 384 * e + 384), IND("Nw", 192 * e, 192 * e + 194, CL), a384("oh"), A.mult)
+        o = V(P1, 512, 560)
+        mm([(o, Z("all", i), V("pr", i, 768, 16)) for i in range(16)])
+        cp(V("j1", 0, 24), V("wr", 15, 384, 16)); ts(V("j1", 24, 48), V("j1", 0, 24), 510, None, A.bitwise_and)
+        for e in range(2): ts(V("s3", 24 * e, 24 * e + 24), V("j1", 24, 48), 4, -8, A.mult, A.add)
+        ts(V("j2", 0, 48), o, 0.125, 7.625, A.mult, A.add); ts(V("s3", 48, 96), o, -0.5, 800, A.is_ge, A.mult)
+        tt(V("s3", 48, 96), V("s3", 48, 96), V("s3", 0, 48), A.add); tt(V("s1", 48, 96), V("s3", 48, 96), V("j2", 0, 48), A.add); cp(V("IL", 0, 48), V("s1", 48, 96))
+        mm(*[[(V(P0, a, b), M("CF"), V("EQ", 1536 + a, 1536 + b)), (V(P0, a, b), M("R0"), V("J8", a, b))] +
+             [(V(P0, a + j, b, 8), M("U%d" % j), V("Rv", a // 8, b // 8)) for j in range(8)] for a, b in sq])
+        cp(V("W2", 0, 768), V(P0, 0, 768), "a")
+        for e in range(2):
+            ge = V("G2", 384 * e, 384 * e + 384); pe = V(P2, 512 * e, 512 * e + 384)
+            cp(ge, IND("W2", 0, 1600, V("IL", 24 * e, 24 * e + 24)), "av")
+            mm([(pe, Z("lo", 0), ge), (pe, M("NLo"), V("pr", 384 * e, 384 * e + 384))])
+            eq(V("e2", 384 * e, 384 * e + 384), pe, 0, 0.0)
+        o = V(P1, 0, 48)
+        mm([(o, Z("u", i), V("G2", i, 768, 16)) for i in range(16)] + [(o, Z("s", i), V("e2", i, 768, 16)) for i in range(16)])
+        tt(V("s1", 0, 48), o, V("pk", 48, 96), A.max); ts(V("AL", 0, 48), V("s1", 0, 48), 512, None, A.add)
+        x0 = 0
+        for e in range(2):
+            tt(IND("Aux", x0, x0 + 6912, V("AL", 24 * e, 24 * e + 24)), V("G2", 384 - 384 * e, 768 - 384 * e), V("NM", 384 * t, 384 * t + 384), A.add)
+        ts(V("j3", 0, 48), o, 0.125, -0.4375, A.mult, A.add)
+        nl = Et // 16
+        cp(V("LA", nl, nl + 24), V("j3", 0, 24)); cp(V("LB", nl, nl + 24), V("j3", 24, 48))
+        tt(V(P3, 32, 800), V(P3, 32, 800), V("nbK", 0, 768), A.not_equal)
+        if last: tt(V(P3, 128, 704), V(P3, 128, 704), n576("dead"), A.is_gt)
+        for Pn, kb, zz, o in ((P0, "Kn", "A", 32), (P2, "Ke", "B", 832)):
+            tt(V(kb, 0, 768), V("RR", o, o + 768), V(P3, 32, 800), A.mult)
+            for a, b in sq:
+                mm([(V(Pn, a, b), M("I"), V(kb, a, b))] + [(V(Pn, a, b), Z(zz, s), V("Aux", x0 + 768 + 8 * a + s, x0 + 768 + 8 * b, 8)) for s in range(8)])
+                cp(V("RR", o + a, o + b), V(Pn, a, b), "av")
+        for a in range(0, Et, 384):
+            b = a + 384; z = a % 1536; zf, zb = V("zf", z, z + 384), V("zb", z, z + 384); xs = V("xw", 32 + a, 32 + b)
+            cp(V("ga", a, b), IND("Aw", 768, 1568, V("LA", a // 16, b // 16)), "av")
+            tt(zf, IND("Bw", 0, 800, V("LB", a // 16, b // 16)), V("ga", a, b), A.add)
+            act(zb, zf, F.Abs)
+            o = V(P3, a // 384 % 2 * 512, a // 384 % 2 * 512 + 384)
+            mm([(o, M("I"), xs), (o, M("nI"), zb)])
+            act(V("ix", a, b), o, F.Sign, pc("mh"))
+            if a // 384 < XACT[t]:
+                rr = V("rl", a % 768, a % 768 + 384); act(rr, o, F.Relu)
+                mm([(o, M("I"), xs), (o, M("nI"), rr)]); cp(xs, o, "a")
+            else:
+                tt(xs, xs, zb, A.min)
+        cp(V("ga", Et, Et + 384), IND("Aw", 768, 1568, V("LA", nl, nl + 24)), "av")
+        tt(a384("zn"), IND("Bw", 0, 800, V("LB", nl, nl + 24)), V("ga", Et, Et + 384), A.add)
+        ts(V("xw", 32 + Et, 416 + Et), a384("zn"), 255, None, A.min)
+        act(V("ix", Et, Et + 384), a384("zn"), F.Sign, pc("mh"))
+        dma("s", [lambda T: (S(T, "own", 0, 168), S(T, "ga", 0, 2688, slice(0, 128, 16)))], [V("ga", 0, 2688)], [V("own", 0, 168)])
+        wp = V(P1, 512, 896)
+        mm(wrap(wp, "RR", 32, 800))
+        if not last: cp(V("W", 0, 384), wp)
+        mm(*[wrap(V(P1, 48 * s, 48 * s + 48), "RR", 832 + 672 * s, 928 + 672 * s) for s in range(2)])
+        cp(V("Eb", 0, 96), V(P1, 0, 96)); tt(V("Ebf", 0, 48), V(P1, 0, 48), V("dum", 0, 48), A.subtract); tt(V("Ebf", 48, 96), V(P1, 48, 96), V("dum", 48, 96), A.subtract)
+        for s in range(2):
+            m0 = 432 * (2 * t + s)
+            cp(V("snd", m0 + 384, m0 + 432), V(P1, 512 + 336 * s, 560 + 336 * s)); cp(V("nbs", 48 * s, 48 * s + 48), V(P1, 512 + 336 * s, 560 + 336 * s), "av")
+            parts(cp, SPL[0], V("Go", 768 * s, 768 * s + 768), IND("xw", 0, 2720, V("Eb", 48 * s, 48 * s + 48)), "av")
+            o = V(P3, 512 * s, 512 * s + 384)
+            mm([(o, M("I256"), V("Go", 768 * s, 768 * s + 384)), (o, M("I"), V("Go", 768 * s + 384, 768 * s + 768))])
+            cp(V("snd", m0, m0 + 384), o)
+        for k, a, b, lat in ([(3, 384, 432, 3000.0), (2, 0, 384, 5000.0)] if last else [(t, 0, 432, 5000.0)]):
+            add("g", (k, t, a, b), [V("snd", 864 * t + 432 * s + a, 864 * t + 432 * s + b) for s in range(2)], [V("net", k, k + 1)], 1500.0 if t else 3000.0, kind="send")
+            add("r", (k, t, a, b), [V("net", k, k + 1)], [V("lnd", 864 * t + 432 * s + a, 864 * t + 432 * s + b) for s in range(2)], 0.0, kind="recv", lat=lat)
+        if last:
+            for a, b in ((32, 1376), (1376, 2720)): act(V("xw", a, b), V("xw", a, b), F.Abs)
+        tt(V("can", 0, 96), V("nbs", 0, 96), V("slf", 0, 96), A.is_gt); ts(V("q1", 0, 48), V("nbs", 0, 48), 128, None, A.is_lt)
+        tt(V("can", 0, 48), V("can", 0, 48), V("q1", 0, 48), A.mult); tt(V("can", 0, 96), V("can", 0, 96), V("Ebf", 0, 96), A.mult)
+        tt(V("can", 0, 96), V("can", 0, 96), V("dum", 0, 96), A.add); cp(V("SS", 0, 96), V("can", 0, 96))
+        ts(V("thr", 48, 96), V("nbs", 48, 96), 704, 1e6, A.is_lt, A.mult)
+        o = V(P3, 0, 168)
+        mm([(o, Z("all", i), V("ix", 168 * i, 168 * i + 168)) for i in range(16) if 168 * i < Et + 384])
+        ts(V("m1", 0, 168), V("own", 0, 168), 1.0 / 2048, None, A.mult); tt(V("m2", 0, 168), V("m1", 0, 168), V("mid", 0, 168), A.subtract)
+        ts(V("m3", 0, 168), o, 1.0, None, A.is_ge); tt(V("m2", 0, 168), V("m2", 0, 168), V("m3", 0, 168), A.mult); tt(V("mid", 0, 168), V("mid", 0, 168), V("m2", 0, 168), A.add)
+        if last:
+            ts(V("m3", 0, 168), V("mid", 0, 168), -32, None, A.add)
+            dma("s", [lambda T: (T.ymid[:, :], S(T, "m3", 0, 168))], [V("m3", 0, 168)], [V("out", 0, 1)])
+
+        def rows_out(Pn, a, b, pa):
+            o = V(Pn, pa, pa + b - a)
+            mm([(o, V("ZO", 64, 192), V("RR", 32 + a, 32 + b)), (o, V("ZO", 0, 128), V("RR", 832 + a, 832 + b))])
+            ts(V("O", a, b), o, -32, -1, A.add, A.max)
+        if last: rows_out(P0, 96, 384, 0); rows_out(P0, 384, 672, 512)
+        l0 = 864 * t
+        ts(V("par", 0, 48), V("lnd", l0 + 384, l0 + 432), 703, -8, A.subtract, A.max); ts(V("par", 48, 96), V("lnd", l0 + 816, l0 + 864), 31, None, A.subtract)
+        for s in range(2):
+            c0 = 512 * s
+            mm(*[[(V(P3, c0 + 96 * m_, c0 + 96 * m_ + 96), M("Wc"), V("RR", 32 + 672 * s, 128 + 672 * s))] +
+                 [(V(P3, c0 + 96 * m_ + z, c0 + 96 * m_ + 96, 2), M("R%d%d" % (m_, z)), V("par", 48 * s, 48 * s + 48)) for z in range(2)] for m_ in range(4)])
+            eq(V("eqs", 384 * s, 384 * s + 384), V(P3, c0, c0 + 384), 31 + 672 * s, pc("ns%d" % s))
+        mm(*[[(V(P3, 48 * s, 48 * s + 48), Z("sp%d" % m_, 8 * z), V("eqs", 384 * s + 96 * m_ + z, 384 * s + 96 * m_ + 96, 2)) for m_ in range(4) for z in range(2)] for s in range(2)])
+        tt(V("q1", 0, 96), V(P3, 0, 96), V("thr", 0, 96), A.is_gt); tt(V("can", 0, 96), V(P3, 0, 96), V("pc8", 0, 96), A.add)
+        tt(V("can", 0, 96), V("can", 0, 96), V("q1", 0, 96), A.mult); cp(V("PL", 0, 96), V("can", 0, 96))
+        for s in range(2):
+            cp(V("i1", 432 * s, 432 * s + 384), V("lnd", l0 + 432 * s, l0 + 432 * s + 384))
+            ts(V("Pw", 16 + 768 * s, 400 + 768 * s), V("i1", 432 * s, 432 * s + 384), 8, None, A.arith_shift_right)
+            ts(V("Pw", 400 + 768 * s, 784 + 768 * s), V("i1", 432 * s, 432 * s + 384), 255, None, A.bitwise_and)
+        for s in range(2):
+            sv = lambda n: V(n, 768 * s, 768 * s + 768)
+            pw = IND("Pw", 0, 784 + 768 * s, V("PL", 48 * s, 48 * s + 48)); xs = IND("xw", 0, 3488, V("SS", 48 * s, 48 * s + 48))
+            parts(tt, SPL[0], sv("mn"), pw, sv("Go"), A.min)
+            for u in range(2):
+                o = V(P3, 512 * u, 512 * u + 384); w = (768 * s + 384 * u, 768 * s + 384 * u + 384)
+                mm([(o, M("I"), V("Go", *w)), (o, M("nI"), V("mn", *w))]); act(V("si", *w), o, F.Sign)
+            if last: parts(cp, SPL[1], xs, sv("mn"))
+            o = V(P3, 0, 96)
+            mm([(o, Z("2", k), V("si", 768 * s + k, 768 * s + 768, 8)) for k in range(8)])
+            ks = V("ks", 96 * s, 96 * s + 96); ts(ks, o, 8.5, None, A.is_lt)
+
+            def drop(s=s, ks=ks):
+                for b in (32, 832): tt(V("RR", b + 672 * s, b + 96 + 672 * s), V("RR", b + 672 * s, b + 96 + 672 * s), ks, A.mult)
+            if last:
+                drop(); rows_out(P0, 672 * s, 672 * s + 96, 512 * s)
+            else:
+                late[0].append(drop)
+                late[1].append(lambda xs=xs, a=sv("mn"), b=sv("sn"): parts(tt, SPL[1], xs, a, b, A.mult))
+        if not last:
+            for u in range(4):
+                o = V(P3, 512 * (u % 2), 512 * (u % 2) + 384); w = (384 * u, 384 * u + 384)
+                mm([(o, M("Blk"), V("si", *w))]); act(V("sn", *w), o, F.Sign, pc("p85"), -1.0)
+        if last:
+            dma("s", [lambda T: (T.ylen[:, :], S(T, "xw", 32, 2720))], [V("xw", 32, 2720)], [V("out", 1, 2)], 4000.0)
+            dma("a", [lambda T: (T.ynb[:, :], S(T, "O", 0, 768, slice(0, 64))), lambda T: (T.yen[:, :], S(T, "O", 0, 768, slice(64, 128)))], [V("O", 0, 768)], [V("out", 2, 3)], 3000.0)
+    pre = len(ops)
+    for n_, c_ in (("m15", -15.0), ("p85", 8.5), ("mh", -0.5), ("one", 1.0), ("mg", MG), ("mg2", 2 * MG), ("ns0", -31.0), ("ns1", -703.0), ("m1", -1.0)): mset(pc(n_), c_)
+    return ops[pre:] + ops[:pre]
+
+
+def span(v):
+    a, b = v[1], v[2]
+    if v[0] in ("P0", "P1", "P2", "P3"):
+        return v[0], a // 512 * 512, (b - 1) // 512 * 512 + 512
+    if v[0] in LOC:
+        return LOC[v[0]][0], a + LOC[v[0]][1], b + LOC[v[0]][1]
+    return v[0], a, b
+
+
+def plan():
+    ops = program(); n = len(ops); hist = {}
+    for i, o in enumerate(ops):
+        dep = {}
+        for v, w in [(v, False) for v in o["rd"]] + [(v, True) for v in o["wr"]]:
+            nm, a, b = span(v); ps = v[0] not in SB and v[0][0] == "P"
+            for (j, c, d, ww) in hist.get(nm, []):
+                if j == i or d <= a or b <= c: continue
+                if ww or w: dep[j] = True
+                elif ps: dep[j] = dep.get(j, False)
+        for v in o["wr"]:
+            nm, a, b = span(v)
+            if not v[4] and v[3] == 1 and v[0] in SB:
+                hist[nm] = [x for x in hist.get(nm, []) if not (a <= x[1] and x[2] <= b)]
+        for v, w in [(v, False) for v in o["rd"]] + [(v, True) for v in o["wr"]]:
+            nm, a, b = span(v); hist.setdefault(nm, []).append((i, a, b, w))
+        o["dep"] = dep
+    succ = [[] for _ in ops]
+    for i, o in enumerate(ops):
+        for j in o["dep"]: succ[j].append(i)
+    SY = 110.0
+    pred = [list(o["dep"]) for o in ops]
+
+    def place(pri, before, after, fixed, bias):
+        busy = {e: [] for e in "vapgsr"}; t0 = [0.0] * n; fin = [0.0] * n; eng = [""] * n
+        left = [len(x) for x in before]; ready = [i for i in range(n) if not left[i]]
+        while ready:
+            i = max(ready, key=lambda k: pri[k]); ready.remove(i); o = ops[i]
+            rt = max([fin[j] + SY for j in before[i]] + [0.0]); c = o["cost"]; best = None
+            pre_, post = (0.0, o["lat"]) if before is pred else (o["lat"], 0.0)
+            for e in (fixed[i] if fixed else o["engs"]):
+                s = rt + pre_; at_ = 0; c = o.get("ca", o["cost"]) if e == "a" else o["cost"]
+                for at_, (a, b) in enumerate(busy[e] + [(1e18, 1e18)]):
+                    if s + c <= a: break
+                    s = max(s, b)
+                key = s + c + (bias if e == "v" else 0.0)
+                if best is None or key < best[0]: best = (key, s, e, at_, c)
+            _, s, e, at_, c = best
+            busy[e].insert(at_, (s, s + c)); t0[i] = s; fin[i] = s + c + post; eng[i] = e
+            for j in after[i]:
+                left[j] -= 1
+                if not left[j]: ready.append(j)
+        return t0, fin, eng
+    pri = [0.0] * n
+    for i in range(n - 1, -1, -1):
+        pri[i] = ops[i]["cost"] + ops[i]["lat"] + SY + max([pri[j] for j in succ[i]] + [0.0])
+    top = None
+    for bias, seed in BIASES:
+        rs = np.random.RandomState(seed); p = [x + float(y) for x, y in zip(pri, rs.uniform(0, JIT if seed else 0.0, n))]
+        for _ in range(PASSES):
+            t0, fin, eng = place(p, pred, succ, None, bias)
+            if top is None or max(fin) < top[0]: top = (max(fin), t0, eng)
+            _, p, _ = place(fin, succ, pred, eng, 0.0)
+    for i, o in enumerate(ops): o["t0"] = top[1][i]; o["e"] = top[2][i]; o["pri"] = pri[i]
+    return ops, sorted(range(n), key=lambda i: (top[1][i], i)), top[0]
+
+
+PLAN = []
+
+
+def rank_program(g, core, T, topo):
+    rank = T.rank_of(core)
+    if rank is None:
+        return
+    if not PLAN: PLAN.append(plan())
+    ops, order, _ = PLAN[0]
+    Q = dict(v=g.vector, a=g.scalar, p=g.tensor, g=g, s=g.sync)
+
+    steps = [0]
+
+    def step(ins):
+        steps[0] += 1; ins.then_inc(T.sem.ax, 1); g.scalar.wait_ge(T.sem.ax, steps[0])
+
+    def ap(v):
+        if v == "step": return step
+        if not isinstance(v, tuple): return v
+        nm, o = LOC.get(v[0], (v[0], 0))
+        x = T[nm][:, o + v[1]:o + v[2]] if v[3] == 1 else T[nm][:, o + v[1]:o + v[2]:v[3]]
+        return x.indirect(ap(v[4])) if v[4] else x
+    at = {i: k for k, i in enumerate(order)}; seen = {e: {} for e in Q}; waits = {}; need = set()
+    for i in order:
+        o = ops[i]; e = o["e"]; waits[i] = []
+        if e == "r": continue
+        best = {}
+        for j, hard in o["dep"].items():
+            d = ops[j]; key = d["e"] if d["kind"] == "c" else j
+            if d["kind"] == "c" and d["e"] == e and (e == "p" or (SOFT_SAME and not hard)): continue
+            if key not in best or at[j] > at[best[key]]: best[key] = j
+        for key, j in best.items():
+            if seen[e].get(key, -1) >= at[j]: continue
+            seen[e][key] = at[j]; waits[i].append(j); need.add(j)
+    token = {}; cnt = {e: 0 for e in "vapg"}; nd = 0; tail = []
+    n = len(T.cores)
+    for i in order:
+        o = ops[i]; e = o["e"]
+        if o["kind"] == "recv":
+            token[i] = (T.sem["r%d" % o["fn"][0]], sum(len(topo.engines(T.cores[(rank + z) % n], core)) // 2 for z in (-1, 1))); continue
+        q = Q[e]
+        for j in waits[i]: q.wait_ge(*token[j])
+        if o["kind"] == "c":
+            ins = o["fn"](q, e, ap)
+            if i in need:
+                cnt[e] += 1; ins.then_inc(T.sem["e" + e], 1); token[i] = (T.sem["e" + e], cnt[e])
+        elif o["kind"] == "d":
+            sem = T.sem["d%d" % nd]; nd += 1
+            for f in o["fn"]:
+                a, b = f(T); q.dma_start(a, b).then_inc(sem, 16)
+            token[i] = (sem, 16 * len(o["fn"]))
+            if i not in need: tail.append(token[i])
+        else:
+            m, t, a, b = o["fn"]; trs = []; used = 0
+            for s in range(2):
+                d = T.cores[(rank + 2 * s - 1) % n]; rid, pid = topo.addr(d, core); en = topo.engines(core, d)
+                k = len(en) // 2; mask = sum(1 << x for x in en[k * s:k * s + k])
+                trs.append(RemoteDMATransfer(dst_ids=[DstId(rid=rid, pnc=pid)], dma_engine_mask=mask, remote_sem=T.sem["r%d" % m],
+                                             src=S(T, "snd", 432 * (2 * t + s) + a, 432 * (2 * t + s) + b), dst=S(T, "lnd", 432 * (2 * t + 1 - s) + a, 432 * (2 * t + 1 - s) + b)))
+                used += k
+            g.remote_dma_fused(trs, local_sem=T.sem["l%d" % m])
+            tail.append((T.sem["l%d" % m], used))
+    for tk in tail: g.wait_ge(*tk)

@@ -3,7 +3,7 @@ from concourse.bass import DstId, RemoteDMATransfer
 from concourse.mybir import AluOpType as A, AxisListType as AX, ActivationFunctionType as F
 
 F32, BF, I32, U16 = "float32", "bfloat16", "int32", "uint16"
-RK = F32
+RK = "float16"
 SOFT_SAME = True
 SB = dict(
     xw=(3488, BF), RR=(2400, BF), Rs=(768, I32), nbw=(384, I32), enw=(384, I32), i1=(864, I32), i2=(384, I32), i3=(384, I32),
@@ -24,19 +24,19 @@ SB = dict(
     SS=(96, U16), PL=(96, U16), pc8=(96, F32), Go=(1536, BF), Pw=(1552, I32), par=(96, BF), eqs=(768, BF), si=(1536, BF), mn=(1536, BF), sn=(1536, BF),
     ks=(192, BF), O=(768, F32),
 )
-SB.update(Aux=(6912, BF), EW=(3840, F32), gz=(4224, F32), zf=(1536, F32), zb=(1536, BF), nbK=(768, F32), Zr=(1536, BF), Zf=(384, F32), ZE=(144, F32),
-          Vf=(768, F32), ab=(768, BF), rl=(768, BF), QL=(6, U16), junk=(288, BF), junk2=(160, BF), id1=(96, BF))
+SB.update(Aux=(6912, BF), EW=(3840, F32), gz=(4224, F32), zf=(1536, F32), zb=(1536, BF), nbK=(768, F32), Zr=(1536, BF), Zf=(384, F32), ZE=(192, F32),
+          Vf=(768, F32), M=(128 * 58, BF), PAT=(240, BF), XL=(112, U16), rl=(1536, BF), ind=(576, RK), MF=(144, RK), MR=(256, RK), cumd=(32, F32), i3=(32, I32), QL=(6, U16), junk=(288, BF), junk2=(160, BF), id1=(96, BF))
 for _k in ("T2", "keep", "ctr"):
     SB.pop(_k)
 ALIAS = dict(ga=("gz", 0), zf=("gz", 2688), EW=("gz", 0), Vf=("O", 0), b1=("si", 0), b2=("sn", 0), b3=("mn", 0), lo8=("Go", 0), hi8=("G1", 4608),
              Rs=("Pw", 0), nbw=("Pw", 768), enw=("Pw", 1152), CO=("tg", 0), Zf=("zn", 0))
 LOC, SCRATCH = {}, {}
-for _d in (F32, BF, I32, U16):
+for _d in (F32, BF, I32, U16, "float16"):
     _n, _o = 0, 0
     for _k, (_w, _e) in SB.items():
         if _e != _d or _k in ALIAS: continue
         if _o + _w > 16384: _n, _o = _n + 1, 0
-        LOC[_k] = ("%s%d" % (_d[0], _n), _o); _o += (_w + 31) // 32 * 32
+        LOC[_k] = ("%s%d" % (_d, _n), _o); _o += (_w + 31) // 32 * 32
         SCRATCH[LOC[_k][0]] = ("sbuf", [128, _o], _d)
 for _k, (_b, _o) in ALIAS.items():
     LOC[_k] = (LOC[_b][0], LOC[_b][1] + _o)
@@ -49,12 +49,13 @@ def S(T, n, a, b, rows=slice(None)):
 ACT_EQ = (1,)
 SPL = [2, 4]
 XACT = [0, 0, 0]
+ROT = 1
 HV = [8, 6, 8, 6, 8, 6]
-BIASES, PASSES, JIT = ((300.0, 0), (1000.0, 0), (2500.0, 0)), 5, 3000.0
+BIASES, PASSES, JIT, SEED, TRIES = ((300.0, 1), (700.0, 0), (700.0, 2)), 5, 800.0, 1, 2500
 for _k in range(4):
     SCRATCH["P%d" % _k] = ("psum", [128, 1024], F32)
 NDMA = 24
-SEMAPHORES = ["ev", "ea", "ep", "eg", "ax"] + ["d%d" % k for k in range(NDMA)] + ["r0", "r1", "r2", "r3", "l0", "l1", "l2", "l3"]
+SEMAPHORES = ["ev", "ea", "ep", "eg", "ax"] + ["d%d" % k for k in range(NDMA)] + [a + str(k) for a in "rl" for k in range(6)]
 CYC = 1.04
 GAT, SCA, PEC = 1.56, 3.8, 0.6
 
@@ -148,11 +149,11 @@ def program():
             return q.iota(ap(o), pat, base, cm, allow_small_or_imprecise_dtypes=True)
         add("g", fn, [], [o], 130 + 2 * CYC * wid(o))
 
-    def mm(*groups):
+    def mm(*groups, first=True, final=True):
         def fn(q, e, ap):
             for gr in groups:
                 for n, (o, l, r) in enumerate(gr):
-                    last = q.matmul(ap(o), ap(l), ap(r), n == 0, n == len(gr) - 1)
+                    last = q.matmul(ap(o), ap(l), ap(r), first and n == 0, final and n == len(gr) - 1)
             return last
         al = [x for gr in groups for x in gr]
         add("p", fn, [x[1] for x in al] + [x[2] for x in al], [x[0] for x in al],
@@ -165,13 +166,12 @@ def program():
     for q, ks in (("s", range(0, 4)), ("a", range(4, 8))):
         dma(q, [(lambda T, k=k, n=n, u=u: (S(T, "Rs", 0, 768, slice(k + u, 128, 16)), T[n][:, 48 * k:48 * k + 48])) for k in ks for n, u in (("nb", 0), ("en", 8))],
             [], [V("Rs", 0, 768)] if q == "s" else [V("Rs2", 0, 768)])
-    dma("s", [lambda T: (S(T, "nbw", 0, 384), T.nb[:, :]), lambda T: (S(T, "enw", 0, 384), T.en[:, :])], [], [V("nbw", 0, 384), V("enw", 0, 384)])
     dma("s", [lambda T: (S(T, "xw", 32, 1568), T.lens[:, :])], [], [V("xw", 32, 1568)], 3500.0)
 
     def zero(z, zw, parts, lat):
         ps = [(n, c, min(b, c + zw)) for n, a, b in parts for c in range(a, b, zw)]
         dma("s", [(lambda T, n=n, a=a, b=b: (S(T, n, a, b), S(T, z, 0, b - a))) for n, a, b in ps], [V(z, 0, zw)], [V(*p) for p in parts], lat)
-    mset(V("Zf", 0, 384), 0); zero("Zf", 384, [("EW", 0, 3072)], 6000.0)
+    mset(V("Zf", 0, 384), 0); zero("Zf", 384, [("EW", 384, 3456)], 6000.0)
     iota(V("Zr", 0, 1536), [[0, 1536]]); zero("Zr", 1536, [("xw", 1568, 2720), ("Z", 0, 1728), ("ix", 1920, 2688)], 5000.0)
     pcn = {}
 
@@ -243,16 +243,25 @@ def program():
     def wrap(o, n, a, b):
         return [(o, Z("W", 0), V(n, a, b, 2)), (o, Z("W", 8), V(n, a + 1, b, 2))]
     mm(wrap(V(P2, 512, 896), "RR", 32, 800)); cp(V("W", 0, 384), V(P2, 512, 896))
+    ts(Z("F"), Z("hi"), 2000, None, A.mult); ts(M("I1536"), M("I"), 1536, None, A.mult)
+    iota(V("Lf", 0, 384), [[2, 384]], 32); act(V("Lf", 0, 384), V("Lf", 0, 384), F.Identity, h)
+    iota(V("Lf", 384, 768), [[0, 16], [16, 24]], 1618); act(V("Lf", 384, 768), V("Lf", 384, 768), F.Identity, r)
+    tt(V("Kn", 0, 384), V("Lf", 0, 384), V(P2, 512, 896), A.is_gt); ts(V("Ke", 0, 768), V("RR", 32, 800), 1, None, A.is_ge)
+    o = V(P1, 0, 384)
+    ts(pc("wp"), h, -94, 96, A.mult, A.add); zm("p", l, pc("wp")); ts(Z("q"), Z("lo"), -1536, None, A.mult); ts(V("G", 0, 768), V("RR", 832, 1600), 16, None, A.is_ge)
+    mm([(o, Z(z_, 8 * u), V(n_, a_ + u, a_ + 768, 2)) for z_, n_, a_ in (("p", "RR", 832), ("q", "G", 0), ("lo", "G", 0), ("F", "Ke", 0)) for u in range(2)] +
+       [(o, M("I1536"), V("Kn", 0, 384))])
+    tt(V("tg", 384, 768), o, V("Lf", 384, 768), A.max); ts(V("EO", 0, 384), V("tg", 384, 768), -1618, None, A.add)
     mm(*[[(V(P3, a, b), Z("lo", 0), V("lo8", a, b)), (V(P3, a, b), Z("hi", 8), V("hi8", a, b))] for a, b in ((0, 512), (512, 800))])
     cp(V("RR", 1600, 2400), V(P3, 0, 800), "av")
     tt(M("Wc"), Z("W", 0), Z("W", 8), A.add); ts(M("Wk"), M("Wc"), -4096, None, A.mult); tt(M("W2"), Z("hi", 0), Z("W", 8), A.add)
-    ts(M("I256"), M("I"), 256, None, A.mult); ts(Z("F"), Z("hi"), 2000, None, A.mult)
+    ts(M("I256"), M("I"), 256, None, A.mult)
     ts(pc("h8"), h, 8, None, A.mult); ts(pc("l8"), l, 8, None, A.mult); ts(pc("l8b"), l, 8, -16, A.mult, A.add); ts(pc("l64"), l, 8, -64, A.mult, A.add)
     ts(pc("El", 8), V("PI", 8, 16), l, None, A.is_equal)
     tt(pc("we"), col(pc("El"), 0), wlh, A.mult); tt(pc("ws"), l, nh, A.mult)
     ts(pc("wu"), E(9), 32, E(8), A.mult, A.add); ts(pc("wu"), pc("wu"), 8, None, A.mult)
     tt(pc("wa"), E(8), E(9), A.add); tt(pc("wb"), E(10), E(11), A.add)
-    zm("all", 0, 1); zm("Y2", pc("h8"), -4); zm("e", 0, pc("we")); zm("s", 0, pc("ws")); zm("u", 0, pc("wu")); zm("A", pc("l8"), pc("wa")); zm("B", pc("l8b"), pc("wb"))
+    zm("all", 0, 1); zm("Y2", pc("h8"), -4); zm("s", 0, pc("ws")); zm("u", 0, pc("wu")); zm("A", pc("l8"), pc("wa")); zm("B", pc("l8b"), pc("wb"))
     zm("0", 0, E(0)); mset(V("junk2", 36, 37), 200)
     zm("2", 8, 1); tt(Z("2"), Z("2"), Z("all"), A.add)
     for m_ in range(4):
@@ -295,15 +304,17 @@ def program():
             tt(V("pu", 0, 64), V("pu", 0, 64), V("pu", 64, 128), A.subtract)
             if z: tt(V("pu", 0, 64), V("pu", 0, 64), dst, A.add)
             tt(dst, V("pu", 0, 64), V("pu", 128, 192), A.add)
-    ts(V("XL", 0, 8), V("PI", 8, 16), 0, r, A.mult, A.add)
-    for n in range(14): tt(M("X%d" % n), IND("PAT", 16 * n, 16 * n + 16, V("XL", 0, 8)), M("Blk"), A.mult)
-    iota(V("Vf", 0, 768), [[1, 768]], 32); ts(V("ZE", 0, 144), V("CMx", 0, 144), 0, E(0), A.is_equal, A.mult); iota(V("i2", 0, 384), [[0, 8], [16, 48]])
+    iota(V("m2", 0, 112), [[16, 14], [0, 8]], -224); iota(V("m3", 0, 112), [[0, 14], [1, 8]]); iota(V("PAT", 224, 240), [[0, 16]])
+    ts(V("m3", 0, 112), V("m3", 0, 112), gr, None, A.is_equal); ts(V("m2", 0, 112), V("m2", 0, 112), r, None, A.add)
+    tt(V("m2", 0, 112), V("m2", 0, 112), V("m3", 0, 112), A.mult); ts(V("XL", 0, 112), V("m2", 0, 112), 224, None, A.add)
+    for n in range(14): M("X%d" % n)
+    for n in range(0, 14, 2): cp(V("M", mn_["X%d" % n], mn_["X%d" % n] + 256), IND("PAT", 0, 240, V("XL", 8 * n, 8 * n + 16)), "a")
     iota(V("Tc", 0, 800), [[2048, 800]]); iota(V("Ac", 0, 800), [[0, 800]], 600); iota(V("Ac", 0, 1), [[0, 1]])
     iota(V("J8", 0, 768), [[0, 96], [8, 8]], 36); iota(V("ids", 0, 192), [[1, 192]], 2); iota(V("im", 0, 384), [[1, 384]]); iota(V("id1", 0, 96), [[1, 96]], 1)
     iota(V("big", 0, 384), [[0, 24], [1, 16]]); ts(V("big", 0, 384), V("big", 0, 384), r, 4096, A.is_equal, A.mult)
     iota(V("W2", 768, 1600), [[0, 832]], -8); ts(V("W2", 768, 1600), V("W2", 768, 1600), E(9), None, A.mult)
     iota(V("c884", 0, 192), [[0, 192]], 884); iota(V("cumb", 0, 1), [[0, 1]], 500); iota(V("num", 0, 2), [[0, 2]], 999); iota(V("Nw", 0, 2), [[0, 2]])
-    iota(V("xw", 0, 32), [[0, 32]]); iota(V("mid", 0, 168), [[0, 168]], 31)
+    iota(V("xw", 0, 32), [[0, 32]]); iota(V("mid", 0, 168), [[0, 168]], 12582912 + 31)
     ts(M("nI"), M("I"), -1, None, A.mult)
     iota(V("thr", 0, 48), [[0, 48]])
     iota(V("slf", 0, 96), [[672, 2], [2, 48]], 32); ts(V("slf", 0, 96), V("slf", 0, 96), h, None, A.add)
@@ -316,15 +327,13 @@ def program():
     for t in range(3):
         ts(pc("nm%d" % t), E(11), 49 + 12 * t, None, A.mult); act(V("NM", 384 * t, 384 * t + 384), V(P3, 0, 384), F.Identity, pc("nm%d" % t))
     a384 = lambda n: V(n, 0, 384)
-    ts(a384("i2"), a384("i2"), r, None, A.add)
-    tt(a384("i3"), a384("i2"), a384("nbw"), A.is_gt); ts(a384("i3"), a384("i3"), 1536, None, A.mult); tt(a384("i3"), a384("i3"), a384("enw"), A.add)
-    ts(a384("i2"), a384("i2"), 1537, None, A.add); ts(a384("i1"), a384("enw"), 0, None, A.is_lt); tt(a384("i1"), a384("i1"), a384("i2"), A.mult)
-    tt(a384("i3"), a384("i3"), a384("i1"), A.add); cp(a384("EO"), a384("i3"))
     for k in range(16):
-        eo = IND("EW", 0, 3840, V("EO", 24 * k, 24 * k + 24)); vf = V("Vf", 384 * (k % 2), 384 * (k % 2) + 384)
+        eo = IND("EW", 0, 3456, V("EO", 24 * k, 24 * k + 24)); vf = V("Vf", 384 * (k % 2), 384 * (k % 2) + 384)
+        iota(vf, [[1, 48], [0, 8]], 32 + 48 * k)
         add("a", lambda q, e, ap, eo=eo, vf=vf: q.activation(ap(eo), ap(vf), F.Silu), [vf], [eo], 80 + CYC * SCA * 384)
-    mm([(V(P3, 0, 192), V("ZE", 15 - i, 143 - i), V("EW", i, 3072, 16)) for i in range(16)])
-    ts(V("i2", 0, 192), V(P3, 0, 192), 1, None, A.max); cp(V("LA", 0, 96), V("i2", 0, 96)); cp(V("LB", 0, 96), V("i2", 96, 192))
+    dma("s", [(lambda T, u=u: (S(T, "ZE", 96 * u, 96 * u + 96), S(T, "EW", 384 + 1536 * u, 1920 + 1536 * u, slice(0, 128, 16)))) for u in range(2)],
+        [V("EW", 384, 3456)], [V("ZE", 0, 192)])
+    ts(V("i2", 0, 192), V("ZE", 0, 192), 1, None, A.max); cp(V("LA", 0, 96), V("i2", 0, 96)); cp(V("LB", 0, 96), V("i2", 96, 192))
     iota(V("ga", 1920, 2688), [[0, 768]]); iota(V("Pw", 0, 16), [[0, 16]], 300)
 
     sp = ((0, 512), (512, 576)); sq = ((0, 512), (512, 768)); late = ([], [])
@@ -336,11 +345,11 @@ def program():
         act(n576("fil"), V("RR", 128, 704), F.Sign, alt=lambda q, ap: q.tensor_scalar(ap(n576("fil")), ap(V("RR", 128, 704)), 1, None, A.is_ge))
         ops[-1]["ca"] = ops[-1]["cost"]; ops[-1]["cost"] = 360.0
         mm(*[[(V(P2, a, b), M("Hi"), V("fil", a, b)), (V(P2, a, b), M("D"), V("dead", a, b))] for a, b in sp])
-        eq(n576("ind"), V(P2, 0, 576), r, pc("nr"))
-        scan(n576("cumd"), n576("ind"), n576("ind"), 0.0, A.add, A.max)
-        mm([(V(P1, 0, 1), V("MF", 0, 128), V("cumd", 575, 576))]); cp(pc("off"), V(P1, 0, 1), "av")
-        act(V(P0, 0, 576), n576("cumd"), F.Identity, pc("off"), alt=lambda q, ap: q.tensor_scalar(ap(V(P0, 0, 576)), ap(n576("cumd")), ap(pc("off")), None, A.add)); tt(n576("rk"), V(P0, 0, 576), n576("ind"), A.mult)
-        mm(*[[(V(P2, a, b), V("MR", 0, 128), V("rk", a, b)), (V(P2, a, b), M("D"), V("dead", a, b))] for a, b in sp])
+        ts(n576("ind"), V(P2, 0, 576), r, None, A.is_equal)
+        scan(V(P0, 0, 576), n576("ind"), n576("ind"), 0.0, A.add, A.max)
+        cp(V("MF", 128, 129), V(P0, 575, 576)); mm([(V(P2, 0, 1), V("MF", 0, 128), V("MF", 128, 129))])
+        tt(n576("rk"), V(P0, 0, 576), n576("ind"), A.mult); ts(V("MR", 128, 256), M("Blk"), V(P2, 0, 1), None, A.mult)
+        mm(*[[(V(P2, a, b), M("D"), V("dead", a, b)), (V(P2, a, b), V("MR", 0, 128), V("rk", a, b)), (V(P2, a, b), V("MR", 128, 256), V("ind", a, b))] for a, b in sp])
         ts(n576("f1"), V(P2, 0, 576), pc("c0"), pc("c1"), A.max, A.min)
         act(V("val", 128, 704), n576("f1"), F.Exp, pc("cb"), -4.6)
         for c in range(8):
@@ -425,7 +434,7 @@ def program():
             mm([(pe, Z("lo", 0), ge), (pe, M("NLo"), V("pr", 384 * e, 384 * e + 384))])
             eq(V("e2", 384 * e, 384 * e + 384), pe, 0, 0.0)
         o = V(P1, 0, 48)
-        mm([(o, Z("u", i), V("G2", i, 768, 16)) for i in range(16)] + [(o, Z("s", i), V("e2", i, 768, 16)) for i in range(16)])
+        mm([(o, Z("u", i), V("G2", i, 768, 16)) for i in range(16)], final=False); mm([(o, Z("s", i), V("e2", i, 768, 16)) for i in range(16)], first=False)
         tt(V("s1", 0, 48), o, V("pk", 48, 96), A.max); ts(V("AL", 0, 48), V("s1", 0, 48), 512, None, A.add)
         x0 = 0
         for e in range(2):
@@ -435,21 +444,22 @@ def program():
         cp(V("LA", nl, nl + 24), V("j3", 0, 24)); cp(V("LB", nl, nl + 24), V("j3", 24, 48))
         tt(V(P3, 32, 800), V(P3, 32, 800), V("nbK", 0, 768), A.not_equal)
         if last: tt(V(P3, 128, 704), V(P3, 128, 704), n576("dead"), A.is_gt)
-        for Pn, kb, zz, o in ((P0, "Kn", "A", 32), (P2, "Ke", "B", 832)):
+        for Pn, kb, zz, o in ((P0, "Kn", "A", 32), (P1, "Ke", "B", 832)):
             tt(V(kb, 0, 768), V("RR", o, o + 768), V(P3, 32, 800), A.mult)
-            for a, b in sq:
-                mm([(V(Pn, a, b), M("I"), V(kb, a, b))] + [(V(Pn, a, b), Z(zz, s), V("Aux", x0 + 768 + 8 * a + s, x0 + 768 + 8 * b, 8)) for s in range(8)])
-                cp(V("RR", o + a, o + b), V(Pn, a, b), "av")
+            for a, b in ((0, 384), (384, 768)):
+                po = V(Pn, a // 3 * 4, a // 3 * 4 + 384)
+                mm([(po, Z(zz, s), V("Aux", x0 + 768 + 8 * a + s, x0 + 768 + 8 * b, 8)) for s in range(8)], final=False); mm([(po, M("I"), V(kb, a, b))], first=False)
+                cp(V("RR", o + a, o + b), po, "av")
         for a in range(0, Et, 384):
             b = a + 384; z = a % 1536; zf, zb = V("zf", z, z + 384), V("zb", z, z + 384); xs = V("xw", 32 + a, 32 + b)
             cp(V("ga", a, b), IND("Aw", 768, 1568, V("LA", a // 16, b // 16)), "av")
             tt(zf, IND("Bw", 0, 800, V("LB", a // 16, b // 16)), V("ga", a, b), A.add)
             act(zb, zf, F.Abs)
-            o = V(P3, a // 384 % 2 * 512, a // 384 % 2 * 512 + 384)
+            o = V((P3, P1)[a // 768 % ROT], a // 384 % 2 * 512, a // 384 % 2 * 512 + 384)
             mm([(o, M("I"), xs), (o, M("nI"), zb)])
             act(V("ix", a, b), o, F.Sign, pc("mh"))
             if a // 384 < XACT[t]:
-                rr = V("rl", a % 768, a % 768 + 384); act(rr, o, F.Relu)
+                rr = V("rl", z, z + 384); act(rr, o, F.Relu)
                 mm([(o, M("I"), xs), (o, M("nI"), rr)]); cp(xs, o, "a")
             else:
                 tt(xs, xs, zb, A.min)
@@ -458,20 +468,20 @@ def program():
         ts(V("xw", 32 + Et, 416 + Et), a384("zn"), 255, None, A.min)
         act(V("ix", Et, Et + 384), a384("zn"), F.Sign, pc("mh"))
         dma("s", [lambda T: (S(T, "own", 0, 168), S(T, "ga", 0, 2688, slice(0, 128, 16)))], [V("ga", 0, 2688)], [V("own", 0, 168)])
-        wp = V(P1, 512, 896)
+        wp = V(P0, 0, 384)
         mm(wrap(wp, "RR", 32, 800))
         if not last: cp(V("W", 0, 384), wp)
         mm(*[wrap(V(P1, 48 * s, 48 * s + 48), "RR", 832 + 672 * s, 928 + 672 * s) for s in range(2)])
         cp(V("Eb", 0, 96), V(P1, 0, 96)); tt(V("Ebf", 0, 48), V(P1, 0, 48), V("dum", 0, 48), A.subtract); tt(V("Ebf", 48, 96), V(P1, 48, 96), V("dum", 48, 96), A.subtract)
         for s in range(2):
             m0 = 432 * (2 * t + s)
-            cp(V("snd", m0 + 384, m0 + 432), V(P1, 512 + 336 * s, 560 + 336 * s)); cp(V("nbs", 48 * s, 48 * s + 48), V(P1, 512 + 336 * s, 560 + 336 * s), "av")
+            cp(V("snd", m0 + 384, m0 + 432), V(P0, 336 * s, 48 + 336 * s)); cp(V("nbs", 48 * s, 48 * s + 48), V(P0, 336 * s, 48 + 336 * s))
             parts(cp, SPL[0], V("Go", 768 * s, 768 * s + 768), IND("xw", 0, 2720, V("Eb", 48 * s, 48 * s + 48)), "av")
             o = V(P3, 512 * s, 512 * s + 384)
             mm([(o, M("I256"), V("Go", 768 * s, 768 * s + 384)), (o, M("I"), V("Go", 768 * s + 384, 768 * s + 768))])
             cp(V("snd", m0, m0 + 384), o)
-        for k, a, b, lat in ([(3, 384, 432, 3000.0), (2, 0, 384, 5000.0)] if last else [(t, 0, 432, 5000.0)]):
-            add("g", (k, t, a, b), [V("snd", 864 * t + 432 * s + a, 864 * t + 432 * s + b) for s in range(2)], [V("net", k, k + 1)], 1500.0 if t else 3000.0, kind="send")
+        for k, a, b, lat in ((3 + t, 384, 432, 3000.0), (t, 0, 384, 5000.0)):
+            add("g", (k, t, a, b), [V("snd", 864 * t + 432 * s + a, 864 * t + 432 * s + b) for s in range(2)], [V("net", k, k + 1)], 1500.0 if k != 3 else 3000.0, kind="send")
             add("r", (k, t, a, b), [V("net", k, k + 1)], [V("lnd", 864 * t + 432 * s + a, 864 * t + 432 * s + b) for s in range(2)], 0.0, kind="recv", lat=lat)
         if last:
             for a, b in ((32, 1376), (1376, 2720)): act(V("xw", a, b), V("xw", a, b), F.Abs)
@@ -481,10 +491,11 @@ def program():
         ts(V("thr", 48, 96), V("nbs", 48, 96), 704, 1e6, A.is_lt, A.mult)
         o = V(P3, 0, 168)
         mm([(o, Z("all", i), V("ix", 168 * i, 168 * i + 168)) for i in range(16) if 168 * i < Et + 384])
-        ts(V("m1", 0, 168), V("own", 0, 168), 1.0 / 2048, None, A.mult); tt(V("m2", 0, 168), V("m1", 0, 168), V("mid", 0, 168), A.subtract)
-        ts(V("m3", 0, 168), o, 1.0, None, A.is_ge); tt(V("m2", 0, 168), V("m2", 0, 168), V("m3", 0, 168), A.mult); tt(V("mid", 0, 168), V("mid", 0, 168), V("m2", 0, 168), A.add)
+        act(V("m3", 0, 168), V("own", 0, 168), F.Identity, pc("md%d" % t), 1.0 / 2048)
+        ts(o, o, 1.0, None, A.is_ge); tt(V("m2", 0, 168), o, V("m3", 0, 168), A.mult); tt(V("mid", 0, 168), V("mid", 0, 168), V("m2", 0, 168), A.max)
         if last:
-            ts(V("m3", 0, 168), V("mid", 0, 168), -32, None, A.add)
+            ts(V("m1", 0, 168), V("mid", 0, 168), -12582912, None, A.add); ts(V("m1", 0, 168), V("m1", 0, 168), 1023, None, A.bitwise_and)
+            ts(V("m3", 0, 168), V("m1", 0, 168), -32, None, A.add)
             dma("s", [lambda T: (T.ymid[:, :], S(T, "m3", 0, 168))], [V("m3", 0, 168)], [V("out", 0, 1)])
 
         def rows_out(Pn, a, b, pa):
@@ -533,7 +544,8 @@ def program():
             dma("s", [lambda T: (T.ylen[:, :], S(T, "xw", 32, 2720))], [V("xw", 32, 2720)], [V("out", 1, 2)], 4000.0)
             dma("a", [lambda T: (T.ynb[:, :], S(T, "O", 0, 768, slice(0, 64))), lambda T: (T.yen[:, :], S(T, "O", 0, 768, slice(64, 128)))], [V("O", 0, 768)], [V("out", 2, 3)], 3000.0)
     pre = len(ops)
-    for n_, c_ in (("m15", -15.0), ("p85", 8.5), ("mh", -0.5), ("one", 1.0), ("mg", MG), ("mg2", 2 * MG), ("ns0", -31.0), ("ns1", -703.0), ("m1", -1.0)): mset(pc(n_), c_)
+    for n_, c_ in (("m15", -15.0), ("p85", 8.5), ("mh", -0.5), ("one", 1.0), ("mg", MG), ("mg2", 2 * MG), ("ns0", -31.0), ("ns1", -703.0), ("m1", -1.0),
+                   ("md0", 12582912.0 + 1024), ("md1", 12582912.0 + 2048), ("md2", 12582912.0 + 3072)): mset(pc(n_), c_)
     return ops[pre:] + ops[:pre]
 
 
@@ -578,10 +590,11 @@ def plan():
             pre_, post = (0.0, o["lat"]) if before is pred else (o["lat"], 0.0)
             for e in (fixed[i] if fixed else o["engs"]):
                 s = rt + pre_; at_ = 0; c = o.get("ca", o["cost"]) if e == "a" else o["cost"]
-                for at_, (a, b) in enumerate(busy[e] + [(1e18, 1e18)]):
-                    if s + c <= a: break
-                    s = max(s, b)
-                key = s + c + (bias if e == "v" else 0.0)
+                bz = busy[e]; at_ = len(bz)
+                while at_ and bz[at_ - 1][1] > s: at_ -= 1
+                while at_ < len(bz) and s + c > bz[at_][0]:
+                    s = max(s, bz[at_][1]); at_ += 1
+                key = s + c + (bias[i] if e == "v" else 0.0)
                 if best is None or key < best[0]: best = (key, s, e, at_, c)
             _, s, e, at_, c = best
             busy[e].insert(at_, (s, s + c)); t0[i] = s; fin[i] = s + c + post; eng[i] = e
@@ -592,13 +605,24 @@ def plan():
     pri = [0.0] * n
     for i in range(n - 1, -1, -1):
         pri[i] = ops[i]["cost"] + ops[i]["lat"] + SY + max([pri[j] for j in succ[i]] + [0.0])
-    top = None
+    top = None; zero = [0.0] * n
     for bias, seed in BIASES:
         rs = np.random.RandomState(seed); p = [x + float(y) for x, y in zip(pri, rs.uniform(0, JIT if seed else 0.0, n))]
         for _ in range(PASSES):
-            t0, fin, eng = place(p, pred, succ, None, bias)
-            if top is None or max(fin) < top[0]: top = (max(fin), t0, eng)
-            _, p, _ = place(fin, succ, pred, eng, 0.0)
+            t0, fin, eng = place(p, pred, succ, None, [bias] * n)
+            if top is None or max(fin) < top[0]: top = (max(fin), t0, eng, p, [bias] * n)
+            _, p, _ = place(fin, succ, pred, eng, zero)
+    rs = np.random.RandomState(SEED); cur = top
+    for _ in range(TRIES):
+        c0 = rs.uniform(0, cur[0]); w = rs.uniform(3000, 30000); amp = rs.choice([300.0, 1000.0, 3000.0]); z = rs.uniform(-amp, amp, n); u = rs.uniform(0, 1, n)
+        near = [abs(x - c0) < w for x in cur[1]]
+        p = [x + float(y) if m and k < 0.3 else x for x, y, m, k in zip(cur[3], z, near, u)]
+        bias = [float(rs.choice([0.0, 700.0, 5000.0])) if m and k > 0.9 else x for x, m, k in zip(cur[4], near, u)]
+        t0, fin, eng = place(p, pred, succ, None, bias)
+        if rs.uniform() < 0.3:
+            _, p, _ = place(fin, succ, pred, eng, zero); t0, fin, eng = place(p, pred, succ, None, bias)
+        if max(fin) <= cur[0] + 200.0: cur = (max(fin), t0, eng, p, bias)
+        if cur[0] < top[0]: top = cur
     for i, o in enumerate(ops): o["t0"] = top[1][i]; o["e"] = top[2][i]; o["pri"] = pri[i]
     return ops, sorted(range(n), key=lambda i: (top[1][i], i)), top[0]
 

@@ -1,37 +1,32 @@
 import numpy as np
 from concourse.bass import DstId, RemoteDMATransfer
-from concourse.mybir import AluOpType as A, AxisListType as AX, ActivationFunctionType as F
+from concourse.mybir import AluOpType as A, ActivationFunctionType as F
 
-F32, BF, I32, U16 = "float32", "bfloat16", "int32", "uint16"
-RK = "float16"
-SOFT_SAME = True
+F32, BF, I32, U16, H16 = "float32", "bfloat16", "int32", "uint16", "float16"
 SB = dict(
-    xw=(3488, BF), RR=(2400, BF), Rs=(768, I32), nbw=(384, I32), enw=(384, I32), i1=(864, I32), i2=(384, I32), i3=(384, I32),
-    EO=(384, U16), EW=(3840, BF), LA=(168, U16), LB=(168, U16), W=(384, U16), SL=(48, U16), XL=(8, U16),
-    lo8=(800, BF), hi8=(800, BF), Tc=(800, F32), NM=(1152, BF), b1=(800, BF), b2=(800, BF), b3=(800, BF),
-    PC=(128, F32), PI=(64, I32), CMx=(144, BF), CH=(128, BF), CO=(192, F32), MZ=(144 * 20, BF), M=(128 * 56, BF), ZO=(192, BF),
-    MF=(128, F32), MR=(128, RK), PAT=(224, BF), cod=(64, BF), pu=(192, BF), jk=(64, I32),
-    fil=(576, BF), dead=(576, BF), ind=(576, BF), cumd=(576, F32), f1=(576, F32), rk=(576, RK), val=(800, BF), G1=(6144, BF), S1=(800, BF),
-    sg=(576, BF), cho=(576, BF), cumc=(592, BF), c96=(576, BF), ctr=(576, BF), junk=(576, BF), junk2=(576, BF), vc=(16, F32), vd=(16, F32), VL=(18, U16),
-    Rv=(288, BF), fv=(96, BF), UL=(144, U16), Us=(48, U16), s1=(96, F32), s2=(96, F32), s3=(96, F32), pos=(48, F32), pk=(192, F32),
-    Lf=(768, F32), tg=(768, F32), Aw=(1568, F32), Ac=(800, F32), Tt=(800, F32), T2=(800, F32), Bw=(800, F32), keep=(768, BF), Kn=(768, BF), Ke=(768, BF),
+    xz=(3488, BF), xw=(2720, BF), Lu=(1536, BF), RR=(2400, BF), Rs=(768, I32), i1=(864, I32), i2=(384, I32),
+    EO=(384, U16), EW=(3840, F32), LA=(168, U16), LB=(168, U16), W=(384, U16), SL=(48, U16), XL=(112, U16),
+    lo8=(800, BF), hi8=(800, BF), c8=(384, BF), cn=(36, H16), NM=(1152, BF), b1=(800, BF), b2=(800, BF), b3=(800, BF),
+    PC=(128, F32), PI=(64, I32), CMx=(144, BF), CH=(128, BF), CO=(192, F32), MZ=(144 * 20, BF), M=(128 * 60, BF), BR=(2048, BF), ZO=(192, BF),
+    PAT=(240, BF), cod=(64, BF), pu=(192, BF), jk=(64, I32), SEL=(16, BF), SW=(272, H16), CX=(96, BF),
+    fil=(576, BF), GD=(800, BF), G1=(6144, BF), KS=(192, F32), OWN=(192, F32), KI=(96, I32), XI=(96, I32), AI=(144, I32), e1=(48, F32), XR=(384, BF), OH=(3456, BF),
+    AE=(96, H16), AO=(96, U16), ch=(36, BF), cc=(40, F32), rkw=(40, F32), cw=(36, BF), TG=(800, F32), ctr=(576 * 3, BF), tg=(768, F32), gb=(1536, F32), clr=(768, BF),
+    junk=(288, BF), junk2=(96, BF), id0=(96, BF), vc=(16, F32), vd=(16, F32), QL=(6, U16), VL=(12, U16),
+    Rv=(192, BF), fv=(96, BF), UL=(48, U16), s1=(96, F32), s2=(96, F32), s3=(96, F32), pos=(48, F32), pk=(192, F32),
+    Lf=(768, F32), Aw=(800, F32), Bw=(800, F32), Kn=(768, BF), Ke=(768, BF),
     G=(768, BF), EQ=(2304, BF), wish=(192, BF), nf=(96, BF), Nw=(400, BF), fw=(384, BF), ok=(192, BF), cumb=(208, F32), c884=(192, F32),
     num=(208, F32), big=(384, BF), ws=(192, F32), we=(192, F32), ZL=(12, U16), Z=(1728, BF), ids=(192, BF), mx=(384, BF), wr=(384, BF), CL=(24, U16),
     im=(384, F32), oh=(384, BF), pr=(768, BF), j1=(48, I32), j2=(48, I32), j3=(48, I32), IL=(48, U16), W2=(1600, BF), J8=(768, BF), G2=(768, BF), e2=(768, BF),
-    AL=(48, U16), Aux=(6912 * 3, BF), ga=(2688, F32), zf=(2304, F32), zn=(384, F32), zb=(2304, BF), ix=(2688, BF), own=(168, F32), mid=(168, F32),
-    m1=(168, I32), m2=(168, F32), m3=(168, F32),
+    AL=(48, U16), Aux=(6912, BF), gz=(3840, F32), ga=(2688, F32), zb=(1536, BF), mk=(1536, BF), rl=(2304, BF), zn=(384, F32), ix=(2688, BF),
+    own=(168, F32), mid=(168, F32), m1=(168, I32), m2=(168, F32), m3=(168, F32),
     snd=(432 * 6, U16), lnd=(432 * 6, U16), Eb=(96, U16), nbs=(96, F32), Ebf=(96, F32), slf=(96, F32), dum=(96, F32), thr=(96, F32), can=(96, F32), q1=(96, F32),
     SS=(96, U16), PL=(96, U16), pc8=(96, F32), Go=(1536, BF), Pw=(1552, I32), par=(96, BF), eqs=(768, BF), si=(1536, BF), mn=(1536, BF), sn=(1536, BF),
-    ks=(192, BF), O=(768, F32),
+    ks=(192, BF), O=(768, F32), Zr=(1536, BF), Zf=(384, F32), ZE=(192, F32), Vf=(768, F32), V0=(384, F32),
 )
-SB.update(Aux=(6912, BF), EW=(3840, F32), gz=(4224, F32), zf=(1536, F32), zb=(1536, BF), nbK=(768, F32), Zr=(1536, BF), Zf=(384, F32), ZE=(192, F32),
-          Vf=(768, F32), M=(128 * 58, BF), PAT=(240, BF), XL=(112, U16), rl=(1536, BF), ind=(576, RK), MF=(144, RK), MR=(256, RK), cumd=(32, F32), i3=(32, I32), QL=(6, U16), junk=(288, BF), junk2=(160, BF), id1=(96, BF))
-for _k in ("T2", "keep", "ctr"):
-    SB.pop(_k)
-ALIAS = dict(ga=("gz", 0), zf=("gz", 2688), EW=("gz", 0), Vf=("O", 0), b1=("si", 0), b2=("sn", 0), b3=("mn", 0), lo8=("Go", 0), hi8=("G1", 4608),
-             Rs=("Pw", 0), nbw=("Pw", 768), enw=("Pw", 1152), CO=("tg", 0), Zf=("zn", 0))
+ALIAS = dict(xw=("xz", 768), ga=("gz", 0), EW=("gz", 0), Vf=("O", 0), b1=("si", 0), b2=("sn", 0), b3=("mn", 0), lo8=("Go", 0), hi8=("OH", 0),
+             Rs=("Pw", 0), CO=("gb", 0), Zf=("zn", 0), Lf=("gb", 768), tg=("gb", 0))
 LOC, SCRATCH = {}, {}
-for _d in (F32, BF, I32, U16, "float16"):
+for _d in (F32, BF, I32, U16, H16):
     _n, _o = 0, 0
     for _k, (_w, _e) in SB.items():
         if _e != _d or _k in ALIAS: continue
@@ -46,26 +41,27 @@ def S(T, n, a, b, rows=slice(None)):
     return T[LOC[n][0]][rows, LOC[n][1] + a:LOC[n][1] + b]
 
 
-ACT_EQ = (1,)
 SPL = [2, 4]
-XACT = [0, 0, 0]
-ROT = 1
-HV = [8, 6, 8, 6, 8, 6]
-BIASES, PASSES, JIT, SEED, TRIES = ((300.0, 1), (700.0, 0), (700.0, 2)), 5, 800.0, 1, 2500
+ACC = [1, 1, 0]
+DV = [0, 0, 0]
+FOLD = [((0, 384), (384, 768)), ((0, 96), (672, 768), (96, 384), (384, 672))]
+EWV = 0
+CHAIN, FAR = ("G1", "G", "EQ", "e2", "G2", "RR", "Nw", "wish", "nf", "fil", "GD"), 5000.0
+BIASES, PASSES, JIT, SEED, TRIES = ((300.0, 1), (700.0, 0), (700.0, 2)), 5, 800.0, 1, 4000
 for _k in range(4):
     SCRATCH["P%d" % _k] = ("psum", [128, 1024], F32)
-NDMA = 24
+NDMA = 48
 SEMAPHORES = ["ev", "ea", "ep", "eg", "ax"] + ["d%d" % k for k in range(NDMA)] + [a + str(k) for a in "rl" for k in range(6)]
 CYC = 1.04
-GAT, SCA, PEC = 1.56, 3.8, 0.6
+GAT, SCA, PEC = 1.56, 3.8, 0.55
 
 
-def V(n, a, b, s=1):
-    return (n, a, b, s, None)
+def V(n, a, b, s=1, rows=None):
+    return (n, a, b, s, None, rows)
 
 
 def IND(n, a, b, off):
-    return (n, a, b, 1, off)
+    return (n, a, b, 1, off, None)
 
 
 def wid(v):
@@ -73,7 +69,20 @@ def wid(v):
 
 
 def two(v):
-    return v[0] in SB and SB[v[0]][1] in (BF, U16)
+    return v[0] in SB and SB[v[0]][1] in (BF, U16, H16)
+
+
+def make_ap(T, v, step):
+    if v == "step": return step
+    if not isinstance(v, tuple): return v
+    nm, o = LOC.get(v[0], (v[0], 0)); rows = slice(*v[5]) if v[5] else slice(None)
+    x = T[nm][rows, o + v[1]:o + v[2]] if v[3] == 1 else T[nm][rows, o + v[1]:o + v[2]:v[3]]
+    return x.indirect(make_ap(T, v[4], step)) if v[4] else x
+
+
+def transfers(o):
+    m, t, a, b = o["fn"]
+    return [(2 * s - 1, V("snd", 432 * (2 * t + s) + a, 432 * (2 * t + s) + b), V("lnd", 432 * (2 * t + 1 - s) + a, 432 * (2 * t + 1 - s) + b)) for s in range(2)]
 
 
 def program():
@@ -103,15 +112,27 @@ def program():
         add("v", fn, [i, s1, s2], [o], 60 + CYC * el(o, i, 0.5 if two(o) and two(i) else 1))
 
     def tt(o, a, b, op):
-        ps = a[0][0] == "P" and a[0] not in SB or b[0] not in SB
-        base = 1 if ps else (1.5 if two(o) and two(a) and two(b) else 2)
+        base = 1 if a[0] not in SB or b[0] not in SB else (1.5 if two(o) and two(a) and two(b) else 2)
         add("v", lambda q, e, ap: q.tensor_tensor(ap(o), ap(a), ap(b), op), [a, b], [o], 60 + CYC * el(o, a, base))
 
+    def either(o, i, fv, fa, more=(), engs="av"):
+        add(engs, lambda q, e, ap: fv(q, ap) if e == "v" else fa(q, ap), [i] + list(more), [o], 60 + CYC * el(o, i, 0.5 if two(o) and two(i) else 1))
+        ops[-1]["ca"] = 80 + CYC * el(o, i, 1)
+
     def cp(o, i, engs="v"):
-        def fn(q, e, ap):
-            if e == "v": return q.tensor_copy(ap(o), ap(i))
-            return q.activation(ap(o), ap(i), F.Copy)
-        add(engs, fn, [i], [o], 60 + CYC * el(o, i, 0.5 if two(o) and two(i) and engs == "v" else 1))
+        either(o, i, lambda q, ap: q.tensor_copy(ap(o), ap(i)), lambda q, ap: q.activation(ap(o), ap(i), F.Copy), engs=engs)
+
+    def neg(o, i, engs="av"):
+        either(o, i, lambda q, ap: q.tensor_scalar(ap(o), ap(i), -1.0, None, A.mult), lambda q, ap: q.activation(ap(o), ap(i), F.Copy, scale=-1.0), engs=engs)
+
+    def relu(o, i, bias=None):
+        if bias is None:
+            either(o, i, lambda q, ap: q.tensor_scalar(ap(o), ap(i), 0.0, None, A.max), lambda q, ap: q.activation(ap(o), ap(i), F.Relu))
+        else:
+            either(o, i, lambda q, ap: q.tensor_scalar(ap(o), ap(i), ap(bias), 0.0, A.add, A.max), lambda q, ap: q.activation(ap(o), ap(i), F.Relu, bias=ap(bias)), [bias])
+
+    def pos_(o, i):
+        either(o, i, lambda q, ap: q.tensor_scalar(ap(o), ap(i), 0.5, None, A.is_gt), lambda q, ap: q.activation(ap(o), ap(i), F.Sign))
 
     def act(o, i, f, bias=0.0, scale=1.0, acc=None, alt=None):
         def fn(q, e, ap):
@@ -121,17 +142,15 @@ def program():
         add("av" if alt else "a", fn, [i, bias, scale], [o] + ([acc] if acc else []), 80 + CYC * wid(o))
 
     def eq(o, i, c, nc):
-        tmp = o
-
         def fn(q, e, ap):
             if e == "v": return q.tensor_scalar(ap(o), ap(i), ap(c), None, A.is_equal)
-            ap("step")(q.activation(ap(tmp), ap(i), F.Abs, bias=ap(nc)))
-            return q.activation(ap(o), ap(tmp), F.Relu, bias=ap(pc("one")), scale=-1.0)
+            ap("step")(q.activation(ap(o), ap(i), F.Abs, bias=ap(nc)))
+            return q.activation(ap(o), ap(o), F.Relu, bias=ap(pc("one")), scale=-1.0)
         add("av", fn, [i, c, nc, pc("one")], [o], 60 + CYC * wid(o)); ops[-1]["ca"] = 270 + 2 * CYC * wid(o)
 
     def parts(f, k, *vs):
         def cut(v, j):
-            if v[4]: return (v[0], v[1], v[2], 1, cut(v[4], j))
+            if v[4]: return (v[0], v[1], v[2], 1, cut(v[4], j), None)
             w = (v[2] - v[1]) // k
             return V(v[0], v[1] + j * w, v[1] + j * w + w)
         for j in range(k): f(*[cut(v, j) if isinstance(v, tuple) else v for v in vs])
@@ -147,7 +166,11 @@ def program():
         def fn(q, e, ap):
             if SB[o[0]][1] == I32: return q.iota(ap(o), pat, base, cm)
             return q.iota(ap(o), pat, base, cm, allow_small_or_imprecise_dtypes=True)
-        add("g", fn, [], [o], 130 + 2 * CYC * wid(o))
+        add("g", fn, [], [o], 150 + 2 * CYC * wid(o))
+
+    def where0(o, pat, base, cm, fill):
+        z = V("Zr", 0, wid(o))
+        add("g", lambda q, e, ap: q.affine_select(ap(o), ap(z), pat, A.not_equal, fill, base, cm), [z], [o], 200 + 2 * CYC * wid(o))
 
     def mm(*groups, first=True, final=True):
         def fn(q, e, ap):
@@ -157,22 +180,23 @@ def program():
             return last
         al = [x for gr in groups for x in gr]
         add("p", fn, [x[1] for x in al] + [x[2] for x in al], [x[0] for x in al],
-            60 + sum(PEC * max(64, wid(o)) * (4 if SB[r[0]][1] == F32 else 1) for o, l, r in al))
+            60 + sum(PEC * max(min(64, wid(l)), wid(o)) * (4 if SB[r[0]][1] == F32 else 1) for o, l, r in al))
 
     def dma(eng, pairs, rd, wr, lat=2200.0):
-        add(eng, pairs, rd, wr, 60.0 * len(pairs), kind="d", lat=lat)
+        add(eng, pairs, rd, wr, (1000.0 if eng == "g" else 60.0) * len(pairs), kind="d", lat=lat)
 
     P0, P1, P2, P3 = "P0", "P1", "P2", "P3"
     for q, ks in (("s", range(0, 4)), ("a", range(4, 8))):
         dma(q, [(lambda T, k=k, n=n, u=u: (S(T, "Rs", 0, 768, slice(k + u, 128, 16)), T[n][:, 48 * k:48 * k + 48])) for k in ks for n, u in (("nb", 0), ("en", 8))],
             [], [V("Rs", 0, 768)] if q == "s" else [V("Rs2", 0, 768)])
     dma("s", [lambda T: (S(T, "xw", 32, 1568), T.lens[:, :])], [], [V("xw", 32, 1568)], 3500.0)
+    neg(V("xw", 32, 1568), V("xw", 32, 1568))
 
     def zero(z, zw, parts, lat):
         ps = [(n, c, min(b, c + zw)) for n, a, b in parts for c in range(a, b, zw)]
         dma("s", [(lambda T, n=n, a=a, b=b: (S(T, n, a, b), S(T, z, 0, b - a))) for n, a, b in ps], [V(z, 0, zw)], [V(*p) for p in parts], lat)
     mset(V("Zf", 0, 384), 0); zero("Zf", 384, [("EW", 384, 3456)], 6000.0)
-    iota(V("Zr", 0, 1536), [[0, 1536]]); zero("Zr", 1536, [("xw", 1568, 2720), ("Z", 0, 1728), ("ix", 1920, 2688)], 5000.0)
+    mset(V("Zr", 0, 1536), 0); zero("Zr", 1536, [("xw", 1568, 2720), ("Z", 0, 1728), ("ix", 1920, 2688), ("GD", 0, 128), ("GD", 704, 800)], 5000.0)
     pcn = {}
 
     def pc(n, w=1):
@@ -216,19 +240,21 @@ def program():
         if n not in mn_: mn_[n] = 128 * len(mn_)
         return V("M", mn_[n], mn_[n] + 128)
 
+    def half(v, u):
+        return V(v[0], v[1] + 64 * u, v[1] + 64 * u + 64)
+
     def zm(n, tg_, w):
         ts(Z(n), V("CMx", 0, 144), tg_, w, A.is_equal, A.mult)
+
+    def diag(n, c):
+        where0(M(n), [[1, 128]], 0, -1, float(c))
     zm("lo", l, nh); zm("hi", l, h); zm("W", l, wlh)
     ts(M("I"), CM0, r, None, A.is_equal)
     ts(V("CH", 0, 128), V("CH", 0, 128), pc("g2"), None, A.subtract)
     ts(M("t1"), V("CH", 0, 128), 0, None, A.is_ge); ts(M("t2"), V("CH", 0, 128), 2, None, A.is_lt); tt(M("Blk"), M("t1"), M("t2"), A.mult)
-    ts(M("Hi"), M("Blk"), h, None, A.mult); ts(M("D"), M("Blk"), E(0), 1000, A.mult, A.mult)
+    ts(pc("mhh"), h, -1, None, A.mult); ts(M("NHi"), M("Blk"), pc("mhh"), None, A.mult)
     ts(M("t1"), CM0, r, None, A.is_gt); tt(M("Tri"), M("t1"), M("Blk"), A.mult)
-    cp(V("MF", 0, 128), M("Tri")); cp(V("MR", 0, 128), M("Blk"))
-    ts(pc("n128"), h, -128, None, A.mult); ts(pc("nr"), r, -1, None, A.mult)
-    ts(pc("c0"), r, 36, None, A.mult); ts(pc("c1"), r, 36, 37, A.mult, A.add); ts(pc("cb"), r, 36 * 4.6, 84.0, A.mult, A.add)
-    ts(M("N92"), M("I"), -92, None, A.mult)
-    mset(V("dead", 0, 576), 0); mset(V("val", 0, 128), 0); mset(V("val", 704, 800), 0); mset(V("S1", 0, 32), 0); iota(V("c96", 0, 576), [[0, 576]], 96); mset(V("cumc", 0, 16), 0)
+    ts(pc("n128"), h, -128, None, A.mult)
     mset(V("RR", 0, 32), 0); mset(V("RR", 800, 832), 0)
     SLv = V("SL", 0, 48); Rsw = IND("Rs", 0, 768, SLv)
     ts(V("b1", 0, 768), Rsw, 1.0 / 32, 128.515625, A.mult, A.add); ops[-1]["rd"].append(V("Rs2", 0, 768))
@@ -237,13 +263,12 @@ def program():
     tt(V("b3", 0, 768), Rsw, V("b2", 0, 768), A.subtract)
     for Pn, za, zb, o in ((P0, Z("lo", 0), Z("lo", 8), 32), (P1, Z("hi", 0), Z("hi", 8), 832)):
         mm(*[[(V(Pn, a, b), za, V("b3", a, b)), (V(Pn, a, b), zb, V("b1", a, b))] for a, b in ((0, 512), (512, 768))])
-        act(V("RR", o, o + 768), V(Pn, 0, 768), F.Relu, pc("n128"),
-            alt=lambda q, ap, o=o, Pn=Pn: q.tensor_scalar(ap(V("RR", o, o + 768)), ap(V(Pn, 0, 768)), ap(pc("n128")), 0.0, A.add, A.max))
+        relu(V("RR", o, o + 768), V(Pn, 0, 768), pc("n128"))
 
     def wrap(o, n, a, b):
         return [(o, Z("W", 0), V(n, a, b, 2)), (o, Z("W", 8), V(n, a + 1, b, 2))]
     mm(wrap(V(P2, 512, 896), "RR", 32, 800)); cp(V("W", 0, 384), V(P2, 512, 896))
-    ts(Z("F"), Z("hi"), 2000, None, A.mult); ts(M("I1536"), M("I"), 1536, None, A.mult)
+    ts(Z("F"), Z("hi"), 2000, None, A.mult); diag("I1536", 1536)
     iota(V("Lf", 0, 384), [[2, 384]], 32); act(V("Lf", 0, 384), V("Lf", 0, 384), F.Identity, h)
     iota(V("Lf", 384, 768), [[0, 16], [16, 24]], 1618); act(V("Lf", 384, 768), V("Lf", 384, 768), F.Identity, r)
     tt(V("Kn", 0, 384), V("Lf", 0, 384), V(P2, 512, 896), A.is_gt); ts(V("Ke", 0, 768), V("RR", 32, 800), 1, None, A.is_ge)
@@ -254,15 +279,24 @@ def program():
     tt(V("tg", 384, 768), o, V("Lf", 384, 768), A.max); ts(V("EO", 0, 384), V("tg", 384, 768), -1618, None, A.add)
     mm(*[[(V(P3, a, b), Z("lo", 0), V("lo8", a, b)), (V(P3, a, b), Z("hi", 8), V("hi8", a, b))] for a, b in ((0, 512), (512, 800))])
     cp(V("RR", 1600, 2400), V(P3, 0, 800), "av")
-    tt(M("Wc"), Z("W", 0), Z("W", 8), A.add); ts(M("Wk"), M("Wc"), -4096, None, A.mult); tt(M("W2"), Z("hi", 0), Z("W", 8), A.add)
-    ts(M("I256"), M("I"), 256, None, A.mult)
+    where0(V("SEL", 0, 16), [[0, 2], [16, 8]], 0, -1, -131072.0)
+    where0(M("SE"), [[1, 8], [-8, 2], [16, 8]], 8, -1, 1.0)
+    iota(M("SN"), [[1, 8], [0, 2], [16, 8]]); ts(pc("gl"), l, pc("g16"), None, A.add); ts(pc("w128"), wlh, 128, None, A.mult)
+    ts(M("SN"), M("SN"), pc("gl"), pc("w128"), A.is_equal, A.mult)
+    iota(V("CX", 0, 48), [[0, 48]], -8); iota(V("CX", 48, 96), [[0, 4], [16, 2], [0, 6]])
+    iota(V("im", 0, 384), [[1, 384]])
+    ts(pc("sw"), pc("g16"), 2, 16, A.mult, A.add); ts(pc("sw"), pc("sw"), r, None, A.add); ts(V("SW", 0, 272), V("im", 0, 272), pc("sw"), None, A.is_equal)
+    for u in range(2): where0(V("BR", 1024 * u, 1024 * u + 1024), [[1, 8], [16, 8], [0, 16]], 8 * u, -1, 4096.0)
+    iota(V("OWN", 96, 192), [[0, 96]], 1000000); iota(V("cc", 0, 1), [[0, 1]], 500); iota(V("rkw", 36, 37), [[0, 1]], 999); iota(V("id0", 0, 96), [[1, 96]])
+    diag("N128", -128); diag("D2", -2); diag("I256", 256); diag("nI", -1)
+    tt(M("Wc"), Z("W", 0), Z("W", 8), A.add); ts(M("Wk"), M("Wc"), 4096, None, A.mult); tt(M("W2"), Z("hi", 0), Z("W", 8), A.add)
     ts(pc("h8"), h, 8, None, A.mult); ts(pc("l8"), l, 8, None, A.mult); ts(pc("l8b"), l, 8, -16, A.mult, A.add); ts(pc("l64"), l, 8, -64, A.mult, A.add)
     ts(pc("El", 8), V("PI", 8, 16), l, None, A.is_equal)
     tt(pc("we"), col(pc("El"), 0), wlh, A.mult); tt(pc("ws"), l, nh, A.mult)
     ts(pc("wu"), E(9), 32, E(8), A.mult, A.add); ts(pc("wu"), pc("wu"), 8, None, A.mult)
     tt(pc("wa"), E(8), E(9), A.add); tt(pc("wb"), E(10), E(11), A.add)
     zm("all", 0, 1); zm("Y2", pc("h8"), -4); zm("s", 0, pc("ws")); zm("u", 0, pc("wu")); zm("A", pc("l8"), pc("wa")); zm("B", pc("l8b"), pc("wb"))
-    zm("0", 0, E(0)); mset(V("junk2", 36, 37), 200)
+    zm("0", 0, E(0)); zm("ir", 0, r)
     zm("2", 8, 1); tt(Z("2"), Z("2"), Z("all"), A.add)
     for m_ in range(4):
         ts(pc("sp%d" % m_), h, 2 * m_ + 1, None, A.add); zm("sp%d" % m_, l, pc("sp%d" % m_))
@@ -308,107 +342,127 @@ def program():
     ts(V("m3", 0, 112), V("m3", 0, 112), gr, None, A.is_equal); ts(V("m2", 0, 112), V("m2", 0, 112), r, None, A.add)
     tt(V("m2", 0, 112), V("m2", 0, 112), V("m3", 0, 112), A.mult); ts(V("XL", 0, 112), V("m2", 0, 112), 224, None, A.add)
     for n in range(14): M("X%d" % n)
-    for n in range(0, 14, 2): cp(V("M", mn_["X%d" % n], mn_["X%d" % n] + 256), IND("PAT", 0, 240, V("XL", 8 * n, 8 * n + 16)), "a")
-    iota(V("Tc", 0, 800), [[2048, 800]]); iota(V("Ac", 0, 800), [[0, 800]], 600); iota(V("Ac", 0, 1), [[0, 1]])
-    iota(V("J8", 0, 768), [[0, 96], [8, 8]], 36); iota(V("ids", 0, 192), [[1, 192]], 2); iota(V("im", 0, 384), [[1, 384]]); iota(V("id1", 0, 96), [[1, 96]], 1)
+    for n in range(0, 14, 2): cp(V("M", mn_["X%d" % n], mn_["X%d" % n] + 256), IND("PAT", 0, 240, V("XL", 8 * n, 8 * n + 16)), "av")
+    iota(V("c8", 0, 384), [[0, 384]], 8); iota(V("Bw", 0, 32), [[0, 32]]); iota(V("Aw", 0, 32), [[-1024, 2], [0, 16]])
+    iota(V("TG", 0, 128), [[0, 128]], -1024); iota(V("TG", 704, 800), [[0, 96]], -1024); ts(V("pk", 0, 36), V("pos", 0, 36), 128, None, A.add)
+    iota(V("J8", 0, 768), [[0, 96], [8, 8]], 36); iota(V("ids", 0, 192), [[1, 192]], 2)
     iota(V("big", 0, 384), [[0, 24], [1, 16]]); ts(V("big", 0, 384), V("big", 0, 384), r, 4096, A.is_equal, A.mult)
     iota(V("W2", 768, 1600), [[0, 832]], -8); ts(V("W2", 768, 1600), V("W2", 768, 1600), E(9), None, A.mult)
     iota(V("c884", 0, 192), [[0, 192]], 884); iota(V("cumb", 0, 1), [[0, 1]], 500); iota(V("num", 0, 2), [[0, 2]], 999); iota(V("Nw", 0, 2), [[0, 2]])
     iota(V("xw", 0, 32), [[0, 32]]); iota(V("mid", 0, 168), [[0, 168]], 12582912 + 31)
-    ts(M("nI"), M("I"), -1, None, A.mult)
     iota(V("thr", 0, 48), [[0, 48]])
     iota(V("slf", 0, 96), [[672, 2], [2, 48]], 32); ts(V("slf", 0, 96), V("slf", 0, 96), h, None, A.add)
     iota(V("pc8", 0, 96), [[768, 2], [16, 48]], 15); ts(V("pc8", 0, 96), V("pc8", 0, 96), pc("h8"), None, A.add)
-    for s in range(2): ts(V("dum", 48 * s, 48 * s + 48), V("pos", 0, 48), 2720, None, A.add)
-    ts(V("pk", 0, 48), V("pos", 0, 48), 1232, None, A.add); ts(V("pk", 48, 96), V("pos", 0, 48), -512, None, A.add); ts(V("pk", 96, 108), V("pos", 0, 12), 308, None, A.add)
-    ts(V("pk", 112, 118), V("pos", 0, 6), 0.5, None, A.add)
+    for s in range(2): cp(V("dum", 48 * s, 48 * s + 48), V("pos", 0, 48), "av")
+    ts(V("pk", 48, 96), V("pos", 0, 48), -512, None, A.add); ts(V("pk", 96, 108), V("pos", 0, 12), 308, None, A.add)
+    ts(V("pk", 112, 118), V("pos", 0, 6), 500.5, None, A.add)
     ts(M("t1"), M("I"), E(10), None, A.mult); ts(M("t2"), M("I"), E(11), None, A.mult)
     mm([(V(P3, 0, 384), M("t1"), V("lo8", 0, 384)), (V(P3, 0, 384), M("t2"), V("hi8", 0, 384))])
     for t in range(3):
         ts(pc("nm%d" % t), E(11), 49 + 12 * t, None, A.mult); act(V("NM", 384 * t, 384 * t + 384), V(P3, 0, 384), F.Identity, pc("nm%d" % t))
     a384 = lambda n: V(n, 0, 384)
+    if EWV: iota(a384("V0"), [[1, 48], [0, 8]], 32)
     for k in range(16):
         eo = IND("EW", 0, 3456, V("EO", 24 * k, 24 * k + 24)); vf = V("Vf", 384 * (k % 2), 384 * (k % 2) + 384)
-        iota(vf, [[1, 48], [0, 8]], 32 + 48 * k)
-        add("a", lambda q, e, ap, eo=eo, vf=vf: q.activation(ap(eo), ap(vf), F.Silu), [vf], [eo], 80 + CYC * SCA * 384)
+        if k >= 16 - EWV:
+            ts(eo, a384("V0"), 1.0, 48.0 * k, A.mult, A.add)
+        else:
+            iota(vf, [[1, 48], [0, 8]], 32 + 48 * k)
+            add("a", lambda q, e, ap, eo=eo, vf=vf: q.activation(ap(eo), ap(vf), F.Silu), [vf], [eo], 80 + CYC * SCA * 384)
     dma("s", [(lambda T, u=u: (S(T, "ZE", 96 * u, 96 * u + 96), S(T, "EW", 384 + 1536 * u, 1920 + 1536 * u, slice(0, 128, 16)))) for u in range(2)],
         [V("EW", 384, 3456)], [V("ZE", 0, 192)])
-    ts(V("i2", 0, 192), V("ZE", 0, 192), 1, None, A.max); cp(V("LA", 0, 96), V("i2", 0, 96)); cp(V("LB", 0, 96), V("i2", 96, 192))
+    ts(V("i2", 0, 192), V("ZE", 0, 192), 16, None, A.max); cp(V("LA", 0, 96), V("i2", 0, 96)); cp(V("LB", 0, 96), V("i2", 96, 192))
     iota(V("ga", 1920, 2688), [[0, 768]]); iota(V("Pw", 0, 16), [[0, 16]], 300)
 
     sp = ((0, 512), (512, 576)); sq = ((0, 512), (512, 768)); late = ([], [])
+    blank = lambda o: (o, V("Zr", 0, 128), V("Zr", 0, wid(o)))
     for t in range(3):
         Et = 1536 + 384 * t; last = t == 2
-        dma("s", [lambda T: (S(T, "Aw", 768, 1568), S(T, "Ac", 0, 800))], [V("Ac", 0, 800)], [V("Aw", 768, 1568)])
         zero("Zr", 1536, [("Aux", 768, 6912)], 8000.0)
         n576 = lambda n: V(n, 0, 576)
-        act(n576("fil"), V("RR", 128, 704), F.Sign, alt=lambda q, ap: q.tensor_scalar(ap(n576("fil")), ap(V("RR", 128, 704)), 1, None, A.is_ge))
-        ops[-1]["ca"] = ops[-1]["cost"]; ops[-1]["cost"] = 360.0
-        mm(*[[(V(P2, a, b), M("Hi"), V("fil", a, b)), (V(P2, a, b), M("D"), V("dead", a, b))] for a, b in sp])
-        ts(n576("ind"), V(P2, 0, 576), r, None, A.is_equal)
-        scan(V(P0, 0, 576), n576("ind"), n576("ind"), 0.0, A.add, A.max)
-        cp(V("MF", 128, 129), V(P0, 575, 576)); mm([(V(P2, 0, 1), V("MF", 0, 128), V("MF", 128, 129))])
-        tt(n576("rk"), V(P0, 0, 576), n576("ind"), A.mult); ts(V("MR", 128, 256), M("Blk"), V(P2, 0, 1), None, A.mult)
-        mm(*[[(V(P2, a, b), M("D"), V("dead", a, b)), (V(P2, a, b), V("MR", 0, 128), V("rk", a, b)), (V(P2, a, b), V("MR", 128, 256), V("ind", a, b))] for a, b in sp])
-        ts(n576("f1"), V(P2, 0, 576), pc("c0"), pc("c1"), A.max, A.min)
-        act(V("val", 128, 704), n576("f1"), F.Exp, pc("cb"), -4.6)
-        for c in range(8):
-            cp(V("G1", 768 * c, 768 * c + 768), IND("val", 0, 800, V("W", 48 * c, 48 * c + 48)), "av" if c % 4 * 2 + c // 4 >= 8 - HV[2 * t] else "a")
-            o = V(P0, 512 * (c // 4) + 96 * (c % 4), 512 * (c // 4) + 96 * (c % 4) + 96)
-            mm([(o, M("I"), V("val", 32 + 96 * c, 128 + 96 * c))] + [(o, M("I"), V("G1", 768 * c + k, 768 * c + 768, 8)) for k in range(8)])
-        for u in range(2): cp(V("S1", 32 + 384 * u, 416 + 384 * u), V(P0, 512 * u, 512 * u + 384), "av")
-        for c in range(6):
-            cp(V("G1", 768 * c, 768 * c + 768), IND("S1", 0, 800, V("W", 48 * c + 48, 48 * c + 96)), "av" if c % 3 * 2 + c // 3 >= 6 - HV[2 * t + 1] else "a")
-            o = V(P1, 512 * (c // 3) + 96 * (c % 3), 512 * (c // 3) + 96 * (c % 3) + 96)
-            mm([(o, M("I"), V("S1", 128 + 96 * c, 224 + 96 * c)), (o, M("N92"), V("val", 128 + 96 * c, 224 + 96 * c))] +
-               [(o, M("I"), V("G1", 768 * c + k, 768 * c + 768, 8)) for k in range(8)])
-        for u in range(2):
-            so, pi = V("sg", 288 * u, 288 * u + 288), V(P1, 512 * u, 512 * u + 288)
-            act(so, pi, F.Sign)
-            po = V(P2, 512 * u, 512 * u + 288); co = V("cho", 288 * u, 288 * u + 288)
-            mm([(po, M("Blk"), so), (po, M("D"), V("dead", 288 * u, 288 * u + 288))])
-            act(co, po, F.Relu, pc("m15"), -1.0, alt=lambda q, ap, co=co, po=po: q.tensor_scalar(ap(co), ap(po), -15.5, None, A.is_lt))
-        scan(V("cumc", 16, 592), n576("cho"), n576("c96"), 0.0, A.add, A.min)
-        cc = V("cumc", 16, 592)
-        for c in range(6): act(V("junk", 48 * c, 48 * c + 36), V("cumc", 31, 592, 16), F.Sign, V("pk", 112 + c, 113 + c), -1.0, acc=V("vc", c, c + 1))
-        mm([(V(P0, 0, 36), Z("0", i), V("cumc", 16 + i, 592, 16)) for i in range(16)]); cp(V("junk2", 0, 36), V(P0, 0, 36))
+        pos_(n576("fil"), V("RR", 128, 704))
+        mm(*[[(V(P1, a, b), M("NHi"), V("fil", a, b))] + [(V(P1, a, b), M("N128"), V("ctr", 576 * u + a, 576 * u + b)) for u in range(t)] for a, b in sp])
+        relu(V("GD", 128, 704), V(P1, 0, 576), pc("ten"))
+        kb = lambda u, B: V(P0, 512 * u + B, 512 * u + 384, 6)
+        mm(*[[blank(V(P0, 512 * u, 512 * u + 384))] + [(kb(u, B), V("RR", o + 128 * B, o + 128 * B + 128), half(M(m_), u)) for B in range(6) for o, m_ in ((32, "SN"), (832, "SE"))]
+             for u in range(2)], final=False)
+        for B in range(6):
+            cp(V("G1", 1024 * B, 1024 * B + 1024), IND("GD", 0, 800, V("W", 64 * B, 64 * B + 64)), "av")
+            mm(*[[(V(P0, 512 * u + 96 * k + B, 512 * u + 96 * k + 96, 6), V("G1", 1024 * B + 4 * u + k, 1024 * B + 1024, 8), V("SEL", 0, 16)) for k in range(4)] for u in range(2)],
+               first=False, final=B == 5)
+        mm([blank(V(P1, 0, 96))] + [(V(P1, B, 96, 6), V(n_, o + 128 * B, o + 128 * B + 128), w_) for B in range(6)
+                                     for n_, o, w_ in (("GD", 32, V("SEL", 0, 16)), ("RR", 1632, V("M", mn_["SN"], mn_["SN"] + 16)))])
+        cp(V("OWN", 0, 96), V(P1, 0, 96), "av")
+        for u in range(4): tt(V("KS", 0, 192), V(P0, 512 * (u // 2) + 192 * (u % 2), 512 * (u // 2) + 192 * (u % 2) + 192), V("KS" if u else "OWN", 0, 192), A.min)
+        tt(V("KI", 0, 96), V("KS", 0, 96), V("KS", 96, 192), A.min)
+        K1, K2 = V("KI", 0, 48), V("KI", 48, 96)
+        ts(V("XI", 0, 48), K1, 11, 63, A.arith_shift_right, A.bitwise_and); ts(V("XI", 48, 96), K1, 7, 15, A.arith_shift_right, A.bitwise_and)
+        tt(V("XR", 0, 96), V("XI", 0, 96), V("CX", 0, 96), A.add); ts(V("XR", 96, 192), V("XR", 0, 96), -1, None, A.add); ts(V("XR", 192, 384), V("XR", 0, 192), -2, None, A.add)
+        for j in range(9):
+            eq(V("OH", 384 * j, 384 * j + 384), a384("XR"), 4 * j, col(pc("m4", 9), j)); ops[-1]["cost"] = 60 + CYC * 192
+        hp = V(P1, 512, 548)
+        mm([(hp, Z("0", i), V("GD", 128 + i, 704, 16)) for i in range(15)], final=False)
+        mm([(V(P1, 512, 548, 1, (c // 12 * 32, c // 12 * 32 + 32)), V("OH", 48 + c, 3072, 96), V("OH", c, 3456, 96)) for c in range(48)] +
+           [(hp, Z("0", 15), V("GD", 143, 704, 16))], first=False)
+        ts(V("ch", 0, 36), hp, 11, None, A.is_equal)
+        mm([(V(P1, 0, 36), M("Blk"), V("ch", 0, 36))]); mm([(V(P0, 0, 36), M("TriM"), V("ch", 0, 36))])
+        scan(V("cc", 1, 37), V(P1, 0, 36), V("Zr", 0, 36), 500.0, A.add, A.max)
+        tt(V("rkw", 0, 36), V(P0, 0, 36), V("cc", 0, 36), A.add)
+        for c in range(6): act(V("junk", 48 * c, 48 * c + 36), V("cc", 1, 37), F.Sign, V("pk", 112 + c, 113 + c), -1.0, acc=V("vc", c, c + 1))
         ts(V("QL", 0, 6), V("vc", 0, 6), 0.5, 18, A.mult, A.add)
-        tt(V("junk2", 64, 160), IND("junk2", 0, 37, V("QL", 0, 6)), V("id1", 0, 96), A.is_lt)
+        tt(V("junk2", 0, 96), IND("rkw", 0, 37, V("QL", 0, 6)), V("id0", 0, 96), A.is_equal)
         ts(V("vd", 0, 6), V("vc", 0, 6), 8, 416, A.mult, A.add); ts(V("vd", 8, 14), V("vc", 0, 6), 35, None, A.is_lt); tt(V("vd", 0, 6), V("vd", 0, 6), V("vd", 8, 14), A.mult)
-        mm([(V(P0, 512, 518), Z("all", i), V("junk2", 64 + i, 160, 16)) for i in range(16)]); tt(V("vd", 8, 14), V(P0, 512, 518), V("vd", 0, 6), A.add)
-        for u in range(3): ts(V("VL", 6 * u, 6 * u + 6), V("vd", 8, 14), 800 * u, None, A.add)
-        mm(*[[(V(P2, a, b), M("I"), V("dead", a, b)), (V(P2, a, b), M("I"), V("cumc", 16 + a, 16 + b)), (V(P2, a, b), M("nI"), V("cumc", 15 + a, 15 + b))] for a, b in sp])
-        cp(n576("dead"), V(P2, 0, 576), "a")
-        cp(V("Rv", 0, 288), IND("RR", 0, 2400, V("VL", 0, 18)))
+        mm([(V(P1, 0, 6), Z("ir", i), V("junk2", i, 96, 16)) for i in range(16)]); tt(V("vd", 8, 14), V(P1, 0, 6), V("vd", 0, 6), A.add)
+        for u in range(2): ts(V("VL", 6 * u, 6 * u + 6), V("vd", 8, 14), 1600 * u, None, A.add)
+        ts(V("AI", 0, 48), K1, 7, 1023, A.arith_shift_right, A.bitwise_and); ts(V("AI", 48, 96), K1, 127, None, A.bitwise_and); ts(V("AI", 96, 144), K2, 31, None, A.bitwise_and)
+        cp(V("AE", 0, 48), V("AI", 0, 48)); ts(V("e1", 0, 48), V("AI", 48, 96), 32, -1400, A.mult, A.add); tt(V("AE", 48, 96), V("e1", 0, 48), V("AI", 96, 144), A.add)
+        mm([blank(V(P2, 0, 432))], final=False)
+        for g in range(8):
+            mm([(V(P2, j, 432, 8, (g // 2 * 32, g // 2 * 32 + 32)), V("SW", 32 * j + 16 - g % 2 * 16, 32 * j + 48 - g % 2 * 16), V("AE", 6 * g, 6 * g + 54)) for j in range(8)] +
+               [blank(V(P2, 0, 48))] * (g == 7), first=False, final=g == 7)
+        cp(V("AO", 0, 48), V(P2, 0, 48)); ts(V("AO", 48, 96), V(P2, 384, 432), 1400, None, A.add)
+        ts(V("cw", 0, 36), V("rkw", 0, 36), 95.5, None, A.is_lt); tt(V("cn", 0, 36), V("cw", 0, 36), V("pk", 0, 36), A.mult)
+        ct = lambda a, b: V("ctr", 576 * t + a, 576 * t + b)
+        for u in range(2):
+            o = V(P2, 512 * u, 512 * u + 288); tgt = V("TG", 128 + 288 * u, 416 + 288 * u)
+            mm(*[[(V(P2, 512 * u + i, 512 * u + 288, 16), V("BR", 128 * i, 128 * i + 128), V("cn", 18 * u, 18 * u + 18))] for i in range(16)])
+            either(tgt, o, lambda q, ap, tgt=tgt, o=o: q.tensor_scalar(ap(tgt), ap(o), -1024.0, None, A.add),
+                   lambda q, ap, tgt=tgt, o=o: q.activation(ap(tgt), ap(o), F.Identity, bias=ap(pc("m1k"))), [pc("m1k")])
+            pos_(ct(288 * u, 288 * u + 288), o)
+        cp(V("Rv", 0, 192), IND("RR", 0, 2400, V("VL", 0, 12)))
         while late[0]: late[0].pop()()
-        mm(wrap(V(P0, 0, 144), "Rv", 0, 288)); cp(V("UL", 0, 144), V(P0, 0, 144))
+        mm(wrap(V(P0, 0, 48), "Rv", 0, 96)); cp(V("UL", 0, 48), V(P0, 0, 48))
         ts(V("fv", 0, 96), V("Rv", 0, 96), 1, None, A.is_ge)
-        o = V(P0, 512, 560)
-        mm(wrap(o, "Rv", 0, 96) + [(o, Z("F", 0), V("fv", 0, 96, 2)), (o, Z("F", 8), V("fv", 1, 96, 2))])
-        tt(V("s1", 0, 48), o, V("pk", 0, 48), A.max); ts(V("Us", 0, 48), V("s1", 0, 48), -1232, None, A.add)
         for u in range(2): cp(V("G", 384 * u, 384 * u + 384), IND("RR", 0, 800, V("UL", 24 * u, 24 * u + 24)), "av")
-        parts(cp, SPL[0], V("Lf", 0, 768), IND("xw", 0, 2720, V("UL", 48, 96)), "av"); parts(cp, SPL[0], V("tg", 0, 768), IND("Tc", 0, 800, V("UL", 96, 144)), "av")
+        parts(cp, SPL[0], V("Lu", 0, 768), IND("xw", 0, 2720, V("AO", 48, 96)), "av"); neg(V("Lu", 768, 1536), V("Lu", 0, 768))
+        parts(cp, SPL[0], V("Aw", 32, 800), IND("TG", 0, 800, V("AO", 0, 48)), "av")
+        parts(relu, SPL[0], V("Bw", 32, 800), V("Aw", 32, 800))
         while late[1]: late[1].pop()()
-        parts(tt, SPL[1], IND("Aw", 0, 1568, V("Us", 0, 48)), V("Lf", 0, 768), V("tg", 0, 768), A.add)
-        MG = 1.5 * 2.0 ** 34
-        mm(*[[(V(P3, a, b), M("Wk"), V("RR", 32 + a, 32 + b))] for a, b in sq]); cp(V("nbK", 0, 768), V(P3, 0, 768), "a")
-        act(V("Tt", 0, 800), V("Aw", 768, 1568), F.Identity, pc("mg"))
-        act(V(P3, 0, 800), V("Tt", 0, 800), F.Identity, pc("mg2"), -2.0); tt(V("Bw", 0, 800), V("Aw", 768, 1568), V(P3, 0, 800), A.add)
-        for it, Pn in enumerate((P1, P2, P0)):
+        for u in range(2):
+            a, b = 384 * u, 384 * u + 384; o = V(P2, 512 * u, 512 * u + 384)
+            mm([(o, M("Wk"), V("RR", 32 + a, 32 + b)), (o, M("N128"), a384("c8"))]); tt(V("clr", a, b), o, V("Aw", 32 + a, 32 + b), A.is_equal)
+        for u, n_ in enumerate(("Aw", "Bw")):
+            dma("g", [lambda T, u=u, n_=n_: (S(T, n_, 32, 800), S(T, "Lu", 768 * u, 768 * u + 768), dict(accum_op=A.add))], [V("Lu", 768 * u, 768 * u + 768), V(n_, 32, 800)], [V(n_, 32, 800)], 3000.0)
+        for kb_, o_ in (("Kn", 32), ("Ke", 832)):
+            for u in range(2):
+                a, b = 384 * u, 384 * u + 384; o = V(P2, 512 * u, 512 * u + 384)
+                mm([(o, M("I"), V("RR", o_ + a, o_ + b)), (V(P2, 512 * u + 96 - 96 * u, 512 * u + 384 - 96 * u), M("N128"), ct(288 * u, 288 * u + 288)), (o, M("N128"), V("clr", a, b))])
+                relu(V(kb_, a, b), o)
+        for it, Pn in enumerate((P1, P0, P1)):
             mm(*[[(V(Pn, a, b), M("W2" if it == 2 else "Wc"), V("G", a, b))] +
-                 [(V(Pn, a + j, b, 8), M("NV") if it == 2 else M("N%d" % ((j + 2 * it + 1) % 8)), V("Rv", a // 8 + (192 if it == 2 else 0), b // 8 + (192 if it == 2 else 0))) for j in range(8)]
+                 [(V(Pn, a + j, b, 8), M("NV") if it == 2 else M("N%d" % ((j + 2 * it + 1) % 8)), V("Rv", a // 8 + (96 if it == 2 else 0), b // 8 + (96 if it == 2 else 0))) for j in range(8)]
                  for a, b in sq])
             for a, b in sq: eq(V("EQ", 768 * it + a, 768 * it + b), V(Pn, a, b), 0, 0.0)
-        mm(*[[(V(P1, 96 * b, 96 * b + 96), M("X%d" % b), V("fv", 0, 96))] + [(V(P1, 96 * b, 96 * b + 96), Z("Y2", j), V("EQ", 768 * b + j, 768 * b + 768, 8)) for j in range(8)] for b in range(2)])
-        act(V("wish", 0, 192), V(P1, 0, 192), F.Relu, pc("m1"), alt=lambda q, ap: q.tensor_scalar(ap(V("wish", 0, 192)), ap(V(P1, 0, 192)), 1.5, None, A.is_ge))
-        mm([(V(P1, 512, 608), Z("all", j), V("EQ", 1536 + j, 2304, 8)) for j in range(8)])
-        act(V("nf", 0, 96), V(P1, 512, 608), F.Identity, pc("l64"))
-        mm(*[[(V(P2, 192 * e + b, 192 * e + 192, 2), M("X%d" % (2 + 4 * sb + 2 * e + b)), V("wish", 96 * sb, 96 * sb + 96)) for sb in range(2)] for e in range(2) for b in range(2)])
-        mm(*[[(V(P2, 512 + 192 * e + b, 704 + 192 * e, 2), M("X%d" % (10 + 2 * e + b)), V("nf", 0, 96))] for e in range(2) for b in range(2)])
-        cp(V("Nw", 2, 386), V(P2, 0, 384), "av")
-        tt(V("fw", 0, 384), V("Nw", 2, 386), V(P2, 512, 896), A.is_lt); tt(V("ok", 0, 192), V("fw", 0, 192), V("fw", 192, 384), A.mult)
-        mm([(V(P1, 512, 704), M("Blk"), V("ok", 0, 192))]); mm([(V(P1, 0, 192), M("TriM"), V("ok", 0, 192))])
-        scan(V("cumb", 1, 193), V(P1, 512, 704), V("c884", 0, 192), 500.0, A.add, A.min)
+        mm(*[[(V(P0, 96 * b, 96 * b + 96), M("X%d" % b), V("fv", 0, 96))] + [(V(P0, 96 * b, 96 * b + 96), Z("Y2", j), V("EQ", 768 * b + j, 768 * b + 768, 8)) for j in range(8)] for b in range(2)])
+        act(V("wish", 0, 192), V(P0, 0, 192), F.Relu, pc("m1"), alt=lambda q, ap: q.tensor_scalar(ap(V("wish", 0, 192)), ap(V(P0, 0, 192)), 1.5, None, A.is_ge))
+        mm([(V(P0, 512, 608), Z("all", j), V("EQ", 1536 + j, 2304, 8)) for j in range(8)])
+        act(V("nf", 0, 96), V(P0, 512, 608), F.Identity, pc("l64"), alt=lambda q, ap: q.tensor_scalar(ap(V("nf", 0, 96)), ap(V(P0, 512, 608)), ap(pc("l64")), None, A.add))
+        mm(*[[(V(P1, 192 * e + b, 192 * e + 192, 2), M("X%d" % (2 + 4 * sb + 2 * e + b)), V("wish", 96 * sb, 96 * sb + 96)) for sb in range(2)] for e in range(2) for b in range(2)])
+        mm(*[[(V(P1, 512 + 192 * e + b, 704 + 192 * e, 2), M("X%d" % (10 + 2 * e + b)), V("nf", 0, 96))] for e in range(2) for b in range(2)])
+        cp(V("Nw", 2, 386), V(P1, 0, 384), "av")
+        tt(V("fw", 0, 384), V("Nw", 2, 386), V(P1, 512, 896), A.is_lt); tt(V("ok", 0, 192), V("fw", 0, 192), V("fw", 192, 384), A.mult)
+        mm([(V(P0, 512, 704), M("Blk"), V("ok", 0, 192))]); mm([(V(P0, 0, 192), M("TriM"), V("ok", 0, 192))])
+        scan(V("cumb", 1, 193), V(P0, 512, 704), V("c884", 0, 192), 500.0, A.add, A.min)
         scan(V("ws", 0, 192), V("big", 0, 192), V("cumb", 0, 192), 0.0, A.add, A.min); scan(V("we", 0, 192), V("big", 0, 192), V("cumb", 1, 193), 0.0, A.add, A.min)
         tt(V("s2", 0, 12), V("we", 15, 192, 16), V("ws", 15, 192, 16), A.is_gt); tt(V("s2", 16, 28), V("s2", 0, 12), V("ws", 15, 192, 16), A.mult)
         tt(V("s2", 32, 44), V("s2", 16, 28), V("pk", 96, 108), A.max); ts(V("ZL", 0, 12), V("s2", 32, 44), -308, None, A.add)
@@ -416,7 +470,7 @@ def program():
         zr = V("Z", 576 * t + 192, 576 * t + 576)
         scan(a384("mx"), zr, zr, 0.0, A.max, A.max); scan(a384("wr"), a384("big"), a384("mx"), 0.0, A.add, A.min)
         cp(V("CL", 0, 24), V("wr", 15, 384, 16)); CL = V("CL", 0, 24)
-        tt(V("num", 2, 194), V(P1, 0, 192), V("cumb", 0, 192), A.add)
+        tt(V("num", 2, 194), V(P0, 0, 192), V("cumb", 0, 192), A.add)
         tt(a384("oh"), IND("num", 0, 194, CL), a384("im"), A.is_equal)
         for e in range(2): tt(V("pr", 384 * e, 384 * e + 384), IND("Nw", 192 * e, 192 * e + 194, CL), a384("oh"), A.mult)
         o = V(P1, 512, 560)
@@ -425,58 +479,58 @@ def program():
         for e in range(2): ts(V("s3", 24 * e, 24 * e + 24), V("j1", 24, 48), 4, -8, A.mult, A.add)
         ts(V("j2", 0, 48), o, 0.125, 7.625, A.mult, A.add); ts(V("s3", 48, 96), o, -0.5, 800, A.is_ge, A.mult)
         tt(V("s3", 48, 96), V("s3", 48, 96), V("s3", 0, 48), A.add); tt(V("s1", 48, 96), V("s3", 48, 96), V("j2", 0, 48), A.add); cp(V("IL", 0, 48), V("s1", 48, 96))
-        mm(*[[(V(P0, a, b), M("CF"), V("EQ", 1536 + a, 1536 + b)), (V(P0, a, b), M("R0"), V("J8", a, b))] +
-             [(V(P0, a + j, b, 8), M("U%d" % j), V("Rv", a // 8, b // 8)) for j in range(8)] for a, b in sq])
-        cp(V("W2", 0, 768), V(P0, 0, 768), "a")
+        mm(*[[(V(P3, a, b), M("CF"), V("EQ", 1536 + a, 1536 + b)), (V(P3, a, b), M("R0"), V("J8", a, b))] +
+             [(V(P3, a + j, b, 8), M("U%d" % j), V("Rv", a // 8, b // 8)) for j in range(8)] for a, b in sq])
+        cp(V("W2", 0, 768), V(P3, 0, 768), "av")
         for e in range(2):
-            ge = V("G2", 384 * e, 384 * e + 384); pe = V(P2, 512 * e, 512 * e + 384)
+            ge = V("G2", 384 * e, 384 * e + 384); pe = V(P0, 512 * e, 512 * e + 384)
             cp(ge, IND("W2", 0, 1600, V("IL", 24 * e, 24 * e + 24)), "av")
             mm([(pe, Z("lo", 0), ge), (pe, M("NLo"), V("pr", 384 * e, 384 * e + 384))])
             eq(V("e2", 384 * e, 384 * e + 384), pe, 0, 0.0)
         o = V(P1, 0, 48)
         mm([(o, Z("u", i), V("G2", i, 768, 16)) for i in range(16)], final=False); mm([(o, Z("s", i), V("e2", i, 768, 16)) for i in range(16)], first=False)
         tt(V("s1", 0, 48), o, V("pk", 48, 96), A.max); ts(V("AL", 0, 48), V("s1", 0, 48), 512, None, A.add)
-        x0 = 0
         for e in range(2):
-            tt(IND("Aux", x0, x0 + 6912, V("AL", 24 * e, 24 * e + 24)), V("G2", 384 - 384 * e, 768 - 384 * e), V("NM", 384 * t, 384 * t + 384), A.add)
+            tt(IND("Aux", 0, 6912, V("AL", 24 * e, 24 * e + 24)), V("G2", 384 - 384 * e, 768 - 384 * e), V("NM", 384 * t, 384 * t + 384), A.add)
         ts(V("j3", 0, 48), o, 0.125, -0.4375, A.mult, A.add)
         nl = Et // 16
         cp(V("LA", nl, nl + 24), V("j3", 0, 24)); cp(V("LB", nl, nl + 24), V("j3", 24, 48))
-        tt(V(P3, 32, 800), V(P3, 32, 800), V("nbK", 0, 768), A.not_equal)
-        if last: tt(V(P3, 128, 704), V(P3, 128, 704), n576("dead"), A.is_gt)
-        for Pn, kb, zz, o in ((P0, "Kn", "A", 32), (P1, "Ke", "B", 832)):
-            tt(V(kb, 0, 768), V("RR", o, o + 768), V(P3, 32, 800), A.mult)
-            for a, b in ((0, 384), (384, 768)):
-                po = V(Pn, a // 3 * 4, a // 3 * 4 + 384)
-                mm([(po, Z(zz, s), V("Aux", x0 + 768 + 8 * a + s, x0 + 768 + 8 * b, 8)) for s in range(8)], final=False); mm([(po, M("I"), V(kb, a, b))], first=False)
-                cp(V("RR", o + a, o + b), po, "av")
+        for n_, (kb_, zz, o, a, b) in enumerate([("Kn", "A", 32, a, b) for a, b in FOLD[0]] + [("Ke", "B", 832, a, b) for a, b in FOLD[1]]):
+            po = V((P0, P1)[n_ // 2 % 2], n_ % 2 * 512, n_ % 2 * 512 + b - a)
+            mm([(po, M("I"), V(kb_, a, b))], final=False); mm([(po, Z(zz, s), V("Aux", 768 + 8 * a + s, 768 + 8 * b, 8)) for s in range(8)], first=False)
+            cp(V("RR", o + a, o + b), po, "av")
+        done = 0
         for a in range(0, Et, 384):
-            b = a + 384; z = a % 1536; zf, zb = V("zf", z, z + 384), V("zb", z, z + 384); xs = V("xw", 32 + a, 32 + b)
-            cp(V("ga", a, b), IND("Aw", 768, 1568, V("LA", a // 16, b // 16)), "av")
-            tt(zf, IND("Bw", 0, 800, V("LB", a // 16, b // 16)), V("ga", a, b), A.add)
-            act(zb, zf, F.Abs)
-            o = V((P3, P1)[a // 768 % ROT], a // 384 % 2 * 512, a // 384 % 2 * 512 + 384)
-            mm([(o, M("I"), xs), (o, M("nI"), zb)])
-            act(V("ix", a, b), o, F.Sign, pc("mh"))
-            if a // 384 < XACT[t]:
-                rr = V("rl", z, z + 384); act(rr, o, F.Relu)
-                mm([(o, M("I"), xs), (o, M("nI"), rr)]); cp(xs, o, "a")
+            b = a + 384; z = a % 1536; zb, mk, rr = V("zb", z, z + 384), V("mk", z, z + 384), V("rl", a, b); xs = V("xw", 32 + a, 32 + b)
+            neg(V("ga", a, b), IND("Aw", 0, 800, V("LA", a // 16, b // 16)))
+            o = V(P2 if ACC[t] or a // 768 % 2 == 0 else P3, a // 384 % 2 * 512, a // 384 % 2 * 512 + 384)
+            if a // 384 < DV[t]:
+                gb = V("gb", a, b); cp(gb, IND("Bw", 0, 800, V("LB", a // 16, b // 16)), "av")
+                dma("g", [lambda T, a=a, b=b: (S(T, "gb", a, b), S(T, "ga", a, b), dict(accum_op=A.add))], [gb, V("ga", a, b)], [gb], 3000.0)
+                act(zb, gb, F.Abs); mm([(o, M("nI"), xs), (o, M("nI"), zb)])
             else:
-                tt(xs, xs, zb, A.min)
-        cp(V("ga", Et, Et + 384), IND("Aw", 768, 1568, V("LA", nl, nl + 24)), "av")
+                tt(zb, IND("Bw", 0, 800, V("LB", a // 16, b // 16)), V("ga", a, b), A.add)
+                relu(mk, zb); mm([(o, M("nI"), xs), (o, M("I"), zb), (o, M("D2"), mk)])
+            relu(rr, o); pos_(V("ix", a, b), rr)
+            if not ACC[t]:
+                mm([(o, M("I"), xs), (o, M("I"), rr)]); cp(xs, o, "av")
+            elif b % 768 == 0 or b == Et:
+                dma("g", [lambda T, c=done, b=b: (S(T, "xw", 32 + c, 32 + b), S(T, "rl", c, b), dict(accum_op=A.add))], [V("rl", done, b), V("xw", 32 + done, 32 + b)], [V("xw", 32 + done, 32 + b)], 3000.0)
+                done = b
+        neg(V("ga", Et, Et + 384), IND("Aw", 0, 800, V("LA", nl, nl + 24)))
         tt(a384("zn"), IND("Bw", 0, 800, V("LB", nl, nl + 24)), V("ga", Et, Et + 384), A.add)
-        ts(V("xw", 32 + Et, 416 + Et), a384("zn"), 255, None, A.min)
-        act(V("ix", Et, Et + 384), a384("zn"), F.Sign, pc("mh"))
+        ts(V("xw", 32 + Et, 416 + Et), a384("zn"), -1, -255, A.mult, A.max)
+        ts(V("ix", Et, Et + 384), V("xw", 32 + Et, 416 + Et), -0.5, None, A.is_lt)
         dma("s", [lambda T: (S(T, "own", 0, 168), S(T, "ga", 0, 2688, slice(0, 128, 16)))], [V("ga", 0, 2688)], [V("own", 0, 168)])
         wp = V(P0, 0, 384)
         mm(wrap(wp, "RR", 32, 800))
         if not last: cp(V("W", 0, 384), wp)
         mm(*[wrap(V(P1, 48 * s, 48 * s + 48), "RR", 832 + 672 * s, 928 + 672 * s) for s in range(2)])
-        cp(V("Eb", 0, 96), V(P1, 0, 96)); tt(V("Ebf", 0, 48), V(P1, 0, 48), V("dum", 0, 48), A.subtract); tt(V("Ebf", 48, 96), V(P1, 48, 96), V("dum", 48, 96), A.subtract)
+        cp(V("Eb", 0, 96), V(P1, 0, 96)); act(V("Ebf", 0, 96), V(P1, 0, 96), F.Identity, pc("p768"))
         for s in range(2):
             m0 = 432 * (2 * t + s)
-            cp(V("snd", m0 + 384, m0 + 432), V(P0, 336 * s, 48 + 336 * s)); cp(V("nbs", 48 * s, 48 * s + 48), V(P0, 336 * s, 48 + 336 * s))
-            parts(cp, SPL[0], V("Go", 768 * s, 768 * s + 768), IND("xw", 0, 2720, V("Eb", 48 * s, 48 * s + 48)), "av")
+            cp(V("snd", m0 + 384, m0 + 432), V(P0, 336 * s, 48 + 336 * s)); cp(V("nbs", 48 * s, 48 * s + 48), V(P0, 336 * s, 48 + 336 * s), "a")
+            parts(neg, SPL[0], V("Go", 768 * s, 768 * s + 768), IND("xw", 0, 2720, V("Eb", 48 * s, 48 * s + 48)), "av")
             o = V(P3, 512 * s, 512 * s + 384)
             mm([(o, M("I256"), V("Go", 768 * s, 768 * s + 384)), (o, M("I"), V("Go", 768 * s + 384, 768 * s + 768))])
             cp(V("snd", m0, m0 + 384), o)
@@ -485,14 +539,13 @@ def program():
             add("r", (k, t, a, b), [V("net", k, k + 1)], [V("lnd", 864 * t + 432 * s + a, 864 * t + 432 * s + b) for s in range(2)], 0.0, kind="recv", lat=lat)
         if last:
             for a, b in ((32, 1376), (1376, 2720)): act(V("xw", a, b), V("xw", a, b), F.Abs)
-        tt(V("can", 0, 96), V("nbs", 0, 96), V("slf", 0, 96), A.is_gt); ts(V("q1", 0, 48), V("nbs", 0, 48), 128, None, A.is_lt)
-        tt(V("can", 0, 48), V("can", 0, 48), V("q1", 0, 48), A.mult); tt(V("can", 0, 96), V("can", 0, 96), V("Ebf", 0, 96), A.mult)
-        tt(V("can", 0, 96), V("can", 0, 96), V("dum", 0, 96), A.add); cp(V("SS", 0, 96), V("can", 0, 96))
+        tt(V("can", 0, 96), V("nbs", 0, 96), V("slf", 0, 96), A.is_gt); tt(V("can", 0, 96), V("can", 0, 96), V("Ebf", 0, 96), A.mult)
+        tt(V("can", 0, 96), V("can", 0, 96), V("dum", 0, 96), A.max); cp(V("SS", 0, 96), V("can", 0, 96))
         ts(V("thr", 48, 96), V("nbs", 48, 96), 704, 1e6, A.is_lt, A.mult)
-        o = V(P3, 0, 168)
+        o = V(P2, 0, 168)
         mm([(o, Z("all", i), V("ix", 168 * i, 168 * i + 168)) for i in range(16) if 168 * i < Et + 384])
-        act(V("m3", 0, 168), V("own", 0, 168), F.Identity, pc("md%d" % t), 1.0 / 2048)
-        ts(o, o, 1.0, None, A.is_ge); tt(V("m2", 0, 168), o, V("m3", 0, 168), A.mult); tt(V("mid", 0, 168), V("mid", 0, 168), V("m2", 0, 168), A.max)
+        act(V("m3", 0, 168), V("own", 0, 168), F.Identity, pc("md%d" % t), -1.0 / 4096)
+        ts(o, o, 8.5, None, A.is_ge); tt(V("m2", 0, 168), o, V("m3", 0, 168), A.mult); tt(V("mid", 0, 168), V("mid", 0, 168), V("m2", 0, 168), A.max)
         if last:
             ts(V("m1", 0, 168), V("mid", 0, 168), -12582912, None, A.add); ts(V("m1", 0, 168), V("m1", 0, 168), 1023, None, A.bitwise_and)
             ts(V("m3", 0, 168), V("m1", 0, 168), -32, None, A.add)
@@ -519,11 +572,11 @@ def program():
             ts(V("Pw", 400 + 768 * s, 784 + 768 * s), V("i1", 432 * s, 432 * s + 384), 255, None, A.bitwise_and)
         for s in range(2):
             sv = lambda n: V(n, 768 * s, 768 * s + 768)
-            pw = IND("Pw", 0, 784 + 768 * s, V("PL", 48 * s, 48 * s + 48)); xs = IND("xw", 0, 3488, V("SS", 48 * s, 48 * s + 48))
+            pw = IND("Pw", 0, 784 + 768 * s, V("PL", 48 * s, 48 * s + 48)); xs = IND("xz", 0, 3488, V("SS", 48 * s, 48 * s + 48))
             parts(tt, SPL[0], sv("mn"), pw, sv("Go"), A.min)
             for u in range(2):
                 o = V(P3, 512 * u, 512 * u + 384); w = (768 * s + 384 * u, 768 * s + 384 * u + 384)
-                mm([(o, M("I"), V("Go", *w)), (o, M("nI"), V("mn", *w))]); act(V("si", *w), o, F.Sign)
+                mm([(o, M("I"), V("Go", *w)), (o, M("nI"), V("mn", *w))]); pos_(V("si", *w), o)
             if last: parts(cp, SPL[1], xs, sv("mn"))
             o = V(P3, 0, 96)
             mm([(o, Z("2", k), V("si", 768 * s + k, 768 * s + 768, 8)) for k in range(8)])
@@ -539,13 +592,14 @@ def program():
         if not last:
             for u in range(4):
                 o = V(P3, 512 * (u % 2), 512 * (u % 2) + 384); w = (384 * u, 384 * u + 384)
-                mm([(o, M("Blk"), V("si", *w))]); act(V("sn", *w), o, F.Sign, pc("p85"), -1.0)
+                mm([(o, M("Blk"), V("si", *w))]); act(V("sn", *w), o, F.Sign, pc("m85"))
         if last:
             dma("s", [lambda T: (T.ylen[:, :], S(T, "xw", 32, 2720))], [V("xw", 32, 2720)], [V("out", 1, 2)], 4000.0)
             dma("a", [lambda T: (T.ynb[:, :], S(T, "O", 0, 768, slice(0, 64))), lambda T: (T.yen[:, :], S(T, "O", 0, 768, slice(64, 128)))], [V("O", 0, 768)], [V("out", 2, 3)], 3000.0)
     pre = len(ops)
-    for n_, c_ in (("m15", -15.0), ("p85", 8.5), ("mh", -0.5), ("one", 1.0), ("mg", MG), ("mg2", 2 * MG), ("ns0", -31.0), ("ns1", -703.0), ("m1", -1.0),
-                   ("md0", 12582912.0 + 1024), ("md1", 12582912.0 + 2048), ("md2", 12582912.0 + 3072)): mset(pc(n_), c_)
+    mset(pc("m85"), -8.5); iota(pc("m4"), [[-4, 9]])
+    for n_, c_ in (("ten", 10), ("m1k", -1024), ("p768", 768), ("one", 1), ("ns0", -31), ("ns1", -703), ("m1", -1),
+                   ("md0", 12582912 + 1024), ("md1", 12582912 + 2048), ("md2", 12582912 + 3072)): iota(pc(n_), [[0, 1]], c_)
     return ops[pre:] + ops[:pre]
 
 
@@ -558,23 +612,27 @@ def span(v):
     return v[0], a, b
 
 
-def plan():
-    ops = program(); n = len(ops); hist = {}
+def depend():
+    ops = program(); hist = {}
     for i, o in enumerate(ops):
-        dep = {}
-        for v, w in [(v, False) for v in o["rd"]] + [(v, True) for v in o["wr"]]:
-            nm, a, b = span(v); ps = v[0] not in SB and v[0][0] == "P"
+        dep = {}; uses = set([(span(v), False, v[0] in SB) for v in o["rd"]] + [(span(v), True, v[0] in SB) for v in o["wr"]])
+        for (nm, a, b), w, sb in uses:
+            ps = not sb and nm[0] == "P"
             for (j, c, d, ww) in hist.get(nm, []):
-                if j == i or d <= a or b <= c: continue
+                if d <= a or b <= c: continue
                 if ww or w: dep[j] = True
                 elif ps: dep[j] = dep.get(j, False)
         for v in o["wr"]:
             nm, a, b = span(v)
-            if not v[4] and v[3] == 1 and v[0] in SB:
+            if (not v[4] and v[3] == 1 and v[0] in SB) or nm[0] == "P":
                 hist[nm] = [x for x in hist.get(nm, []) if not (a <= x[1] and x[2] <= b)]
-        for v, w in [(v, False) for v in o["rd"]] + [(v, True) for v in o["wr"]]:
-            nm, a, b = span(v); hist.setdefault(nm, []).append((i, a, b, w))
+        for (nm, a, b), w, sb in sorted(uses): hist.setdefault(nm, []).append((i, a, b, w))
         o["dep"] = dep
+    return ops
+
+
+def plan():
+    ops = depend(); n = len(ops)
     succ = [[] for _ in ops]
     for i, o in enumerate(ops):
         for j in o["dep"]: succ[j].append(i)
@@ -586,10 +644,10 @@ def plan():
         left = [len(x) for x in before]; ready = [i for i in range(n) if not left[i]]
         while ready:
             i = max(ready, key=lambda k: pri[k]); ready.remove(i); o = ops[i]
-            rt = max([fin[j] + SY for j in before[i]] + [0.0]); c = o["cost"]; best = None
+            rt = max([fin[j] + SY for j in before[i]] + [0.0]); best = None
             pre_, post = (0.0, o["lat"]) if before is pred else (o["lat"], 0.0)
             for e in (fixed[i] if fixed else o["engs"]):
-                s = rt + pre_; at_ = 0; c = o.get("ca", o["cost"]) if e == "a" else o["cost"]
+                s = rt + pre_; c = o.get("ca", o["cost"]) if e == "a" else o["cost"]
                 bz = busy[e]; at_ = len(bz)
                 while at_ and bz[at_ - 1][1] > s: at_ -= 1
                 while at_ < len(bz) and s + c > bz[at_][0]:
@@ -608,9 +666,10 @@ def plan():
     top = None; zero = [0.0] * n
     for bias, seed in BIASES:
         rs = np.random.RandomState(seed); p = [x + float(y) for x, y in zip(pri, rs.uniform(0, JIT if seed else 0.0, n))]
+        bias = [bias if o["wr"][0][0] in CHAIN else FAR for o in ops]
         for _ in range(PASSES):
-            t0, fin, eng = place(p, pred, succ, None, [bias] * n)
-            if top is None or max(fin) < top[0]: top = (max(fin), t0, eng, p, [bias] * n)
+            t0, fin, eng = place(p, pred, succ, None, bias)
+            if top is None or max(fin) < top[0]: top = (max(fin), t0, eng, p, bias)
             _, p, _ = place(fin, succ, pred, eng, zero)
     rs = np.random.RandomState(SEED); cur = top
     for _ in range(TRIES):
@@ -643,12 +702,7 @@ def rank_program(g, core, T, topo):
     def step(ins):
         steps[0] += 1; ins.then_inc(T.sem.ax, 1); g.scalar.wait_ge(T.sem.ax, steps[0])
 
-    def ap(v):
-        if v == "step": return step
-        if not isinstance(v, tuple): return v
-        nm, o = LOC.get(v[0], (v[0], 0))
-        x = T[nm][:, o + v[1]:o + v[2]] if v[3] == 1 else T[nm][:, o + v[1]:o + v[2]:v[3]]
-        return x.indirect(ap(v[4])) if v[4] else x
+    ap = lambda v: make_ap(T, v, step)
     at = {i: k for k, i in enumerate(order)}; seen = {e: {} for e in Q}; waits = {}; need = set()
     for i in order:
         o = ops[i]; e = o["e"]; waits[i] = []
@@ -656,7 +710,7 @@ def rank_program(g, core, T, topo):
         best = {}
         for j, hard in o["dep"].items():
             d = ops[j]; key = d["e"] if d["kind"] == "c" else j
-            if d["kind"] == "c" and d["e"] == e and (e == "p" or (SOFT_SAME and not hard)): continue
+            if d["kind"] == "c" and d["e"] == e and (e == "p" or not hard): continue
             if key not in best or at[j] > at[best[key]]: best[key] = j
         for key, j in best.items():
             if seen[e].get(key, -1) >= at[j]: continue
@@ -676,16 +730,15 @@ def rank_program(g, core, T, topo):
         elif o["kind"] == "d":
             sem = T.sem["d%d" % nd]; nd += 1
             for f in o["fn"]:
-                a, b = f(T); q.dma_start(a, b).then_inc(sem, 16)
+                z = f(T); q.dma_start(z[0], z[1], **(z[2] if len(z) > 2 else {})).then_inc(sem, 16)
             token[i] = (sem, 16 * len(o["fn"]))
             if i not in need: tail.append(token[i])
         else:
-            m, t, a, b = o["fn"]; trs = []; used = 0
-            for s in range(2):
-                d = T.cores[(rank + 2 * s - 1) % n]; rid, pid = topo.addr(d, core); en = topo.engines(core, d)
+            m = o["fn"][0]; trs = []; used = 0
+            for s, (dr, src, dst) in enumerate(transfers(o)):
+                d = T.cores[(rank + dr) % n]; rid, pid = topo.addr(d, core); en = topo.engines(core, d)
                 k = len(en) // 2; mask = sum(1 << x for x in en[k * s:k * s + k])
-                trs.append(RemoteDMATransfer(dst_ids=[DstId(rid=rid, pnc=pid)], dma_engine_mask=mask, remote_sem=T.sem["r%d" % m],
-                                             src=S(T, "snd", 432 * (2 * t + s) + a, 432 * (2 * t + s) + b), dst=S(T, "lnd", 432 * (2 * t + 1 - s) + a, 432 * (2 * t + 1 - s) + b)))
+                trs.append(RemoteDMATransfer(dst_ids=[DstId(rid=rid, pnc=pid)], dma_engine_mask=mask, remote_sem=T.sem["r%d" % m], src=ap(src), dst=ap(dst)))
                 used += k
             g.remote_dma_fused(trs, local_sem=T.sem["l%d" % m])
             tail.append((T.sem["l%d" % m], used))

@@ -1,13 +1,12 @@
 import numpy as np
-from concourse.bass import DstId, RemoteDMATransfer
 from concourse.mybir import AluOpType as A, ActivationFunctionType as F
 
 F32, BF, I32, U16, H16 = "float32", "bfloat16", "int32", "uint16", "float16"
 SB = dict(
-    xz=(3488, BF), xw=(2720, BF), Lu=(1536, BF), RR=(2400, BF), Rs=(768, I32), i1=(864, I32), i2=(384, I32),
+    xz=(3488, BF), xw=(2720, BF), Lu=(1536, BF), RR=(2400, BF), Rs=(768, I32), NW=(768, I32), i2=(192, I32),
     EO=(384, U16), EW=(3840, F32), LA=(168, U16), LB=(168, U16), W=(384, U16), SL=(48, U16), XL=(112, U16),
     lo8=(800, BF), hi8=(800, BF), c8=(384, BF), cn=(36, H16), NM=(1152, BF), b1=(800, BF), b2=(800, BF), b3=(800, BF),
-    PC=(128, F32), PI=(64, I32), CMx=(144, BF), CH=(128, BF), CO=(192, F32), MZ=(144 * 20, BF), M=(128 * 60, BF), BR=(2048, BF), ZO=(192, BF),
+    PC=(128, F32), PI=(64, I32), CMx=(144, BF), CH=(128, BF), CO=(192, F32), MZ=(144 * 20, BF), M=(128 * 54, BF), BR=(2048, BF), ZO=(192, BF),
     PAT=(240, BF), cod=(64, BF), pu=(192, BF), jk=(64, I32), SEL=(16, BF), SW=(272, H16), CX=(96, BF),
     fil=(576, BF), GD=(800, BF), G1=(6144, BF), KS=(192, F32), OWN=(192, F32), KI=(96, I32), XI=(96, I32), AI=(144, I32), e1=(48, F32), XR=(384, BF), OH=(3456, BF),
     AE=(96, H16), AO=(96, U16), ch=(36, BF), cc=(40, F32), rkw=(40, F32), cw=(36, BF), TG=(800, F32), ctr=(576 * 3, BF), tg=(768, F32), gb=(1536, F32), clr=(768, BF),
@@ -19,12 +18,14 @@ SB = dict(
     im=(384, F32), oh=(384, BF), pr=(768, BF), j1=(48, I32), j2=(48, I32), j3=(48, I32), IL=(48, U16), W2=(1600, BF), J8=(768, BF), G2=(768, BF), e2=(768, BF),
     AL=(48, U16), Aux=(6912, BF), gz=(3840, F32), ga=(2688, F32), zb=(1536, BF), mk=(1536, BF), rl=(2304, BF), zn=(384, F32), ix=(2688, BF),
     own=(168, F32), mid=(168, F32), m1=(168, I32), m2=(168, F32), m3=(168, F32),
-    snd=(432 * 6, U16), lnd=(432 * 6, U16), Eb=(96, U16), nbs=(96, F32), Ebf=(96, F32), slf=(96, F32), dum=(96, F32), thr=(96, F32), can=(96, F32), q1=(96, F32),
-    SS=(96, U16), PL=(96, U16), pc8=(96, F32), Go=(1536, BF), Pw=(1552, I32), par=(96, BF), eqs=(768, BF), si=(1536, BF), mn=(1536, BF), sn=(1536, BF),
-    ks=(192, BF), O=(768, F32), Zr=(1536, BF), Zf=(384, F32), ZE=(192, F32), Vf=(768, F32), V0=(384, F32),
+    sk=(144, U16), lk=(144, U16), sy=(1152, BF), ly=(1152, BF), s3m=(1248, BF), l3m=(1248, BF), Eb=(96, U16), E2=(48, U16), SS=(48, U16), ZS=(6, U16),
+    slf=(96, F32), fl=(96, BF), CT=(112, F32), PT=(112, F32), cs=(100, F32), w5=(192, F32), s4=(96, F32), s5=(24, F32), Zs=(1440, BF), id16=(96, BF),
+    mx2=(384, BF), wr2=(384, BF), oh2=(384, BF), cx=(384, H16), bb=(24, BF), Gn=(384, BF), ohc=(384, BF), nm=(384, BF), dd=(384, BF), rs=(384, BF),
+    pp=(384, BF), pn=(384, BF), Go=(1536, BF), sn=(768, BF), PN=(3488, BF), FR=(416, BF), PL=(48, U16), cm1=(384, BF),
+    O=(768, F32), Zr=(1536, BF), Zf=(384, F32), ZE=(192, F32), Vf=(768, F32),
 )
-ALIAS = dict(xw=("xz", 768), ga=("gz", 0), EW=("gz", 0), Vf=("O", 0), b1=("si", 0), b2=("sn", 0), b3=("mn", 0), lo8=("Go", 0), hi8=("OH", 0),
-             Rs=("Pw", 0), CO=("gb", 0), Zf=("zn", 0), Lf=("gb", 768), tg=("gb", 0))
+ALIAS = dict(xw=("xz", 768), ga=("gz", 0), EW=("gz", 0), Vf=("O", 0), b1=("EQ", 0), b2=("EQ", 800), b3=("rl", 0), lo8=("Go", 0), hi8=("OH", 0),
+             CO=("gb", 0), Lf=("gb", 768), tg=("gb", 0), i2=("Rs", 0))
 LOC, SCRATCH = {}, {}
 for _d in (F32, BF, I32, U16, H16):
     _n, _o = 0, 0
@@ -41,19 +42,27 @@ def S(T, n, a, b, rows=slice(None)):
     return T[LOC[n][0]][rows, LOC[n][1] + a:LOC[n][1] + b]
 
 
-SPL = [2, 4]
-ACC = [1, 1, 0]
+SPL = [2, 1]
+ACC = [4, 4, 2]
+EARLY = [("EW", 3, 30000.0, 1e6), ("LA", 0, 10000.0, 1e6)] + [(n, k, up, 25000.0) for n, k in (("zb", 0), ("zb", 4), ("zb", 9), ("zb", 3), ("zb", 8), ("zb", 14)) for up in (5000.0, 10000.0)]
+TWO = 0
+BRV = 4
+ABS = [0, 3, 3]
+MIDB = ("P2", 512, 680)
 DV = [0, 0, 0]
-FOLD = [((0, 384), (384, 768)), ((0, 96), (672, 768), (96, 384), (384, 672))]
-EWV = 0
-CHAIN, FAR = ("G1", "G", "EQ", "e2", "G2", "RR", "Nw", "wish", "nf", "fil", "GD"), 5000.0
-BIASES, PASSES, JIT, SEED, TRIES = ((300.0, 1), (700.0, 0), (700.0, 2)), 5, 800.0, 1, 4000
+FOLD = [(0, 672, 768, "P0", 0), (1, 672, 768, "P0", 512), (0, 0, 384, "P1", 0), (0, 384, 672, "P1", 512), (1, 0, 96, "P0", 512),
+        (1, 96, 384, "P1", 0), (1, 384, 672, "P1", 512)]
+FIRST = [0, 0, 0]
+KEYS = 4
+EWV = 3
+BIASES, PASSES, SEED, TRIES, SY, MOVE, LIFT, HEAT = (300.0, 700.0, 2000.0), 3, 2, 6500, 190.0, 0.5, 0.75, 300.0
 for _k in range(4):
     SCRATCH["P%d" % _k] = ("psum", [128, 1024], F32)
 NDMA = 48
-SEMAPHORES = ["ev", "ea", "ep", "eg", "ax"] + ["d%d" % k for k in range(NDMA)] + [a + str(k) for a in "rl" for k in range(6)]
+SEMAPHORES = ["ev", "ea", "ep", "eg", "ax"] + ["d%d" % k for k in range(NDMA)] + [a + str(k) for a in "rl" for k in range(12)]
+SEND, LAT = 1500.0, (3600.0, 5500.0)
 CYC = 1.04
-GAT, SCA, PEC = 1.56, 3.8, 0.55
+GAT, SCA, PEC = 1.56, 3.8, 0.6
 
 
 def V(n, a, b, s=1, rows=None):
@@ -78,11 +87,6 @@ def make_ap(T, v, step):
     nm, o = LOC.get(v[0], (v[0], 0)); rows = slice(*v[5]) if v[5] else slice(None)
     x = T[nm][rows, o + v[1]:o + v[2]] if v[3] == 1 else T[nm][rows, o + v[1]:o + v[2]:v[3]]
     return x.indirect(make_ap(T, v[4], step)) if v[4] else x
-
-
-def transfers(o):
-    m, t, a, b = o["fn"]
-    return [(2 * s - 1, V("snd", 432 * (2 * t + s) + a, 432 * (2 * t + s) + b), V("lnd", 432 * (2 * t + 1 - s) + a, 432 * (2 * t + 1 - s) + b)) for s in range(2)]
 
 
 def program():
@@ -122,8 +126,11 @@ def program():
     def cp(o, i, engs="v"):
         either(o, i, lambda q, ap: q.tensor_copy(ap(o), ap(i)), lambda q, ap: q.activation(ap(o), ap(i), F.Copy), engs=engs)
 
-    def neg(o, i, engs="av"):
-        either(o, i, lambda q, ap: q.tensor_scalar(ap(o), ap(i), -1.0, None, A.mult), lambda q, ap: q.activation(ap(o), ap(i), F.Copy, scale=-1.0), engs=engs)
+    def scl(o, i, c=-1.0):
+        either(o, i, lambda q, ap: q.tensor_scalar(ap(o), ap(i), ap(c), None, A.mult), lambda q, ap: q.activation(ap(o), ap(i), F.Copy, scale=ap(c)), [c])
+
+    def plus(o, i, c):
+        either(o, i, lambda q, ap: q.tensor_scalar(ap(o), ap(i), ap(c), None, A.add), lambda q, ap: q.activation(ap(o), ap(i), F.Identity, bias=ap(c)), [c])
 
     def relu(o, i, bias=None):
         if bias is None:
@@ -134,12 +141,11 @@ def program():
     def pos_(o, i):
         either(o, i, lambda q, ap: q.tensor_scalar(ap(o), ap(i), 0.5, None, A.is_gt), lambda q, ap: q.activation(ap(o), ap(i), F.Sign))
 
-    def act(o, i, f, bias=0.0, scale=1.0, acc=None, alt=None):
+    def act(o, i, f, bias=0.0, scale=1.0, acc=None):
         def fn(q, e, ap):
-            if e == "v": return alt(q, ap)
             if acc: return q.activation(ap(o), ap(i), f, bias=ap(bias), scale=ap(scale), accum_out=ap(acc))
             return q.activation(ap(o), ap(i), f, bias=ap(bias), scale=ap(scale))
-        add("av" if alt else "a", fn, [i, bias, scale], [o] + ([acc] if acc else []), 80 + CYC * wid(o))
+        add("a", fn, [i, bias, scale], [o] + ([acc] if acc else []), 80 + CYC * wid(o))
 
     def eq(o, i, c, nc):
         def fn(q, e, ap):
@@ -168,9 +174,11 @@ def program():
             return q.iota(ap(o), pat, base, cm, allow_small_or_imprecise_dtypes=True)
         add("g", fn, [], [o], 150 + 2 * CYC * wid(o))
 
+    def select(o, i, pat, op, fill, base, cm):
+        add("g", lambda q, e, ap: q.affine_select(ap(o), ap(i), pat, op, float(fill), base, cm), [i], [o], 200 + 2 * CYC * wid(o))
+
     def where0(o, pat, base, cm, fill):
-        z = V("Zr", 0, wid(o))
-        add("g", lambda q, e, ap: q.affine_select(ap(o), ap(z), pat, A.not_equal, fill, base, cm), [z], [o], 200 + 2 * CYC * wid(o))
+        select(o, V("Zr", 0, wid(o)), pat, A.not_equal, fill, base, cm)
 
     def mm(*groups, first=True, final=True):
         def fn(q, e, ap):
@@ -185,18 +193,23 @@ def program():
     def dma(eng, pairs, rd, wr, lat=2200.0):
         add(eng, pairs, rd, wr, (1000.0 if eng == "g" else 60.0) * len(pairs), kind="d", lat=lat)
 
+    def plus_dma(o, i):
+        dma("g", [lambda T: (S(T, o[0], o[1], o[2]), S(T, i[0], i[1], i[2]), dict(accum_op=A.add))], [o, i], [o], 3600.0)
+
     P0, P1, P2, P3 = "P0", "P1", "P2", "P3"
+    a384 = lambda n: V(n, 0, 384)
     for q, ks in (("s", range(0, 4)), ("a", range(4, 8))):
         dma(q, [(lambda T, k=k, n=n, u=u: (S(T, "Rs", 0, 768, slice(k + u, 128, 16)), T[n][:, 48 * k:48 * k + 48])) for k in ks for n, u in (("nb", 0), ("en", 8))],
             [], [V("Rs", 0, 768)] if q == "s" else [V("Rs2", 0, 768)])
+    dma("s", [lambda T: (S(T, "NW", 0, 384), T.nb[:, :])], [], [V("NW", 0, 384)]); dma("a", [lambda T: (S(T, "NW", 384, 768), T.en[:, :])], [], [V("NW", 384, 768)])
     dma("s", [lambda T: (S(T, "xw", 32, 1568), T.lens[:, :])], [], [V("xw", 32, 1568)], 3500.0)
-    neg(V("xw", 32, 1568), V("xw", 32, 1568))
+    for a in (32, 800): scl(V("xw", a, a + 768), V("xw", a, a + 768))
 
     def zero(z, zw, parts, lat):
         ps = [(n, c, min(b, c + zw)) for n, a, b in parts for c in range(a, b, zw)]
         dma("s", [(lambda T, n=n, a=a, b=b: (S(T, n, a, b), S(T, z, 0, b - a))) for n, a, b in ps], [V(z, 0, zw)], [V(*p) for p in parts], lat)
     mset(V("Zf", 0, 384), 0); zero("Zf", 384, [("EW", 384, 3456)], 6000.0)
-    mset(V("Zr", 0, 1536), 0); zero("Zr", 1536, [("xw", 1568, 2720), ("Z", 0, 1728), ("ix", 1920, 2688), ("GD", 0, 128), ("GD", 704, 800)], 5000.0)
+    mset(V("Zr", 0, 1536), 0); zero("Zr", 1536, [("xw", 1568, 2720), ("Z", 0, 1728), ("Zs", 0, 1440), ("PN", 768, 3488), ("FR", 0, 32), ("ix", 1920, 2688), ("GD", 0, 128), ("GD", 704, 800)], 5000.0)
     pcn = {}
 
     def pc(n, w=1):
@@ -210,7 +223,6 @@ def program():
     iota(V("CMx", 0, 144), [[1, 144]], -15)
     iota(V("CH", 0, 128), [[1, 16], [0, 8]])
     iota(V("PI", 8, 24), [[1, 16]])
-    iota(V("PI", 32, 40), [[1, 4], [4, 2]])
     iota(V("pos", 0, 48), [[1, 48]])
     iota(V("lo8", 0, 800), [[0, 25], [1, 32]])
     iota(V("hi8", 0, 800), [[1, 25], [0, 32]])
@@ -247,13 +259,13 @@ def program():
         ts(Z(n), V("CMx", 0, 144), tg_, w, A.is_equal, A.mult)
 
     def diag(n, c):
-        where0(M(n), [[1, 128]], 0, -1, float(c))
+        where0(M(n), [[1, 128]], 0, -1, c)
     zm("lo", l, nh); zm("hi", l, h); zm("W", l, wlh)
     ts(M("I"), CM0, r, None, A.is_equal)
     ts(V("CH", 0, 128), V("CH", 0, 128), pc("g2"), None, A.subtract)
     ts(M("t1"), V("CH", 0, 128), 0, None, A.is_ge); ts(M("t2"), V("CH", 0, 128), 2, None, A.is_lt); tt(M("Blk"), M("t1"), M("t2"), A.mult)
-    ts(pc("mhh"), h, -1, None, A.mult); ts(M("NHi"), M("Blk"), pc("mhh"), None, A.mult)
-    ts(M("t1"), CM0, r, None, A.is_gt); tt(M("Tri"), M("t1"), M("Blk"), A.mult)
+    ts(pc("mhh"), h, -1, None, A.mult); scl(M("NHi"), M("Blk"), pc("mhh"))
+    ts(M("t1"), CM0, r, None, A.is_gt); tt(M("TriM"), M("t1"), M("Blk"), A.mult); select(M("TriM"), M("TriM"), [[1, 128]], A.not_equal, -500, 0, -1)
     ts(pc("n128"), h, -128, None, A.mult)
     mset(V("RR", 0, 32), 0); mset(V("RR", 800, 832), 0)
     SLv = V("SL", 0, 48); Rsw = IND("Rs", 0, 768, SLv)
@@ -262,56 +274,54 @@ def program():
     act(V("b2", 0, 768), V("b1", 0, 768), F.Relu, pc("b4128"), 32.0)
     tt(V("b3", 0, 768), Rsw, V("b2", 0, 768), A.subtract)
     for Pn, za, zb, o in ((P0, Z("lo", 0), Z("lo", 8), 32), (P1, Z("hi", 0), Z("hi", 8), 832)):
-        mm(*[[(V(Pn, a, b), za, V("b3", a, b)), (V(Pn, a, b), zb, V("b1", a, b))] for a, b in ((0, 512), (512, 768))])
+        mm(*[[(V(Pn, a, b), zb, V("b1", a, b))] for a, b in ((0, 512), (512, 768))], final=False)
+        mm(*[[(V(Pn, a, b), za, V("b3", a, b))] for a, b in ((0, 512), (512, 768))], first=False)
         relu(V("RR", o, o + 768), V(Pn, 0, 768), pc("n128"))
 
     def wrap(o, n, a, b):
         return [(o, Z("W", 0), V(n, a, b, 2)), (o, Z("W", 8), V(n, a + 1, b, 2))]
-    mm(wrap(V(P2, 512, 896), "RR", 32, 800)); cp(V("W", 0, 384), V(P2, 512, 896))
-    ts(Z("F"), Z("hi"), 2000, None, A.mult); diag("I1536", 1536)
-    iota(V("Lf", 0, 384), [[2, 384]], 32); act(V("Lf", 0, 384), V("Lf", 0, 384), F.Identity, h)
-    iota(V("Lf", 384, 768), [[0, 16], [16, 24]], 1618); act(V("Lf", 384, 768), V("Lf", 384, 768), F.Identity, r)
-    tt(V("Kn", 0, 384), V("Lf", 0, 384), V(P2, 512, 896), A.is_gt); ts(V("Ke", 0, 768), V("RR", 32, 800), 1, None, A.is_ge)
-    o = V(P1, 0, 384)
-    ts(pc("wp"), h, -94, 96, A.mult, A.add); zm("p", l, pc("wp")); ts(Z("q"), Z("lo"), -1536, None, A.mult); ts(V("G", 0, 768), V("RR", 832, 1600), 16, None, A.is_ge)
-    mm([(o, Z(z_, 8 * u), V(n_, a_ + u, a_ + 768, 2)) for z_, n_, a_ in (("p", "RR", 832), ("q", "G", 0), ("lo", "G", 0), ("F", "Ke", 0)) for u in range(2)] +
-       [(o, M("I1536"), V("Kn", 0, 384))])
-    tt(V("tg", 384, 768), o, V("Lf", 384, 768), A.max); ts(V("EO", 0, 384), V("tg", 384, 768), -1618, None, A.add)
+    nbw, enw = V("NW", 0, 384), V("NW", 384, 768)
+    ts(V("W", 0, 384), nbw, 32, None, A.add); ts(V("Ke", 0, 384), nbw, 0, 4, A.is_ge, A.mult)
+    for i in range(BRV): ts(V("BR", 128 * i, 128 * i + 128), M("Blk"), E(i), 4096, A.mult, A.mult)
+    for u in range(BRV // 4, 4): where0(V("BR", 512 * u, 512 * u + 512), [[1, 4], [16, 8], [0, 16]], 4 * u, -1, 4096)
+    mm([(V(P2, 0, 36), M("I"), V("Ke", 48 * k + 6, 48 * k + 42)) for k in range(8)]); cp(V("cw", 0, 36), V(P2, 0, 36), "av")
+    for u in range(2):
+        mm([(V(P2, 512 * u + i, 512 * u + 288, 16), V("BR", 128 * i, 128 * i + 128), V("cw", 18 * u, 18 * u + 18)) for i in range(16)])
+        act(V("GD", 128 + 288 * u, 416 + 288 * u), V(P2, 512 * u, 512 * u + 288), F.Relu, pc("ten"), -1.0 / 16384)
+    diag("D96", 96); diag("D1536", 1536); diag("N1536", -1536)
+    iota(V("Lf", 0, 384), [[0, 8], [16, 48]]); plus(V("Lf", 0, 384), V("Lf", 0, 384), r)
+    iota(V("Lf", 384, 768), [[0, 16], [16, 24]], -192255); plus(V("Lf", 384, 768), V("Lf", 384, 768), r)
+    tt(V("Kn", 0, 384), nbw, V("Lf", 0, 384), A.is_lt); cp(a384("cx"), enw); ts(V("Kn", 384, 768), enw, 1.0 / 16, 128.53125, A.mult, A.add)
+    o = V(P3, 0, 384)
+    mm([(o, M("D96"), a384("cx")), (o, M("N1536"), V("Kn", 384, 768)), (o, M("I"), V("Kn", 384, 768)), (o, M("D1536"), V("Ke", 0, 384)), (o, M("D1536"), V("Kn", 0, 384))])
+    tt(V("tg", 384, 768), o, V("Lf", 384, 768), A.max); ts(V("EO", 0, 384), V("tg", 384, 768), 192255, None, A.add)
     mm(*[[(V(P3, a, b), Z("lo", 0), V("lo8", a, b)), (V(P3, a, b), Z("hi", 8), V("hi8", a, b))] for a, b in ((0, 512), (512, 800))])
     cp(V("RR", 1600, 2400), V(P3, 0, 800), "av")
-    where0(V("SEL", 0, 16), [[0, 2], [16, 8]], 0, -1, -131072.0)
-    where0(M("SE"), [[1, 8], [-8, 2], [16, 8]], 8, -1, 1.0)
-    iota(M("SN"), [[1, 8], [0, 2], [16, 8]]); ts(pc("gl"), l, pc("g16"), None, A.add); ts(pc("w128"), wlh, 128, None, A.mult)
-    ts(M("SN"), M("SN"), pc("gl"), pc("w128"), A.is_equal, A.mult)
+    where0(V("SEL", 0, 16), [[0, 2], [16, 8]], 0, -1, -131072)
+    where0(M("SE"), [[1, 8], [-8, 2], [16, 8]], 8, -1, 1)
+    where0(M("SN"), [[1, 8], [0, 2], [16, 8]], 0, -1, 128); select(M("SN"), M("SN"), [[1, 8], [0, 2], [16, 8]], A.not_equal, 4096, 8, -1)
     iota(V("CX", 0, 48), [[0, 48]], -8); iota(V("CX", 48, 96), [[0, 4], [16, 2], [0, 6]])
     iota(V("im", 0, 384), [[1, 384]])
     ts(pc("sw"), pc("g16"), 2, 16, A.mult, A.add); ts(pc("sw"), pc("sw"), r, None, A.add); ts(V("SW", 0, 272), V("im", 0, 272), pc("sw"), None, A.is_equal)
-    for u in range(2): where0(V("BR", 1024 * u, 1024 * u + 1024), [[1, 8], [16, 8], [0, 16]], 8 * u, -1, 4096.0)
     iota(V("OWN", 96, 192), [[0, 96]], 1000000); iota(V("cc", 0, 1), [[0, 1]], 500); iota(V("rkw", 36, 37), [[0, 1]], 999); iota(V("id0", 0, 96), [[1, 96]])
-    diag("N128", -128); diag("D2", -2); diag("I256", 256); diag("nI", -1)
-    tt(M("Wc"), Z("W", 0), Z("W", 8), A.add); ts(M("Wk"), M("Wc"), 4096, None, A.mult); tt(M("W2"), Z("hi", 0), Z("W", 8), A.add)
-    ts(pc("h8"), h, 8, None, A.mult); ts(pc("l8"), l, 8, None, A.mult); ts(pc("l8b"), l, 8, -16, A.mult, A.add); ts(pc("l64"), l, 8, -64, A.mult, A.add)
-    ts(pc("El", 8), V("PI", 8, 16), l, None, A.is_equal)
-    tt(pc("we"), col(pc("El"), 0), wlh, A.mult); tt(pc("ws"), l, nh, A.mult)
+    diag("N128", -128); diag("D2", -2); diag("nI", -1)
+    tt(M("Wc"), Z("W", 0), Z("W", 8), A.add); scl(M("Wk"), M("Wc"), 4096.0); scl(M("NWk"), M("Wc"), -4096.0); tt(M("W2"), Z("hi", 0), Z("W", 8), A.add)
+    ts(pc("h8"), h, 8, None, A.mult); ts(pc("l8"), l, 8, None, A.mult); ts(pc("l8b"), l, 8, -16, A.mult, A.add); ts(pc("l64"), l, -8, 64, A.mult, A.add)
+    ts(pc("we"), l, 0, wlh, A.is_equal, A.mult); tt(pc("ws"), l, nh, A.mult)
     ts(pc("wu"), E(9), 32, E(8), A.mult, A.add); ts(pc("wu"), pc("wu"), 8, None, A.mult)
     tt(pc("wa"), E(8), E(9), A.add); tt(pc("wb"), E(10), E(11), A.add)
     zm("all", 0, 1); zm("Y2", pc("h8"), -4); zm("s", 0, pc("ws")); zm("u", 0, pc("wu")); zm("A", pc("l8"), pc("wa")); zm("B", pc("l8b"), pc("wb"))
-    zm("0", 0, E(0)); zm("ir", 0, r)
-    zm("2", 8, 1); tt(Z("2"), Z("2"), Z("all"), A.add)
-    for m_ in range(4):
-        ts(pc("sp%d" % m_), h, 2 * m_ + 1, None, A.add); zm("sp%d" % m_, l, pc("sp%d" % m_))
+    zm("0", 0, E(0)); zm("ir", 0, r); zm("uh", 0, h); zm("lh", 0, nh); zm("aw", 0, wlh); zm("a0", 0, pc("we"))
+    zm("2", 8, 1); tt(Z("2"), Z("2"), Z("all"), A.add); scl(Z("2"), Z("2"), -8.0)
     ts(M("t1"), V("CH", 0, 128), -99, None, A.add); tt(M("t2"), M("t1"), M("Blk"), A.mult); ts(V("CH", 0, 128), M("t2"), 99, None, A.add)
     CH = V("CH", 0, 128)
     ts(V("PI", 24, 32), V("PI", 8, 16), -1, l, A.mult, A.add); ts(V("PI", 24, 32), V("PI", 24, 32), 7, None, A.bitwise_and); cp(pc("dd", 8), V("PI", 24, 32))
     ts(pc("nw"), wlh, -1, None, A.mult); ts(pc("nwe"), pc("we"), -1, None, A.mult)
     for k in range(8): ts(M("N%d" % k), CH, col(pc("dd"), k), pc("nw"), A.is_equal, A.mult)
     ts(M("NV"), CH, 1, pc("nwe"), A.is_equal, A.mult); ts(M("NLo"), CH, 0, -1, A.is_equal, A.mult); ts(M("R0"), CH, 0, E(0), A.is_equal, A.mult)
-    ts(pc("de", 8), V("PI", 32, 40), -2, r, A.mult, A.add)
-    for k in range(8): ts(M("R%d%d" % (k // 2, k % 2)), CH, col(pc("de"), k), -1, A.is_equal, A.mult)
-    ts(M("t1"), M("I"), -500, None, A.mult); tt(M("TriM"), M("t1"), M("Tri"), A.add)
     ts(M("t1"), CM0, l, -1, A.is_gt, A.mult); tt(M("t2"), M("t1"), M("NLo"), A.mult); ts(M("t1"), CM0, l, -100, A.is_equal, A.mult); tt(M("CF"), M("t1"), M("t2"), A.add)
-    ts(pc("t8"), h, 8, None, A.add)
-    for j in range(8): ts(M("U%d" % j), CM0, pc("t8"), col(pc("El"), j), A.is_equal, A.mult)
+    u0 = [M("U%d" % j) for j in range(8)][0][1]; zero("Zr", 1536, [("M", u0, u0 + 1024), ("W2", 768, 1600)], 3000.0)
+    for u in range(2): where0(V("M", u0 + 8 + u, u0 + 1024, 16), [[1, 8], [16, 8]], 8 * u, -1, 1)
     iota(V("CO", 0, 192), [[1, 192]], -64)
     ts(pc("to"), gr, 8, l, A.mult, A.add); ts(V("ZO", 0, 192), V("CO", 0, 192), pc("to"), wlh, A.is_equal, A.mult)
     iota(V("jk", 0, 32), [[0, 4], [1, 8]]); iota(V("jk", 32, 64), [[1, 4], [1, 8]], 1)
@@ -343,63 +353,66 @@ def program():
     tt(V("m2", 0, 112), V("m2", 0, 112), V("m3", 0, 112), A.mult); ts(V("XL", 0, 112), V("m2", 0, 112), 224, None, A.add)
     for n in range(14): M("X%d" % n)
     for n in range(0, 14, 2): cp(V("M", mn_["X%d" % n], mn_["X%d" % n] + 256), IND("PAT", 0, 240, V("XL", 8 * n, 8 * n + 16)), "av")
-    iota(V("c8", 0, 384), [[0, 384]], 8); iota(V("Bw", 0, 32), [[0, 32]]); iota(V("Aw", 0, 32), [[-1024, 2], [0, 16]])
+    TR = M("TR8")
+    select(TR, V("Zr", 0, 128), [[-16, 8], [0, 2], [-1, 8]], A.is_ge, 1, -8, 1); select(TR, TR, [[-16, 8], [0, 16]], A.is_ge, 0, -8, 1)
+    select(TR, TR, [[16, 8], [0, 2], [1, 8]], A.not_equal, -500, 8, -1)
+    iota(V("c8", 0, 384), [[0, 384]], 8); iota(a384("cm1"), [[0, 384]], -1); iota(V("Bw", 0, 32), [[0, 32]]); iota(V("Aw", 0, 32), [[-1024, 2], [0, 16]])
     iota(V("TG", 0, 128), [[0, 128]], -1024); iota(V("TG", 704, 800), [[0, 96]], -1024); ts(V("pk", 0, 36), V("pos", 0, 36), 128, None, A.add)
     iota(V("J8", 0, 768), [[0, 96], [8, 8]], 36); iota(V("ids", 0, 192), [[1, 192]], 2)
     iota(V("big", 0, 384), [[0, 24], [1, 16]]); ts(V("big", 0, 384), V("big", 0, 384), r, 4096, A.is_equal, A.mult)
-    iota(V("W2", 768, 1600), [[0, 832]], -8); ts(V("W2", 768, 1600), V("W2", 768, 1600), E(9), None, A.mult)
+    ts(pc("m9"), E(9), -8, None, A.mult); plus(V("W2", 768, 1600), V("W2", 768, 1600), pc("m9"))
     iota(V("c884", 0, 192), [[0, 192]], 884); iota(V("cumb", 0, 1), [[0, 1]], 500); iota(V("num", 0, 2), [[0, 2]], 999); iota(V("Nw", 0, 2), [[0, 2]])
-    iota(V("xw", 0, 32), [[0, 32]]); iota(V("mid", 0, 168), [[0, 168]], 12582912 + 31)
-    iota(V("thr", 0, 48), [[0, 48]])
-    iota(V("slf", 0, 96), [[672, 2], [2, 48]], 32); ts(V("slf", 0, 96), V("slf", 0, 96), h, None, A.add)
-    iota(V("pc8", 0, 96), [[768, 2], [16, 48]], 15); ts(V("pc8", 0, 96), V("pc8", 0, 96), pc("h8"), None, A.add)
-    for s in range(2): cp(V("dum", 48 * s, 48 * s + 48), V("pos", 0, 48), "av")
+    iota(V("xw", 0, 32), [[-300, 2], [0, 16]]); iota(V("mid", 0, 168), [[0, 168]], 12582912 + 31)
+    ts(pc("far"), nh, 10000, None, A.mult); iota(V("slf", 0, 96), [[1, 96]], 704); plus(V("slf", 0, 96), V("slf", 0, 96), pc("far"))
+    ts(pc("cb"), h, 657, -1360, A.mult, A.add); iota(V("id16", 0, 96), [[1, 96]], 16); iota(V("cs", 0, 1), [[0, 1]], 500)
+    iota(V("PT", 0, 16), [[0, 16]], 999); iota(V("CT", 0, 16), [[0, 16]]); ts(V("pk", 120, 126), V("pos", 0, 6), 404, None, A.add)
     ts(V("pk", 48, 96), V("pos", 0, 48), -512, None, A.add); ts(V("pk", 96, 108), V("pos", 0, 12), 308, None, A.add)
-    ts(V("pk", 112, 118), V("pos", 0, 6), 500.5, None, A.add)
-    ts(M("t1"), M("I"), E(10), None, A.mult); ts(M("t2"), M("I"), E(11), None, A.mult)
+    ts(V("pk", 128, 152), V("pos", 0, 24), 500.5, None, A.add)
+    scl(M("t1"), M("I"), E(10)); scl(M("t2"), M("I"), E(11))
     mm([(V(P3, 0, 384), M("t1"), V("lo8", 0, 384)), (V(P3, 0, 384), M("t2"), V("hi8", 0, 384))])
     for t in range(3):
-        ts(pc("nm%d" % t), E(11), 49 + 12 * t, None, A.mult); act(V("NM", 384 * t, 384 * t + 384), V(P3, 0, 384), F.Identity, pc("nm%d" % t))
-    a384 = lambda n: V(n, 0, 384)
-    if EWV: iota(a384("V0"), [[1, 48], [0, 8]], 32)
+        ts(pc("nm%d" % t), E(11), 49 + 12 * t, None, A.mult); plus(V("NM", 384 * t, 384 * t + 384), V(P3, 0, 384), pc("nm%d" % t))
+    iota(V("Vf", 0, 768), [[1, 768]], 32)
     for k in range(16):
         eo = IND("EW", 0, 3456, V("EO", 24 * k, 24 * k + 24)); vf = V("Vf", 384 * (k % 2), 384 * (k % 2) + 384)
-        if k >= 16 - EWV:
-            ts(eo, a384("V0"), 1.0, 48.0 * k, A.mult, A.add)
-        else:
-            iota(vf, [[1, 48], [0, 8]], 32 + 48 * k)
-            add("a", lambda q, e, ap, eo=eo, vf=vf: q.activation(ap(eo), ap(vf), F.Silu), [vf], [eo], 80 + CYC * SCA * 384)
+        either(eo, vf, lambda q, ap, eo=eo, vf=vf: q.tensor_copy(ap(eo), ap(vf)), lambda q, ap, eo=eo, vf=vf: q.activation(ap(eo), ap(vf), F.Silu))
     dma("s", [(lambda T, u=u: (S(T, "ZE", 96 * u, 96 * u + 96), S(T, "EW", 384 + 1536 * u, 1920 + 1536 * u, slice(0, 128, 16)))) for u in range(2)],
         [V("EW", 384, 3456)], [V("ZE", 0, 192)])
     ts(V("i2", 0, 192), V("ZE", 0, 192), 16, None, A.max); cp(V("LA", 0, 96), V("i2", 0, 96)); cp(V("LB", 0, 96), V("i2", 96, 192))
-    iota(V("ga", 1920, 2688), [[0, 768]]); iota(V("Pw", 0, 16), [[0, 16]], 300)
+    zero("Zf", 384, [("ga", 1920, 2688)], 2500.0)
 
-    sp = ((0, 512), (512, 576)); sq = ((0, 512), (512, 768)); late = ([], [])
+    sp = ((0, 512), (512, 576)); sq = ((0, 512), (512, 768)); late = []
     blank = lambda o: (o, V("Zr", 0, 128), V("Zr", 0, wid(o)))
     for t in range(3):
         Et = 1536 + 384 * t; last = t == 2
-        zero("Zr", 1536, [("Aux", 768, 6912)], 8000.0)
         n576 = lambda n: V(n, 0, 576)
-        pos_(n576("fil"), V("RR", 128, 704))
-        mm(*[[(V(P1, a, b), M("NHi"), V("fil", a, b))] + [(V(P1, a, b), M("N128"), V("ctr", 576 * u + a, 576 * u + b)) for u in range(t)] for a, b in sp])
-        relu(V("GD", 128, 704), V(P1, 0, 576), pc("ten"))
+        if t:
+            pos_(n576("fil"), V("RR", 128, 704))
+            mm(*[[(V(P1, a, b), M("N128"), V("ctr", 576 * u + a, 576 * u + b)) for u in range(t)] + [(V(P1, a, b), M("NHi"), V("fil", a, b))] for a, b in sp])
+            relu(V("GD", 128, 704), V(P1, 0, 576), pc("ten"))
+            inner()
+        zero("Zr", 1536, [("Aux", 768, 6912)], 8000.0)
         kb = lambda u, B: V(P0, 512 * u + B, 512 * u + 384, 6)
-        mm(*[[blank(V(P0, 512 * u, 512 * u + 384))] + [(kb(u, B), V("RR", o + 128 * B, o + 128 * B + 128), half(M(m_), u)) for B in range(6) for o, m_ in ((32, "SN"), (832, "SE"))]
-             for u in range(2)], final=False)
-        for B in range(6):
+        keys = lambda o, m_, first: mm(*[[(kb(u, B), V("RR", o + 128 * B, o + 128 * B + 128), half(M(m_), u)) for B in range(6)] for u in range(2)], first=first, final=False)
+        for k in range(0 if t else 8):
+            cp(V("G1", 768 * k, 768 * k + 768), IND("GD", 0, 800, V("W", 48 * k, 48 * k + 48)), "av"); c = 512 * (k // 4) + 96 * (k % 4)
+            mm([(V(P0, c + B, c + 96, 6), V("G1", 768 * k + 128 * B, 768 * k + 128 * B + 128), V("SEL", 0, 16)) for B in range(6)], first=k % 4 == 0, final=False)
+        keys(32, "SN", t > 0)
+        if not t: keys(832, "SE", False); mm([blank(V(P0, 0, 8))], [blank(V(P0, 512, 520))], first=False)
+        for B in range(6 if t else 0):
+            if B == KEYS: keys(832, "SE", False)
             cp(V("G1", 1024 * B, 1024 * B + 1024), IND("GD", 0, 800, V("W", 64 * B, 64 * B + 64)), "av")
             mm(*[[(V(P0, 512 * u + 96 * k + B, 512 * u + 96 * k + 96, 6), V("G1", 1024 * B + 4 * u + k, 1024 * B + 1024, 8), V("SEL", 0, 16)) for k in range(4)] for u in range(2)],
                first=False, final=B == 5)
-        mm([blank(V(P1, 0, 96))] + [(V(P1, B, 96, 6), V(n_, o + 128 * B, o + 128 * B + 128), w_) for B in range(6)
-                                     for n_, o, w_ in (("GD", 32, V("SEL", 0, 16)), ("RR", 1632, V("M", mn_["SN"], mn_["SN"] + 16)))])
+        mm([(V(P1, B, 96, 6), V(n_, o + 128 * B, o + 128 * B + 128), w_) for B in range(6)
+            for n_, o, w_ in (("GD", 32, V("SEL", 0, 16)), ("RR", 1632, V("M", mn_["SN"], mn_["SN"] + 16)))])
         cp(V("OWN", 0, 96), V(P1, 0, 96), "av")
         for u in range(4): tt(V("KS", 0, 192), V(P0, 512 * (u // 2) + 192 * (u % 2), 512 * (u // 2) + 192 * (u % 2) + 192), V("KS" if u else "OWN", 0, 192), A.min)
         tt(V("KI", 0, 96), V("KS", 0, 96), V("KS", 96, 192), A.min)
         K1, K2 = V("KI", 0, 48), V("KI", 48, 96)
         ts(V("XI", 0, 48), K1, 11, 63, A.arith_shift_right, A.bitwise_and); ts(V("XI", 48, 96), K1, 7, 15, A.arith_shift_right, A.bitwise_and)
         tt(V("XR", 0, 96), V("XI", 0, 96), V("CX", 0, 96), A.add); ts(V("XR", 96, 192), V("XR", 0, 96), -1, None, A.add); ts(V("XR", 192, 384), V("XR", 0, 192), -2, None, A.add)
-        for j in range(9):
-            eq(V("OH", 384 * j, 384 * j + 384), a384("XR"), 4 * j, col(pc("m4", 9), j)); ops[-1]["cost"] = 60 + CYC * 192
+        for j in range(9): ts(V("OH", 384 * j, 384 * j + 384), a384("XR"), 4 * j, None, A.is_equal)
         hp = V(P1, 512, 548)
         mm([(hp, Z("0", i), V("GD", 128 + i, 704, 16)) for i in range(15)], final=False)
         mm([(V(P1, 512, 548, 1, (c // 12 * 32, c // 12 * 32 + 32)), V("OH", 48 + c, 3072, 96), V("OH", c, 3456, 96)) for c in range(48)] +
@@ -408,7 +421,7 @@ def program():
         mm([(V(P1, 0, 36), M("Blk"), V("ch", 0, 36))]); mm([(V(P0, 0, 36), M("TriM"), V("ch", 0, 36))])
         scan(V("cc", 1, 37), V(P1, 0, 36), V("Zr", 0, 36), 500.0, A.add, A.max)
         tt(V("rkw", 0, 36), V(P0, 0, 36), V("cc", 0, 36), A.add)
-        for c in range(6): act(V("junk", 48 * c, 48 * c + 36), V("cc", 1, 37), F.Sign, V("pk", 112 + c, 113 + c), -1.0, acc=V("vc", c, c + 1))
+        for c in range(6): act(V("junk", 48 * c, 48 * c + 36), V("cc", 1, 37), F.Sign, V("pk", 128 + c, 129 + c), -1.0, acc=V("vc", c, c + 1))
         ts(V("QL", 0, 6), V("vc", 0, 6), 0.5, 18, A.mult, A.add)
         tt(V("junk2", 0, 96), IND("rkw", 0, 37, V("QL", 0, 6)), V("id0", 0, 96), A.is_equal)
         ts(V("vd", 0, 6), V("vc", 0, 6), 8, 416, A.mult, A.add); ts(V("vd", 8, 14), V("vc", 0, 6), 35, None, A.is_lt); tt(V("vd", 0, 6), V("vd", 0, 6), V("vd", 8, 14), A.mult)
@@ -424,43 +437,45 @@ def program():
         ts(V("cw", 0, 36), V("rkw", 0, 36), 95.5, None, A.is_lt); tt(V("cn", 0, 36), V("cw", 0, 36), V("pk", 0, 36), A.mult)
         ct = lambda a, b: V("ctr", 576 * t + a, 576 * t + b)
         for u in range(2):
-            o = V(P2, 512 * u, 512 * u + 288); tgt = V("TG", 128 + 288 * u, 416 + 288 * u)
-            mm(*[[(V(P2, 512 * u + i, 512 * u + 288, 16), V("BR", 128 * i, 128 * i + 128), V("cn", 18 * u, 18 * u + 18))] for i in range(16)])
-            either(tgt, o, lambda q, ap, tgt=tgt, o=o: q.tensor_scalar(ap(tgt), ap(o), -1024.0, None, A.add),
-                   lambda q, ap, tgt=tgt, o=o: q.activation(ap(tgt), ap(o), F.Identity, bias=ap(pc("m1k"))), [pc("m1k")])
-            pos_(ct(288 * u, 288 * u + 288), o)
-        cp(V("Rv", 0, 192), IND("RR", 0, 2400, V("VL", 0, 12)))
-        while late[0]: late[0].pop()()
+            o = V(P2, 512 * u, 512 * u + 288)
+            mm([(V(P2, 512 * u + i, 512 * u + 288, 16), V("BR", 128 * i, 128 * i + 128), V("cn", 18 * u, 18 * u + 18)) for i in range(16)])
+            plus(V("TG", 128 + 288 * u, 416 + 288 * u), o, pc("m1k")); pos_(ct(288 * u, 288 * u + 288), o)
+        if not FIRST[t]: cp(V("Rv", 0, 192), IND("RR", 0, 2400, V("VL", 0, 12)))
+        for f in late: f()
+        late.clear()
+        if FIRST[t]: cp(V("Rv", 0, 192), IND("RR", 0, 2400, V("VL", 0, 12)))
         mm(wrap(V(P0, 0, 48), "Rv", 0, 96)); cp(V("UL", 0, 48), V(P0, 0, 48))
         ts(V("fv", 0, 96), V("Rv", 0, 96), 1, None, A.is_ge)
         for u in range(2): cp(V("G", 384 * u, 384 * u + 384), IND("RR", 0, 800, V("UL", 24 * u, 24 * u + 24)), "av")
-        parts(cp, SPL[0], V("Lu", 0, 768), IND("xw", 0, 2720, V("AO", 48, 96)), "av"); neg(V("Lu", 768, 1536), V("Lu", 0, 768))
+        parts(cp, SPL[0], V("Lu", 0, 768), IND("xw", 0, 2720, V("AO", 48, 96)), "av"); scl(V("Lu", 768, 1536), V("Lu", 0, 768))
         parts(cp, SPL[0], V("Aw", 32, 800), IND("TG", 0, 800, V("AO", 0, 48)), "av")
         parts(relu, SPL[0], V("Bw", 32, 800), V("Aw", 32, 800))
-        while late[1]: late[1].pop()()
+        if TWO: parts(cp, SPL[0], V("tg", 0, 768), IND("TG", 0, 800, V("AO", 0, 48)), "av")
         for u in range(2):
             a, b = 384 * u, 384 * u + 384; o = V(P2, 512 * u, 512 * u + 384)
-            mm([(o, M("Wk"), V("RR", 32 + a, 32 + b)), (o, M("N128"), a384("c8"))]); tt(V("clr", a, b), o, V("Aw", 32 + a, 32 + b), A.is_equal)
-        for u, n_ in enumerate(("Aw", "Bw")):
-            dma("g", [lambda T, u=u, n_=n_: (S(T, n_, 32, 800), S(T, "Lu", 768 * u, 768 * u + 768), dict(accum_op=A.add))], [V("Lu", 768 * u, 768 * u + 768), V(n_, 32, 800)], [V(n_, 32, 800)], 3000.0)
+            mm([(o, M("Wk"), V("RR", 32 + a, 32 + b)), (o, M("N128"), a384("c8"))]); tt(V("clr", a, b), o, V("tg", a, b) if TWO else V("Aw", 32 + a, 32 + b), A.is_equal)
+        plus_dma(V("Aw", 32, 800), V("Lu", 0, 768)); plus_dma(V("Bw", 32, 800), V("Lu", 768, 1536))
         for kb_, o_ in (("Kn", 32), ("Ke", 832)):
             for u in range(2):
                 a, b = 384 * u, 384 * u + 384; o = V(P2, 512 * u, 512 * u + 384)
                 mm([(o, M("I"), V("RR", o_ + a, o_ + b)), (V(P2, 512 * u + 96 - 96 * u, 512 * u + 384 - 96 * u), M("N128"), ct(288 * u, 288 * u + 288)), (o, M("N128"), V("clr", a, b))])
                 relu(V(kb_, a, b), o)
-        for it, Pn in enumerate((P1, P0, P1)):
-            mm(*[[(V(Pn, a, b), M("W2" if it == 2 else "Wc"), V("G", a, b))] +
-                 [(V(Pn, a + j, b, 8), M("NV") if it == 2 else M("N%d" % ((j + 2 * it + 1) % 8)), V("Rv", a // 8 + (96 if it == 2 else 0), b // 8 + (96 if it == 2 else 0))) for j in range(8)]
-                 for a, b in sq])
-            for a, b in sq: eq(V("EQ", 768 * it + a, 768 * it + b), V(Pn, a, b), 0, 0.0)
-        mm(*[[(V(P0, 96 * b, 96 * b + 96), M("X%d" % b), V("fv", 0, 96))] + [(V(P0, 96 * b, 96 * b + 96), Z("Y2", j), V("EQ", 768 * b + j, 768 * b + 768, 8)) for j in range(8)] for b in range(2)])
-        act(V("wish", 0, 192), V(P0, 0, 192), F.Relu, pc("m1"), alt=lambda q, ap: q.tensor_scalar(ap(V("wish", 0, 192)), ap(V(P0, 0, 192)), 1.5, None, A.is_ge))
+        for n_, (it, a) in enumerate([(it, a) for a in (0, 384) for it in (0, 1, 2)]):
+            Pn, c = (P1, P0)[n_ // 2 % 2], n_ % 2 * 512; rv = V("Rv", a // 8 + 96 * (it == 2), a // 8 + 48 + 96 * (it == 2))
+            mm([(V(Pn, c + j, c + 384, 8), M("NV") if it == 2 else M("N%d" % ((j + 2 * it + 1) % 8)), rv) for j in range(8)], final=False)
+            mm([(V(Pn, c, c + 384), M("W2" if it == 2 else "Wc"), V("G", a, a + 384))], first=False)
+            eq(V("EQ", 768 * it + a, 768 * it + a + 384), V(Pn, c, c + 384), 0, 0.0)
+        for b in range(2):
+            mm([(V(P0, 96 * b, 96 * b + 96), M("X%d" % b), V("fv", 0, 96))] + [(V(P0, 96 * b, 96 * b + 96), Z("Y2", j), V("EQ", 768 * b + j, 768 * b + 768, 8)) for j in range(8)])
+        relu(V("wish", 0, 192), V(P0, 0, 192), pc("m1"))
         mm([(V(P0, 512, 608), Z("all", j), V("EQ", 1536 + j, 2304, 8)) for j in range(8)])
-        act(V("nf", 0, 96), V(P0, 512, 608), F.Identity, pc("l64"), alt=lambda q, ap: q.tensor_scalar(ap(V("nf", 0, 96)), ap(V(P0, 512, 608)), ap(pc("l64")), None, A.add))
-        mm(*[[(V(P1, 192 * e + b, 192 * e + 192, 2), M("X%d" % (2 + 4 * sb + 2 * e + b)), V("wish", 96 * sb, 96 * sb + 96)) for sb in range(2)] for e in range(2) for b in range(2)])
-        mm(*[[(V(P1, 512 + 192 * e + b, 704 + 192 * e, 2), M("X%d" % (10 + 2 * e + b)), V("nf", 0, 96))] for e in range(2) for b in range(2)])
-        cp(V("Nw", 2, 386), V(P1, 0, 384), "av")
-        tt(V("fw", 0, 384), V("Nw", 2, 386), V(P1, 512, 896), A.is_lt); tt(V("ok", 0, 192), V("fw", 0, 192), V("fw", 192, 384), A.mult)
+        nf, po = V("nf", 0, 96), V(P0, 512, 608)
+        either(nf, po, lambda q, ap: q.tensor_scalar(ap(nf), ap(po), -1.0, ap(pc("l64")), A.mult, A.add),
+               lambda q, ap: q.activation(ap(nf), ap(po), F.Identity, bias=ap(pc("l64")), scale=-1.0), [pc("l64")])
+        codes = lambda c: [(V(P1, c + 192 * e + b, c + 192 * e + 192, 2), M("X%d" % (2 + 4 * sb + 2 * e + b)), V("wish", 96 * sb, 96 * sb + 96)) for e in range(2) for b in range(2) for sb in range(2)]
+        mm([(V(P1, 512 + 192 * e + b, 704 + 192 * e, 2), M("X%d" % (10 + 2 * e + b)), nf) for e in range(2) for b in range(2)], final=False)
+        mm(codes(512), first=False); mm(codes(0)); cp(V("Nw", 2, 386), V(P1, 0, 384), "av")
+        ts(V("fw", 0, 384), V(P1, 512, 896), -0.5, None, A.is_lt); tt(V("ok", 0, 192), V("fw", 0, 192), V("fw", 192, 384), A.mult)
         mm([(V(P0, 512, 704), M("Blk"), V("ok", 0, 192))]); mm([(V(P0, 0, 192), M("TriM"), V("ok", 0, 192))])
         scan(V("cumb", 1, 193), V(P0, 512, 704), V("c884", 0, 192), 500.0, A.add, A.min)
         scan(V("ws", 0, 192), V("big", 0, 192), V("cumb", 0, 192), 0.0, A.add, A.min); scan(V("we", 0, 192), V("big", 0, 192), V("cumb", 1, 193), 0.0, A.add, A.min)
@@ -472,20 +487,21 @@ def program():
         cp(V("CL", 0, 24), V("wr", 15, 384, 16)); CL = V("CL", 0, 24)
         tt(V("num", 2, 194), V(P0, 0, 192), V("cumb", 0, 192), A.add)
         tt(a384("oh"), IND("num", 0, 194, CL), a384("im"), A.is_equal)
-        for e in range(2): tt(V("pr", 384 * e, 384 * e + 384), IND("Nw", 192 * e, 192 * e + 194, CL), a384("oh"), A.mult)
-        o = V(P1, 512, 560)
-        mm([(o, Z("all", i), V("pr", i, 768, 16)) for i in range(16)])
+        for e in range(2):
+            tt(V("pr", 384 * e, 384 * e + 384), IND("Nw", 192 * e, 192 * e + 194, CL), a384("oh"), A.mult)
+            mm([(V(P1, 512 * e, 512 * e + 24), Z("all", i), V("pr", 384 * e + i, 384 * e + 384, 16)) for i in range(16)])
         cp(V("j1", 0, 24), V("wr", 15, 384, 16)); ts(V("j1", 24, 48), V("j1", 0, 24), 510, None, A.bitwise_and)
-        for e in range(2): ts(V("s3", 24 * e, 24 * e + 24), V("j1", 24, 48), 4, -8, A.mult, A.add)
-        ts(V("j2", 0, 48), o, 0.125, 7.625, A.mult, A.add); ts(V("s3", 48, 96), o, -0.5, 800, A.is_ge, A.mult)
-        tt(V("s3", 48, 96), V("s3", 48, 96), V("s3", 0, 48), A.add); tt(V("s1", 48, 96), V("s3", 48, 96), V("j2", 0, 48), A.add); cp(V("IL", 0, 48), V("s1", 48, 96))
-        mm(*[[(V(P3, a, b), M("CF"), V("EQ", 1536 + a, 1536 + b)), (V(P3, a, b), M("R0"), V("J8", a, b))] +
-             [(V(P3, a + j, b, 8), M("U%d" % j), V("Rv", a // 8, b // 8)) for j in range(8)] for a, b in sq])
+        ts(V("s3", 0, 24), V("j1", 24, 48), 4, -8, A.mult, A.add); ts(V("s3", 24, 48), V("pk", 128, 152), V("cumb", 192, 193), 800, A.is_gt, A.mult)
+        tt(V("s3", 48, 72), V("s3", 0, 24), V("s3", 24, 48), A.add)
+        mm(*[[(V(P3, a, b), M("R0"), V("J8", a, b))] + [(V(P3, a + j, b, 8), M("U%d" % j), V("Rv", a // 8, b // 8)) for j in range(8)] for a, b in sq], final=False)
+        mm(*[[(V(P3, a, b), M("CF"), V("EQ", 1536 + a, 1536 + b))] for a, b in sq], first=False)
         cp(V("W2", 0, 768), V(P3, 0, 768), "av")
         for e in range(2):
+            w = (24 * e, 24 * e + 24)
+            ts(V("j2", *w), V(P1, 512 * e, 512 * e + 24), 0.125, 7.625, A.mult, A.add); tt(V("s1", 48 + w[0], 48 + w[1]), V("s3", 48, 72), V("j2", *w), A.add); cp(V("IL", *w), V("s1", 48 + w[0], 48 + w[1]))
             ge = V("G2", 384 * e, 384 * e + 384); pe = V(P0, 512 * e, 512 * e + 384)
-            cp(ge, IND("W2", 0, 1600, V("IL", 24 * e, 24 * e + 24)), "av")
-            mm([(pe, Z("lo", 0), ge), (pe, M("NLo"), V("pr", 384 * e, 384 * e + 384))])
+            cp(ge, IND("W2", 0, 1600, V("IL", *w)), "av")
+            mm([(pe, M("NLo"), V("pr", 384 * e, 384 * e + 384))], final=False); mm([(pe, Z("lo", 0), ge)], first=False)
             eq(V("e2", 384 * e, 384 * e + 384), pe, 0, 0.0)
         o = V(P1, 0, 48)
         mm([(o, Z("u", i), V("G2", i, 768, 16)) for i in range(16)], final=False); mm([(o, Z("s", i), V("e2", i, 768, 16)) for i in range(16)], first=False)
@@ -495,54 +511,71 @@ def program():
         ts(V("j3", 0, 48), o, 0.125, -0.4375, A.mult, A.add)
         nl = Et // 16
         cp(V("LA", nl, nl + 24), V("j3", 0, 24)); cp(V("LB", nl, nl + 24), V("j3", 24, 48))
-        for n_, (kb_, zz, o, a, b) in enumerate([("Kn", "A", 32, a, b) for a, b in FOLD[0]] + [("Ke", "B", 832, a, b) for a, b in FOLD[1]]):
-            po = V((P0, P1)[n_ // 2 % 2], n_ % 2 * 512, n_ % 2 * 512 + b - a)
+        def fold(u, a, b, Pn, c):
+            kb_, zz, o = (("Kn", "A", 32), ("Ke", "B", 832))[u]; po = V(Pn, c, c + b - a)
             mm([(po, M("I"), V(kb_, a, b))], final=False); mm([(po, Z(zz, s), V("Aux", 768 + 8 * a + s, 768 + 8 * b, 8)) for s in range(8)], first=False)
             cp(V("RR", o + a, o + b), po, "av")
+        for x in FOLD[:5]: fold(*x)
+        inner = lambda fold=fold: [fold(*x) for x in FOLD[5:]]
+        if last: inner()
         done = 0
         for a in range(0, Et, 384):
             b = a + 384; z = a % 1536; zb, mk, rr = V("zb", z, z + 384), V("mk", z, z + 384), V("rl", a, b); xs = V("xw", 32 + a, 32 + b)
-            neg(V("ga", a, b), IND("Aw", 0, 800, V("LA", a // 16, b // 16)))
-            o = V(P2 if ACC[t] or a // 768 % 2 == 0 else P3, a // 384 % 2 * 512, a // 384 % 2 * 512 + 384)
+            scl(V("ga", a, b), IND("Aw", 0, 800, V("LA", a // 16, b // 16)))
+            o = V(P2 if not last or a // 768 % 2 == 0 else P3, a // 384 % 2 * 512, a // 384 % 2 * 512 + 384)
             if a // 384 < DV[t]:
-                gb = V("gb", a, b); cp(gb, IND("Bw", 0, 800, V("LB", a // 16, b // 16)), "av")
-                dma("g", [lambda T, a=a, b=b: (S(T, "gb", a, b), S(T, "ga", a, b), dict(accum_op=A.add))], [gb, V("ga", a, b)], [gb], 3000.0)
+                gb = V("gb", a, b); cp(gb, IND("Bw", 0, 800, V("LB", a // 16, b // 16)), "av"); plus_dma(gb, V("ga", a, b))
                 act(zb, gb, F.Abs); mm([(o, M("nI"), xs), (o, M("nI"), zb)])
             else:
                 tt(zb, IND("Bw", 0, 800, V("LB", a // 16, b // 16)), V("ga", a, b), A.add)
-                relu(mk, zb); mm([(o, M("nI"), xs), (o, M("I"), zb), (o, M("D2"), mk)])
+                if a // 384 < ABS[t]: act(mk, zb, F.Abs); mm([(o, M("nI"), xs), (o, M("nI"), mk)])
+                else: relu(mk, zb); mm([(o, M("nI"), xs), (o, M("I"), zb), (o, M("D2"), mk)])
             relu(rr, o); pos_(V("ix", a, b), rr)
-            if not ACC[t]:
+            if a >= 384 * ACC[t]:
                 mm([(o, M("I"), xs), (o, M("I"), rr)]); cp(xs, o, "av")
-            elif b % 768 == 0 or b == Et:
-                dma("g", [lambda T, c=done, b=b: (S(T, "xw", 32 + c, 32 + b), S(T, "rl", c, b), dict(accum_op=A.add))], [V("rl", done, b), V("xw", 32 + done, 32 + b)], [V("xw", 32 + done, 32 + b)], 3000.0)
-                done = b
-        neg(V("ga", Et, Et + 384), IND("Aw", 0, 800, V("LA", nl, nl + 24)))
+            elif b % 768 == 0 or b == 384 * ACC[t]:
+                plus_dma(V("xw", 32 + done, 32 + b), V("rl", done, b)); done = b
+        scl(V("ga", Et, Et + 384), IND("Aw", 0, 800, V("LA", nl, nl + 24)))
         tt(a384("zn"), IND("Bw", 0, 800, V("LB", nl, nl + 24)), V("ga", Et, Et + 384), A.add)
         ts(V("xw", 32 + Et, 416 + Et), a384("zn"), -1, -255, A.mult, A.max)
-        ts(V("ix", Et, Et + 384), V("xw", 32 + Et, 416 + Et), -0.5, None, A.is_lt)
+        pos_(V("ix", Et, Et + 384), a384("zn"))
         dma("s", [lambda T: (S(T, "own", 0, 168), S(T, "ga", 0, 2688, slice(0, 128, 16)))], [V("ga", 0, 2688)], [V("own", 0, 168)])
-        wp = V(P0, 0, 384)
-        mm(wrap(wp, "RR", 32, 800))
-        if not last: cp(V("W", 0, 384), wp)
-        mm(*[wrap(V(P1, 48 * s, 48 * s + 48), "RR", 832 + 672 * s, 928 + 672 * s) for s in range(2)])
-        cp(V("Eb", 0, 96), V(P1, 0, 96)); act(V("Ebf", 0, 96), V(P1, 0, 96), F.Identity, pc("p768"))
-        for s in range(2):
-            m0 = 432 * (2 * t + s)
-            cp(V("snd", m0 + 384, m0 + 432), V(P0, 336 * s, 48 + 336 * s)); cp(V("nbs", 48 * s, 48 * s + 48), V(P0, 336 * s, 48 + 336 * s), "a")
-            parts(neg, SPL[0], V("Go", 768 * s, 768 * s + 768), IND("xw", 0, 2720, V("Eb", 48 * s, 48 * s + 48)), "av")
-            o = V(P3, 512 * s, 512 * s + 384)
-            mm([(o, M("I256"), V("Go", 768 * s, 768 * s + 384)), (o, M("I"), V("Go", 768 * s + 384, 768 * s + 768))])
-            cp(V("snd", m0, m0 + 384), o)
-        for k, a, b, lat in ((3 + t, 384, 432, 3000.0), (t, 0, 384, 5000.0)):
-            add("g", (k, t, a, b), [V("snd", 864 * t + 432 * s + a, 864 * t + 432 * s + b) for s in range(2)], [V("net", k, k + 1)], 1500.0 if k != 3 else 3000.0, kind="send")
-            add("r", (k, t, a, b), [V("net", k, k + 1)], [V("lnd", 864 * t + 432 * s + a, 864 * t + 432 * s + b) for s in range(2)], 0.0, kind="recv", lat=lat)
-        if last:
-            for a, b in ((32, 1376), (1376, 2720)): act(V("xw", a, b), V("xw", a, b), F.Abs)
-        tt(V("can", 0, 96), V("nbs", 0, 96), V("slf", 0, 96), A.is_gt); tt(V("can", 0, 96), V("can", 0, 96), V("Ebf", 0, 96), A.mult)
-        tt(V("can", 0, 96), V("can", 0, 96), V("dum", 0, 96), A.max); cp(V("SS", 0, 96), V("can", 0, 96))
-        ts(V("thr", 48, 96), V("nbs", 48, 96), 704, 1e6, A.is_lt, A.mult)
-        o = V(P2, 0, 168)
+        if not last:
+            mm(wrap(V(P0, 0, 384), "RR", 32, 800)); cp(V("W", 0, 384), V(P0, 0, 384))
+        mm(*[wrap(V(P2, 48 * s, 48 * s + 48), "RR", 832 + 672 * s, 928 + 672 * s) for s in range(2)])
+        cp(V("Eb", 0, 96), V(P2, 0, 96))
+
+        def send(k, dr, src, dst, lat):
+            add("g", (k, dr, src, dst), [src], [V("net", k, k + 1)], SEND if k else 2 * SEND, kind="send")
+            add("r", (k, dr, src, dst), [V("net", k, k + 1)], [dst], 0.0, kind="recv", lat=lat)
+
+        def spare(o, valid, name, base, u):
+            a, b = V("s4", 48 * u, 48 * u + 24), V("s4", 48 * u + 24, 48 * u + 48)
+            ts(a, valid, 0.5, base, A.is_gt, A.mult); tt(b, name, a, A.add); tt(a, b, V("pos", 0, 24), A.max); cp(o, a)
+        o = V(P3, 0, 96)
+        mm([(o, Z("W", 0), V("RR", 1504, 1600)), (o, Z("W", 8), V("RR", 704, 800))])
+        tt(V("fl", 0, 96), o, V("slf", 0, 96), A.is_gt); plus(V("CT", 16, 112), o, pc("cb"))
+        mm([(V(P3, 512, 608), M("Blk"), V("fl", 0, 96))]); mm([(o, M("TR8"), V("fl", 0, 96))])
+        scan(V("cs", 1, 97), V(P3, 512, 608), V("Zr", 0, 96), 500.0, A.add, A.max)
+        tt(V("PT", 16, 112), o, V("cs", 0, 96), A.add)
+        scan(V("w5", 0, 96), V("big", 0, 96), V("cs", 0, 96), 0.0, A.add, A.min); scan(V("w5", 96, 192), V("big", 0, 96), V("cs", 1, 97), 0.0, A.add, A.min)
+        tt(V("s5", 0, 6), V("w5", 111, 192, 16), V("w5", 15, 96, 16), A.is_gt); tt(V("s5", 8, 14), V("s5", 0, 6), V("w5", 15, 96, 16), A.mult)
+        tt(V("s5", 16, 22), V("s5", 8, 14), V("pk", 120, 126), A.max); ts(V("ZS", 0, 6), V("s5", 16, 22), -404, None, A.add)
+        cp(IND("Zs", 480 * t, 480 * t + 480, V("ZS", 0, 6)), V("id16", 0, 96))
+        zr = V("Zs", 480 * t + 96, 480 * t + 480)
+        scan(a384("mx2"), zr, zr, 0.0, A.max, A.max); scan(a384("wr2"), a384("big"), a384("mx2"), 0.0, A.add, A.min)
+        ka, kf = V("sk", 48 * t, 48 * t + 24), V("sk", 48 * t + 24, 48 * t + 48)
+        cp(ka, V("wr2", 15, 384, 16))
+        tt(a384("oh2"), IND("PT", 0, 112, ka), a384("im"), A.is_equal); tt(a384("cx"), IND("CT", 0, 112, ka), a384("oh2"), A.mult)
+        pn_, pf_ = V(P3, 0, 24), V(P3, 512, 536)
+        mm([(pf_, Z("uh", i), V("cx", i, 384, 16)) for i in range(16)]); mm([(pn_, Z("lh", i), V("cx", i, 384, 16)) for i in range(16)])
+        cp(kf, pf_); ts(V("E2", 0, 24), pn_, 1360, None, A.add); spare(V("SS", 0, 24), kf, pn_, 2128, 0)
+        send(4 * t, 1, V("sk", 48 * t, 48 * t + 48), V("lk", 48 * t, 48 * t + 48), LAT[0])
+        cp(V("sy", 384 * t, 384 * t + 384), IND("xw", 0, 2720, V("E2", 0, 24)), "av")
+        send(4 * t + 1, 1, V("sy", 384 * t, 384 * t + 384), V("ly", 384 * t, 384 * t + 384), LAT[1])
+        cp(IND("PN", 0, 3488, V("SS", 0, 24)), V("RR", 1632, 2016)); parts(cp, SPL[0], V("Go", 768, 1536), IND("PN", 768, 3488, V("Eb", 48, 96)), "av")
+        o = V(P3, 0, 48); mm([(o, Z("a0", i), V("Go", 768 + i, 1536, 16)) for i in range(16)]); cp(V("PL", 0, 48), o)
+        o = V(*MIDB)
         mm([(o, Z("all", i), V("ix", 168 * i, 168 * i + 168)) for i in range(16) if 168 * i < Et + 384])
         act(V("m3", 0, 168), V("own", 0, 168), F.Identity, pc("md%d" % t), -1.0 / 4096)
         ts(o, o, 8.5, None, A.is_ge); tt(V("m2", 0, 168), o, V("m3", 0, 168), A.mult); tt(V("mid", 0, 168), V("mid", 0, 168), V("m2", 0, 168), A.max)
@@ -551,54 +584,53 @@ def program():
             ts(V("m3", 0, 168), V("m1", 0, 168), -32, None, A.add)
             dma("s", [lambda T: (T.ymid[:, :], S(T, "m3", 0, 168))], [V("m3", 0, 168)], [V("out", 0, 1)])
 
-        def rows_out(Pn, a, b, pa):
+        def rows_out(Pn, a, b, pa, more=()):
             o = V(Pn, pa, pa + b - a)
             mm([(o, V("ZO", 64, 192), V("RR", 32 + a, 32 + b)), (o, V("ZO", 0, 128), V("RR", 832 + a, 832 + b))])
             ts(V("O", a, b), o, -32, -1, A.add, A.max)
         if last: rows_out(P0, 96, 384, 0); rows_out(P0, 384, 672, 512)
-        l0 = 864 * t
-        ts(V("par", 0, 48), V("lnd", l0 + 384, l0 + 432), 703, -8, A.subtract, A.max); ts(V("par", 48, 96), V("lnd", l0 + 816, l0 + 864), 31, None, A.subtract)
+        la = V("lk", 48 * t, 48 * t + 24); yr = V("ly", 384 * t, 384 * t + 384); mn = V("s3m", 416 * t, 416 * t + 384); o = V(P2, 512, 896)
+        cp(V("bb", 0, 24), V("lk", 48 * t + 24, 48 * t + 48)); cp(a384("Gn"), IND("RR", 16, 128, la), "av")
+        mm([(V(P2, 512 + i, 896, 16), V("BR", 128 * i, 128 * i + 128), V("bb", 0, 24)) for i in range(16)], final=False); mm([(o, M("NWk"), a384("Gn"))], first=False)
+        eq(a384("ohc"), o, -4096.0 * 31, pc("c31")); tt(a384("nm"), IND("RR", 816, 928, la), a384("ohc"), A.mult)
+        o = V(P2, 512, 536)
+        mm([(o, Z("aw", i), V("nm", i, 384, 16)) for i in range(16)])
+        ts(V("E2", 24, 48), o, 16, None, A.max); spare(V("SS", 24, 48), o, o, 768, 1)
+        tt(a384("dd"), IND("xw", 0, 2720, V("E2", 24, 48)), yr, A.subtract)
+        ts(a384("pp"), a384("dd"), 0.5, None, A.is_gt); relu(a384("rs"), a384("dd")); ts(a384("pn"), a384("dd"), -0.5, None, A.is_lt)
+        o = V(P3, 512, 536); mm([(o, Z("all", i), V("pp", i, 384, 16)) for i in range(16)]); ts(V("s3m", 416 * t + 384, 416 * t + 408), o, 8.5, None, A.is_ge)
+        send(4 * t + 2, -1, V("s3m", 416 * t + 384, 416 * t + 408), V("l3m", 416 * t + 384, 416 * t + 408), LAT[0])
+        o = V(P3, 0, 384); mm([(o, M("I"), yr)], final=False); mm([(o, M("I"), a384("rs"))], first=False); cp(mn, o, "av")
+        send(4 * t + 3, -1, mn, V("l3m", 416 * t, 416 * t + 384), LAT[1])
+        o = V(P3, 512, 896); mm([(o, M("Blk"), a384("pn"))]); act(V("sn", 0, 384), o, F.Sign, pc("p85"), -1.0)
         for s in range(2):
-            c0 = 512 * s
-            mm(*[[(V(P3, c0 + 96 * m_, c0 + 96 * m_ + 96), M("Wc"), V("RR", 32 + 672 * s, 128 + 672 * s))] +
-                 [(V(P3, c0 + 96 * m_ + z, c0 + 96 * m_ + 96, 2), M("R%d%d" % (m_, z)), V("par", 48 * s, 48 * s + 48)) for z in range(2)] for m_ in range(4)])
-            eq(V("eqs", 384 * s, 384 * s + 384), V(P3, c0, c0 + 384), 31 + 672 * s, pc("ns%d" % s))
-        mm(*[[(V(P3, 48 * s, 48 * s + 48), Z("sp%d" % m_, 8 * z), V("eqs", 384 * s + 96 * m_ + z, 384 * s + 96 * m_ + 96, 2)) for m_ in range(4) for z in range(2)] for s in range(2)])
-        tt(V("q1", 0, 96), V(P3, 0, 96), V("thr", 0, 96), A.is_gt); tt(V("can", 0, 96), V(P3, 0, 96), V("pc8", 0, 96), A.add)
-        tt(V("can", 0, 96), V("can", 0, 96), V("q1", 0, 96), A.mult); cp(V("PL", 0, 96), V("can", 0, 96))
-        for s in range(2):
-            cp(V("i1", 432 * s, 432 * s + 384), V("lnd", l0 + 432 * s, l0 + 432 * s + 384))
-            ts(V("Pw", 16 + 768 * s, 400 + 768 * s), V("i1", 432 * s, 432 * s + 384), 8, None, A.arith_shift_right)
-            ts(V("Pw", 400 + 768 * s, 784 + 768 * s), V("i1", 432 * s, 432 * s + 384), 255, None, A.bitwise_and)
-        for s in range(2):
-            sv = lambda n: V(n, 768 * s, 768 * s + 768)
-            pw = IND("Pw", 0, 784 + 768 * s, V("PL", 48 * s, 48 * s + 48)); xs = IND("xz", 0, 3488, V("SS", 48 * s, 48 * s + 48))
-            parts(tt, SPL[0], sv("mn"), pw, sv("Go"), A.min)
-            for u in range(2):
-                o = V(P3, 512 * u, 512 * u + 384); w = (768 * s + 384 * u, 768 * s + 384 * u + 384)
-                mm([(o, M("I"), V("Go", *w)), (o, M("nI"), V("mn", *w))]); pos_(V("si", *w), o)
-            if last: parts(cp, SPL[1], xs, sv("mn"))
-            o = V(P3, 0, 96)
-            mm([(o, Z("2", k), V("si", 768 * s + k, 768 * s + 768, 8)) for k in range(8)])
-            ks = V("ks", 96 * s, 96 * s + 96); ts(ks, o, 8.5, None, A.is_lt)
-
-            def drop(s=s, ks=ks):
-                for b in (32, 832): tt(V("RR", b + 672 * s, b + 96 + 672 * s), V("RR", b + 672 * s, b + 96 + 672 * s), ks, A.mult)
-            if last:
-                drop(); rows_out(P0, 672 * s, 672 * s + 96, 512 * s)
+            if s:
+                o = V(P3, 0, 384); mn = V("l3m", 416 * t, 416 * t + 384)
+                mm([(V(P3, i, 384, 16), V("BR", 128 * i, 128 * i + 128), V("l3m", 416 * t + 384, 416 * t + 408)) for i in range(16)])
+                cp(V("FR", 32, 416), o, "av"); parts(cp, SPL[0], V("Go", 768, 1536), IND("FR", 0, 416, V("PL", 0, 48)), "av")
+                if last: tt(IND("G1", 0, 3488, V("SS", 0, 24)), mn, a384("cm1"), A.mult)
+                else: act(V("sn", 384, 768), o, F.Sign, pc("p85"), -1.0); tt(IND("xz", 0, 3488, V("SS", 0, 24)), mn, V("sn", 384, 768), A.mult)
             else:
-                late[0].append(drop)
-                late[1].append(lambda xs=xs, a=sv("mn"), b=sv("sn"): parts(tt, SPL[1], xs, a, b, A.mult))
-        if not last:
-            for u in range(4):
-                o = V(P3, 512 * (u % 2), 512 * (u % 2) + 384); w = (384 * u, 384 * u + 384)
-                mm([(o, M("Blk"), V("si", *w))]); act(V("sn", *w), o, F.Sign, pc("m85"))
+                tt(IND("xz", 0, 3488, V("SS", 24, 48)), mn, V("sn", 0, 384), A.mult)
+                parts(relu, SPL[0], V("Go", 0, 768), IND("xw", 0, 2720, V("Eb", 0, 48)))
+                if last:
+                    for a in range(0, 2688, 672): act(V("G1", 800 + a, 1472 + a), V("xw", 32 + a, 704 + a), F.Abs)
+
+
+        def drop(s, u, Pn, c):
+            o = V(Pn, c, c + 96); b = 32 + 800 * u + 672 * s
+            mm([(o, M("I"), V("RR", b, b + 96))] + [(o, Z("2", k), V("Go", 768 * s + k, 768 * s + 768, 8)) for k in range(8)]); relu(V("RR", b, b + 96), o)
         if last:
-            dma("s", [lambda T: (T.ylen[:, :], S(T, "xw", 32, 2720))], [V("xw", 32, 2720)], [V("out", 1, 2)], 4000.0)
+            for s in range(2):
+                drop(s, 0, P1, 0); drop(s, 1, P1, 512); rows_out(P0, 672 * s, 672 * s + 96, 512 * s)
+        else:
+            late.append(lambda drop=drop: [drop(*x) for x in ((0, 0, P3, 512), (0, 1, P3, 512), (1, 0, P3, 512), (1, 1, P3, 0))])
+        if last:
+            dma("s", [lambda T: (T.ylen[:, :], S(T, "G1", 800, 3488))], [V("G1", 800, 3488)], [V("out", 1, 2)], 4000.0)
             dma("a", [lambda T: (T.ynb[:, :], S(T, "O", 0, 768, slice(0, 64))), lambda T: (T.yen[:, :], S(T, "O", 0, 768, slice(64, 128)))], [V("O", 0, 768)], [V("out", 2, 3)], 3000.0)
     pre = len(ops)
-    mset(pc("m85"), -8.5); iota(pc("m4"), [[-4, 9]])
-    for n_, c_ in (("ten", 10), ("m1k", -1024), ("p768", 768), ("one", 1), ("ns0", -31), ("ns1", -703), ("m1", -1),
+    mset(pc("p85"), 8.5)
+    for n_, c_ in (("ten", 10), ("m1k", -1024), ("c31", 4096 * 31), ("one", 1), ("m1", -1),
                    ("md0", 12582912 + 1024), ("md1", 12582912 + 2048), ("md2", 12582912 + 3072)): iota(pc(n_), [[0, 1]], c_)
     return ops[pre:] + ops[:pre]
 
@@ -636,53 +668,77 @@ def plan():
     succ = [[] for _ in ops]
     for i, o in enumerate(ops):
         for j in o["dep"]: succ[j].append(i)
-    SY = 110.0
     pred = [list(o["dep"]) for o in ops]
+    lat = [o["lat"] for o in ops]
+    how = [[(e, o.get("ca", o["cost"]) if e == "a" else o["cost"]) for e in o["engs"]] for o in ops]
 
     def place(pri, before, after, fixed, bias):
-        busy = {e: [] for e in "vapgsr"}; t0 = [0.0] * n; fin = [0.0] * n; eng = [""] * n
-        left = [len(x) for x in before]; ready = [i for i in range(n) if not left[i]]
+        busy = {e: [] for e in "vapgsr"}; t0 = [0.0] * n; fin = [0.0] * n; eng = [None] * n; why = [-1] * n; rdy = [0.0] * n
+        left = [len(x) for x in before]; ready = [i for i in range(n) if not left[i]]; back = before is succ
         while ready:
-            i = max(ready, key=lambda k: pri[k]); ready.remove(i); o = ops[i]
-            rt = max([fin[j] + SY for j in before[i]] + [0.0]); best = None
-            pre_, post = (0.0, o["lat"]) if before is pred else (o["lat"], 0.0)
-            for e in (fixed[i] if fixed else o["engs"]):
-                s = rt + pre_; c = o.get("ca", o["cost"]) if e == "a" else o["cost"]
-                bz = busy[e]; at_ = len(bz)
+            i = max(ready, key=lambda k: pri[k]); ready.remove(i)
+            rt = rdy[i] + lat[i] if back else rdy[i]; best = None
+            for ec in ([fixed[i]] if fixed else how[i]):
+                s = rt; c = ec[1]; bz = busy[ec[0]]; at_ = m = len(bz); by = -1
                 while at_ and bz[at_ - 1][1] > s: at_ -= 1
-                while at_ < len(bz) and s + c > bz[at_][0]:
-                    s = max(s, bz[at_][1]); at_ += 1
-                key = s + c + (bias[i] if e == "v" else 0.0)
-                if best is None or key < best[0]: best = (key, s, e, at_, c)
-            _, s, e, at_, c = best
-            busy[e].insert(at_, (s, s + c)); t0[i] = s; fin[i] = s + c + post; eng[i] = e
+                while at_ < m and s + c > bz[at_][0]:
+                    if bz[at_][1] > s: s = bz[at_][1]; by = bz[at_][2]
+                    at_ += 1
+                key = s + c + bias[i] if ec[0] == "v" else s + c
+                if best is None or key < best[0]: best = (key, s, ec, at_, by)
+            _, s, ec, at_, by = best
+            busy[ec[0]].insert(at_, (s, s + ec[1], i)); t0[i] = s; f = fin[i] = s + ec[1] if back else s + ec[1] + lat[i]; eng[i] = ec
+            if by >= 0: why[i] = -2 - by
+            f += SY
             for j in after[i]:
                 left[j] -= 1
+                if f > rdy[j]: rdy[j] = f; why[j] = i
                 if not left[j]: ready.append(j)
-        return t0, fin, eng
+        return max(fin), t0, eng, pri, bias, fin, why
     pri = [0.0] * n
     for i in range(n - 1, -1, -1):
-        pri[i] = ops[i]["cost"] + ops[i]["lat"] + SY + max([pri[j] for j in succ[i]] + [0.0])
+        pri[i] = ops[i]["cost"] + lat[i] + SY + max([pri[j] for j in succ[i]] + [0.0])
+    def lift(p, x, up, t0, since):
+        todo = [x]; got = {x}
+        while todo:
+            j = todo.pop(); p[j] += up
+            for k in pred[j]:
+                if k not in got and t0[k] > since: got.add(k); todo.append(k)
     top = None; zero = [0.0] * n
-    for bias, seed in BIASES:
-        rs = np.random.RandomState(seed); p = [x + float(y) for x, y in zip(pri, rs.uniform(0, JIT if seed else 0.0, n))]
-        bias = [bias if o["wr"][0][0] in CHAIN else FAR for o in ops]
+    for bias in BIASES:
+        p = pri
         for _ in range(PASSES):
-            t0, fin, eng = place(p, pred, succ, None, bias)
-            if top is None or max(fin) < top[0]: top = (max(fin), t0, eng, p, bias)
-            _, p, _ = place(fin, succ, pred, eng, zero)
+            cur = place(p, pred, succ, None, [bias] * n)
+            for name, nth, up, span_ in EARLY:
+                p = list(cur[3]); x = [i for i, o in enumerate(ops) if o["wr"][0][0] == name][nth]; lift(p, x, up, cur[1], cur[1][x] - span_)
+                new = place(p, pred, succ, None, [bias] * n)
+                if new[0] < cur[0] + 1000.0: cur = new
+            if top is None or cur[0] < top[0]: top = cur
+            p = place(cur[5], succ, pred, cur[2], zero)[5]
     rs = np.random.RandomState(SEED); cur = top
-    for _ in range(TRIES):
-        c0 = rs.uniform(0, cur[0]); w = rs.uniform(3000, 30000); amp = rs.choice([300.0, 1000.0, 3000.0]); z = rs.uniform(-amp, amp, n); u = rs.uniform(0, 1, n)
-        near = [abs(x - c0) < w for x in cur[1]]
-        p = [x + float(y) if m and k < 0.3 else x for x, y, m, k in zip(cur[3], z, near, u)]
-        bias = [float(rs.choice([0.0, 700.0, 5000.0])) if m and k > 0.9 else x for x, m, k in zip(cur[4], near, u)]
-        t0, fin, eng = place(p, pred, succ, None, bias)
-        if rs.uniform() < 0.3:
-            _, p, _ = place(fin, succ, pred, eng, zero); t0, fin, eng = place(p, pred, succ, None, bias)
-        if max(fin) <= cur[0] + 200.0: cur = (max(fin), t0, eng, p, bias)
+    for it in range(TRIES):
+        i = max(range(n), key=lambda k: cur[5][k]); held = []
+        while i != -1:
+            j = cur[6][i]
+            if j < -1: j = -2 - j; held.append((j, i))
+            i = j
+        p = list(cur[3]); bias = list(cur[4])
+        if held and rs.uniform() < LIFT:
+            x = held[rs.randint(len(held))][rs.randint(2)]; lift(p, x, rs.uniform(500, 8000), cur[1], cur[1][x] - rs.uniform(3000, 30000))
+        elif held and rs.uniform() < MOVE:
+            for _ in range(rs.randint(1, 4)):
+                x, y = held[rs.randint(len(held))]
+                if len(how[x]) > 1 and rs.uniform() < 0.5: bias[x] = 1e5 if cur[2][x][0] == "v" else -1e5
+                elif len(how[y]) > 1 and rs.uniform() < 0.3: bias[y] = 1e5 if cur[2][y][0] == "v" else -1e5
+                else: p[x] = min(p[x], p[y]) - rs.uniform(0, 3000)
+        else:
+            c0 = rs.uniform(0, cur[0]); w = rs.uniform(2000, 15000); z = rs.uniform(-1, 1, n) * rs.choice([300.0, 1000.0, 3000.0]) * (rs.uniform(0, 1, n) < 0.3)
+            p = [x + float(y) if abs(t - c0) < w else x for x, y, t in zip(p, z, cur[1])]
+        new = place(p, pred, succ, None, bias)
+        if rs.uniform() < 0.1: new = place(place(new[5], succ, pred, new[2], zero)[5], pred, succ, None, bias)
+        if new[0] <= cur[0] + HEAT * (1 - it / TRIES) * rs.exponential(): cur = new
         if cur[0] < top[0]: top = cur
-    for i, o in enumerate(ops): o["t0"] = top[1][i]; o["e"] = top[2][i]; o["pri"] = pri[i]
+    for i, o in enumerate(ops): o["t0"] = top[1][i]; o["e"] = top[2][i][0]; o["pri"] = pri[i]
     return ops, sorted(range(n), key=lambda i: (top[1][i], i)), top[0]
 
 
@@ -720,7 +776,7 @@ def rank_program(g, core, T, topo):
     for i in order:
         o = ops[i]; e = o["e"]
         if o["kind"] == "recv":
-            token[i] = (T.sem["r%d" % o["fn"][0]], sum(len(topo.engines(T.cores[(rank + z) % n], core)) // 2 for z in (-1, 1))); continue
+            token[i] = (T.sem["r%d" % o["fn"][0]], len(topo.engines(T.cores[(rank - o["fn"][1]) % n], core))); continue
         q = Q[e]
         for j in waits[i]: q.wait_ge(*token[j])
         if o["kind"] == "c":
@@ -734,12 +790,7 @@ def rank_program(g, core, T, topo):
             token[i] = (sem, 16 * len(o["fn"]))
             if i not in need: tail.append(token[i])
         else:
-            m = o["fn"][0]; trs = []; used = 0
-            for s, (dr, src, dst) in enumerate(transfers(o)):
-                d = T.cores[(rank + dr) % n]; rid, pid = topo.addr(d, core); en = topo.engines(core, d)
-                k = len(en) // 2; mask = sum(1 << x for x in en[k * s:k * s + k])
-                trs.append(RemoteDMATransfer(dst_ids=[DstId(rid=rid, pnc=pid)], dma_engine_mask=mask, remote_sem=T.sem["r%d" % m], src=ap(src), dst=ap(dst)))
-                used += k
-            g.remote_dma_fused(trs, local_sem=T.sem["l%d" % m])
-            tail.append((T.sem["l%d" % m], used))
+            m, dr, src, dst = o["fn"]; d = T.cores[(rank + dr) % n]; rid, pid = topo.addr(d, core)
+            g.remote_dma(ap(dst), ap(src), T.sem["r%d" % m], T.sem["l%d" % m], pid, rid, topo.mask(core, d))
+            tail.append((T.sem["l%d" % m], len(topo.engines(core, d))))
     for tk in tail: g.wait_ge(*tk)

@@ -4,17 +4,17 @@ from concourse.mybir import AluOpType as A, ActivationFunctionType as F
 F32, BF, I32, U16, H16 = "float32", "bfloat16", "int32", "uint16", "float16"
 SB = dict(
     xz=(3488, BF), xw=(2720, BF), Lu=(1536, BF), RR=(2400, BF), Rs=(768, I32), NW=(768, I32), i2=(192, I32),
-    EO=(384, U16), EW=(3840, F32), LA=(168, U16), LB=(168, U16), W=(384, U16), SL=(48, U16), XL=(112, U16),
+    EO=(384, U16), EW=(3840, F32), LA=(168, U16), LB=(168, U16), W=(384, U16), SL=(48, U16), XL=(16, U16),
     lo8=(800, BF), hi8=(800, BF), c8=(384, BF), cn=(36, H16), NM=(1152, BF), b1=(800, BF), b2=(800, BF), b3=(800, BF),
-    PC=(128, F32), PI=(64, I32), CMx=(144, BF), CH=(128, BF), CO=(192, F32), MZ=(144 * 20, BF), M=(128 * 54, BF), BR=(2048, BF), ZO=(192, BF),
+    PC=(128, F32), PI=(64, I32), CMx=(144, BF), CH=(128, BF), CO=(192, F32), MZ=(144 * 20, BF), M=(128 * 40, BF), MX=(2048, BF), PX=(256, BF), BR=(2048, BF), ZO=(192, BF),
     PAT=(240, BF), cod=(64, BF), pu=(192, BF), jk=(64, I32), SEL=(16, BF), SW=(272, H16), CX=(96, BF),
     fil=(576, BF), GD=(800, BF), G1=(6144, BF), KS=(192, F32), OWN=(192, F32), KI=(96, I32), XI=(96, I32), AI=(144, I32), e1=(48, F32), XR=(384, BF), OH=(3456, BF),
     AE=(96, H16), AO=(96, U16), ch=(36, BF), cc=(40, F32), rkw=(40, F32), cw=(36, BF), TG=(800, F32), ctr=(576 * 3, BF), tg=(768, F32), gb=(1536, F32), clr=(768, BF),
-    junk=(288, BF), junk2=(96, BF), id0=(96, BF), vc=(16, F32), vd=(16, F32), QL=(6, U16), VL=(12, U16),
+    junk=(288, BF), junk2=(96, BF), id0=(96, BF), vc=(16, F32), vd=(16, F32), vb=(6, BF), QL=(6, U16), VL=(12, U16),
     Rv=(192, BF), fv=(96, BF), UL=(48, U16), s1=(96, F32), s2=(96, F32), s3=(96, F32), pos=(48, F32), pk=(192, F32),
     Lf=(768, F32), Aw=(800, F32), Bw=(800, F32), Kn=(768, BF), Ke=(768, BF),
-    G=(768, BF), EQ=(2304, BF), wish=(192, BF), nf=(96, BF), Nw=(400, BF), fw=(384, BF), ok=(192, BF), cumb=(208, F32), c884=(192, F32),
-    num=(208, F32), big=(384, BF), ws=(192, F32), we=(192, F32), ZL=(12, U16), Z=(1728, BF), ids=(192, BF), mx=(384, BF), wr=(384, BF), CL=(24, U16),
+    G=(768, BF), EQ=(2304, BF), wish=(192, BF), nf=(96, BF), Nw=(400, BF), fw=(384, BF), ok=(192, BF), cumb=(208, F32),
+    num=(208, F32), big=(384, BF), ws=(192, F32), ZL=(12, U16), Z=(2880, BF), ids=(192, BF), mx=(384, BF), wr=(384, BF), CL=(24, U16),
     im=(384, F32), oh=(384, BF), pr=(768, BF), j1=(48, I32), j2=(48, I32), j3=(48, I32), IL=(48, U16), W2=(1600, BF), J8=(768, BF), G2=(768, BF), e2=(768, BF),
     AL=(48, U16), Aux=(6912, BF), gz=(3840, F32), ga=(2688, F32), zb=(1536, BF), mk=(1536, BF), rl=(2304, BF), zn=(384, F32), ix=(2688, BF),
     own=(168, F32), mid=(168, F32), m1=(168, I32), m2=(168, F32), m3=(168, F32),
@@ -43,26 +43,25 @@ def S(T, n, a, b, rows=slice(None)):
 
 
 SPL = [2, 1]
-ACC = [4, 4, 2]
+ACC = [4, 4, 0]
 EARLY = [("EW", 3, 30000.0, 1e6), ("LA", 0, 10000.0, 1e6)] + [(n, k, up, 25000.0) for n, k in (("zb", 0), ("zb", 4), ("zb", 9), ("zb", 3), ("zb", 8), ("zb", 14)) for up in (5000.0, 10000.0)]
-TWO = 0
-BRV = 4
+PIECE = 1200.0
+BRV = 8
 ABS = [0, 3, 3]
-MIDB = ("P2", 512, 680)
+MIDB = ("P2", 0, 168)
 DV = [0, 0, 0]
-FOLD = [(0, 672, 768, "P0", 0), (1, 672, 768, "P0", 512), (0, 0, 384, "P1", 0), (0, 384, 672, "P1", 512), (1, 0, 96, "P0", 512),
-        (1, 96, 384, "P1", 0), (1, 384, 672, "P1", 512)]
+FOLD = [(0, 0, 384, "P1", 0), (0, 384, 768, "P1", 512), (1, 0, 96, "P0", 512), (1, 672, 768, "P0", 512), (1, 96, 384, "P1", 0), (1, 384, 672, "P1", 512)]
 FIRST = [0, 0, 0]
-KEYS = 4
+KEYS = 5
 EWV = 3
-BIASES, PASSES, SEED, TRIES, SY, MOVE, LIFT, HEAT = (300.0, 700.0, 2000.0), 3, 2, 6500, 190.0, 0.5, 0.75, 300.0
+BIASES, PASSES, SEED, TRIES, SY, MOVE, LIFT, HEAT = (300.0, 700.0, 2000.0), 3, 1, 5200, 170.0, 0.5, 0.75, 300.0
 for _k in range(4):
     SCRATCH["P%d" % _k] = ("psum", [128, 1024], F32)
 NDMA = 48
 SEMAPHORES = ["ev", "ea", "ep", "eg", "ax"] + ["d%d" % k for k in range(NDMA)] + [a + str(k) for a in "rl" for k in range(12)]
 SEND, LAT = 1500.0, (3600.0, 5500.0)
 CYC = 1.04
-GAT, SCA, PEC = 1.56, 3.8, 0.6
+GAT, SCA, PEC, WEIGHT = 1.56, 3.8, 0.6, 0.6
 
 
 def V(n, a, b, s=1, rows=None):
@@ -152,7 +151,7 @@ def program():
             if e == "v": return q.tensor_scalar(ap(o), ap(i), ap(c), None, A.is_equal)
             ap("step")(q.activation(ap(o), ap(i), F.Abs, bias=ap(nc)))
             return q.activation(ap(o), ap(o), F.Relu, bias=ap(pc("one")), scale=-1.0)
-        add("av", fn, [i, c, nc, pc("one")], [o], 60 + CYC * wid(o)); ops[-1]["ca"] = 270 + 2 * CYC * wid(o)
+        add("av", fn, [i, c, nc, pc("one")], [o], 60 + CYC * wid(o)); ops[-1]["ca"] = 160 + SY + 2 * CYC * wid(o)
 
     def parts(f, k, *vs):
         def cut(v, j):
@@ -181,14 +180,13 @@ def program():
         select(o, V("Zr", 0, wid(o)), pat, A.not_equal, fill, base, cm)
 
     def mm(*groups, first=True, final=True):
-        def fn(q, e, ap):
-            for gr in groups:
-                for n, (o, l, r) in enumerate(gr):
-                    last = q.matmul(ap(o), ap(l), ap(r), first and n == 0, final and n == len(gr) - 1)
-            return last
-        al = [x for gr in groups for x in gr]
-        add("p", fn, [x[1] for x in al] + [x[2] for x in al], [x[0] for x in al],
-            60 + sum(PEC * max(min(64, wid(l)), wid(o)) * (4 if SB[r[0]][1] == F32 else 1) for o, l, r in al))
+        al = [(o, l, r, first and n == 0, final and n == len(gr) - 1, PEC * max(min(64, wid(l)), wid(o))) for gr in groups for n, (o, l, r) in enumerate(gr)]
+        k = int(sum(x[5] for x in al) // PIECE) + 1
+        for j in range(k):
+            run = al[j * len(al) // k:(j + 1) * len(al) // k]
+            if run:
+                add("p", lambda q, e, ap, run=run: [q.matmul(ap(x[0]), ap(x[1]), ap(x[2]), x[3], x[4]) for x in run][-1],
+                    [x[1] for x in run] + [x[2] for x in run], [x[0] for x in run], (60 if j == 0 else 10) + sum(x[5] for x in run))
 
     def dma(eng, pairs, rd, wr, lat=2200.0):
         add(eng, pairs, rd, wr, (1000.0 if eng == "g" else 60.0) * len(pairs), kind="d", lat=lat)
@@ -209,7 +207,7 @@ def program():
         ps = [(n, c, min(b, c + zw)) for n, a, b in parts for c in range(a, b, zw)]
         dma("s", [(lambda T, n=n, a=a, b=b: (S(T, n, a, b), S(T, z, 0, b - a))) for n, a, b in ps], [V(z, 0, zw)], [V(*p) for p in parts], lat)
     mset(V("Zf", 0, 384), 0); zero("Zf", 384, [("EW", 384, 3456)], 6000.0)
-    mset(V("Zr", 0, 1536), 0); zero("Zr", 1536, [("xw", 1568, 2720), ("Z", 0, 1728), ("Zs", 0, 1440), ("PN", 768, 3488), ("FR", 0, 32), ("ix", 1920, 2688), ("GD", 0, 128), ("GD", 704, 800)], 5000.0)
+    mset(V("Zr", 0, 1536), 0); zero("Zr", 1536, [("xw", 1568, 2720), ("Zs", 0, 1440), ("PN", 768, 3488), ("FR", 0, 32), ("ix", 1920, 2688), ("GD", 0, 128), ("GD", 704, 800)], 5000.0)
     pcn = {}
 
     def pc(n, w=1):
@@ -311,6 +309,7 @@ def program():
     ts(pc("wu"), E(9), 32, E(8), A.mult, A.add); ts(pc("wu"), pc("wu"), 8, None, A.mult)
     tt(pc("wa"), E(8), E(9), A.add); tt(pc("wb"), E(10), E(11), A.add)
     zm("all", 0, 1); zm("Y2", pc("h8"), -4); zm("s", 0, pc("ws")); zm("u", 0, pc("wu")); zm("A", pc("l8"), pc("wa")); zm("B", pc("l8b"), pc("wb"))
+    ts(pc("tc"), pc("wa"), 8, None, A.mult); ts(pc("wc"), E(11), 32, E(10), A.mult, A.add); ts(pc("wc"), pc("wu"), 0.125, pc("wc"), A.mult, A.add); zm("C", pc("tc"), pc("wc"))
     zm("0", 0, E(0)); zm("ir", 0, r); zm("uh", 0, h); zm("lh", 0, nh); zm("aw", 0, wlh); zm("a0", 0, pc("we"))
     zm("2", 8, 1); tt(Z("2"), Z("2"), Z("all"), A.add); scl(Z("2"), Z("2"), -8.0)
     ts(M("t1"), V("CH", 0, 128), -99, None, A.add); tt(M("t2"), M("t1"), M("Blk"), A.mult); ts(V("CH", 0, 128), M("t2"), 99, None, A.add)
@@ -348,11 +347,11 @@ def program():
             tt(V("pu", 0, 64), V("pu", 0, 64), V("pu", 64, 128), A.subtract)
             if z: tt(V("pu", 0, 64), V("pu", 0, 64), dst, A.add)
             tt(dst, V("pu", 0, 64), V("pu", 128, 192), A.add)
-    iota(V("m2", 0, 112), [[16, 14], [0, 8]], -224); iota(V("m3", 0, 112), [[0, 14], [1, 8]]); iota(V("PAT", 224, 240), [[0, 16]])
-    ts(V("m3", 0, 112), V("m3", 0, 112), gr, None, A.is_equal); ts(V("m2", 0, 112), V("m2", 0, 112), r, None, A.add)
-    tt(V("m2", 0, 112), V("m2", 0, 112), V("m3", 0, 112), A.mult); ts(V("XL", 0, 112), V("m2", 0, 112), 224, None, A.add)
-    for n in range(14): M("X%d" % n)
-    for n in range(0, 14, 2): cp(V("M", mn_["X%d" % n], mn_["X%d" % n] + 256), IND("PAT", 0, 240, V("XL", 8 * n, 8 * n + 16)), "av")
+    iota(V("PAT", 224, 240), [[0, 16]]); ts(pc("x16"), pc("r16"), 224, None, A.min); ts(V("XL", 0, 16), V("PI", 8, 24), pc("x16"), None, A.add)
+    cp(V("PX", 0, 256), IND("PAT", 0, 240, V("XL", 0, 16)), "av"); zero("Zr", 1536, [("MX", 0, 2048)], 3000.0)
+    dma("s", [(lambda T, g=g: (S(T, "MX", 256 * g, 256 * g + 256, slice(16 * g, 16 * g + 16)), S(T, "PX", 0, 256, slice(16 * g, 16 * g + 16)))) for g in range(8)],
+        [V("PX", 0, 256)], [V("MX", 0, 2048)])
+    X = lambda n: V("MX", n, 2048, 16)
     TR = M("TR8")
     select(TR, V("Zr", 0, 128), [[-16, 8], [0, 2], [-1, 8]], A.is_ge, 1, -8, 1); select(TR, TR, [[-16, 8], [0, 16]], A.is_ge, 0, -8, 1)
     select(TR, TR, [[16, 8], [0, 2], [1, 8]], A.not_equal, -500, 8, -1)
@@ -361,7 +360,7 @@ def program():
     iota(V("J8", 0, 768), [[0, 96], [8, 8]], 36); iota(V("ids", 0, 192), [[1, 192]], 2)
     iota(V("big", 0, 384), [[0, 24], [1, 16]]); ts(V("big", 0, 384), V("big", 0, 384), r, 4096, A.is_equal, A.mult)
     ts(pc("m9"), E(9), -8, None, A.mult); plus(V("W2", 768, 1600), V("W2", 768, 1600), pc("m9"))
-    iota(V("c884", 0, 192), [[0, 192]], 884); iota(V("cumb", 0, 1), [[0, 1]], 500); iota(V("num", 0, 2), [[0, 2]], 999); iota(V("Nw", 0, 2), [[0, 2]])
+    iota(V("cumb", 0, 1), [[0, 1]], 500); iota(V("num", 0, 2), [[0, 2]], 999); iota(V("Nw", 0, 2), [[0, 2]])
     iota(V("xw", 0, 32), [[-300, 2], [0, 16]]); iota(V("mid", 0, 168), [[0, 168]], 12582912 + 31)
     ts(pc("far"), nh, 10000, None, A.mult); iota(V("slf", 0, 96), [[1, 96]], 704); plus(V("slf", 0, 96), V("slf", 0, 96), pc("far"))
     ts(pc("cb"), h, 657, -1360, A.mult, A.add); iota(V("id16", 0, 96), [[1, 96]], 16); iota(V("cs", 0, 1), [[0, 1]], 500)
@@ -378,7 +377,7 @@ def program():
         either(eo, vf, lambda q, ap, eo=eo, vf=vf: q.tensor_copy(ap(eo), ap(vf)), lambda q, ap, eo=eo, vf=vf: q.activation(ap(eo), ap(vf), F.Silu))
     dma("s", [(lambda T, u=u: (S(T, "ZE", 96 * u, 96 * u + 96), S(T, "EW", 384 + 1536 * u, 1920 + 1536 * u, slice(0, 128, 16)))) for u in range(2)],
         [V("EW", 384, 3456)], [V("ZE", 0, 192)])
-    ts(V("i2", 0, 192), V("ZE", 0, 192), 16, None, A.max); cp(V("LA", 0, 96), V("i2", 0, 96)); cp(V("LB", 0, 96), V("i2", 96, 192))
+    for u, n_ in enumerate(("LA", "LB")): ts(V(n_, 0, 96), V("ZE", 96 * u, 96 * u + 96), 16, 0.25, A.max, A.add)
     zero("Zf", 384, [("ga", 1920, 2688)], 2500.0)
 
     sp = ((0, 512), (512, 576)); sq = ((0, 512), (512, 768)); late = []
@@ -424,9 +423,9 @@ def program():
         for c in range(6): act(V("junk", 48 * c, 48 * c + 36), V("cc", 1, 37), F.Sign, V("pk", 128 + c, 129 + c), -1.0, acc=V("vc", c, c + 1))
         ts(V("QL", 0, 6), V("vc", 0, 6), 0.5, 18, A.mult, A.add)
         tt(V("junk2", 0, 96), IND("rkw", 0, 37, V("QL", 0, 6)), V("id0", 0, 96), A.is_equal)
-        ts(V("vd", 0, 6), V("vc", 0, 6), 8, 416, A.mult, A.add); ts(V("vd", 8, 14), V("vc", 0, 6), 35, None, A.is_lt); tt(V("vd", 0, 6), V("vd", 0, 6), V("vd", 8, 14), A.mult)
-        mm([(V(P1, 0, 6), Z("ir", i), V("junk2", i, 96, 16)) for i in range(16)]); tt(V("vd", 8, 14), V(P1, 0, 6), V("vd", 0, 6), A.add)
-        for u in range(2): ts(V("VL", 6 * u, 6 * u + 6), V("vd", 8, 14), 1600 * u, None, A.add)
+        ts(V("vd", 0, 6), V("vc", 0, 6), 8, 416, A.mult, A.add); ts(V("vd", 8, 14), V("vc", 0, 6), 35, None, A.is_lt); tt(V("vb", 0, 6), V("vd", 0, 6), V("vd", 8, 14), A.mult)
+        mm([(V(P1, 0, 6), Z("ir", i), V("junk2", i, 96, 16)) for i in range(16)] + [(V(P1, 0, 6), M("I"), V("vb", 0, 6))])
+        for u in range(2): ts(V("VL", 6 * u, 6 * u + 6), V(P1, 0, 6), 1600 * u, None, A.add)
         ts(V("AI", 0, 48), K1, 7, 1023, A.arith_shift_right, A.bitwise_and); ts(V("AI", 48, 96), K1, 127, None, A.bitwise_and); ts(V("AI", 96, 144), K2, 31, None, A.bitwise_and)
         cp(V("AE", 0, 48), V("AI", 0, 48)); ts(V("e1", 0, 48), V("AI", 48, 96), 32, -1400, A.mult, A.add); tt(V("AE", 48, 96), V("e1", 0, 48), V("AI", 96, 144), A.add)
         mm([blank(V(P2, 0, 432))], final=False)
@@ -447,13 +446,12 @@ def program():
         mm(wrap(V(P0, 0, 48), "Rv", 0, 96)); cp(V("UL", 0, 48), V(P0, 0, 48))
         ts(V("fv", 0, 96), V("Rv", 0, 96), 1, None, A.is_ge)
         for u in range(2): cp(V("G", 384 * u, 384 * u + 384), IND("RR", 0, 800, V("UL", 24 * u, 24 * u + 24)), "av")
-        parts(cp, SPL[0], V("Lu", 0, 768), IND("xw", 0, 2720, V("AO", 48, 96)), "av"); scl(V("Lu", 768, 1536), V("Lu", 0, 768))
+        cp(V("Lu", 0, 768), IND("xw", 0, 2720, V("AO", 48, 96)), "av"); scl(V("Lu", 768, 1536), V("Lu", 0, 768))
         parts(cp, SPL[0], V("Aw", 32, 800), IND("TG", 0, 800, V("AO", 0, 48)), "av")
-        parts(relu, SPL[0], V("Bw", 32, 800), V("Aw", 32, 800))
-        if TWO: parts(cp, SPL[0], V("tg", 0, 768), IND("TG", 0, 800, V("AO", 0, 48)), "av")
+        relu(V("Bw", 32, 800), V("Aw", 32, 800))
         for u in range(2):
             a, b = 384 * u, 384 * u + 384; o = V(P2, 512 * u, 512 * u + 384)
-            mm([(o, M("Wk"), V("RR", 32 + a, 32 + b)), (o, M("N128"), a384("c8"))]); tt(V("clr", a, b), o, V("tg", a, b) if TWO else V("Aw", 32 + a, 32 + b), A.is_equal)
+            mm([(o, M("Wk"), V("RR", 32 + a, 32 + b)), (o, M("N128"), a384("c8"))]); tt(V("clr", a, b), o, V("Aw", 32 + a, 32 + b), A.is_equal)
         plus_dma(V("Aw", 32, 800), V("Lu", 0, 768)); plus_dma(V("Bw", 32, 800), V("Lu", 768, 1536))
         for kb_, o_ in (("Kn", 32), ("Ke", 832)):
             for u in range(2):
@@ -466,23 +464,23 @@ def program():
             mm([(V(Pn, c, c + 384), M("W2" if it == 2 else "Wc"), V("G", a, a + 384))], first=False)
             eq(V("EQ", 768 * it + a, 768 * it + a + 384), V(Pn, c, c + 384), 0, 0.0)
         for b in range(2):
-            mm([(V(P0, 96 * b, 96 * b + 96), M("X%d" % b), V("fv", 0, 96))] + [(V(P0, 96 * b, 96 * b + 96), Z("Y2", j), V("EQ", 768 * b + j, 768 * b + 768, 8)) for j in range(8)])
+            mm([(V(P0, 96 * b, 96 * b + 96), X(b), V("fv", 0, 96))] + [(V(P0, 96 * b, 96 * b + 96), Z("Y2", j), V("EQ", 768 * b + j, 768 * b + 768, 8)) for j in range(8)])
         relu(V("wish", 0, 192), V(P0, 0, 192), pc("m1"))
         mm([(V(P0, 512, 608), Z("all", j), V("EQ", 1536 + j, 2304, 8)) for j in range(8)])
         nf, po = V("nf", 0, 96), V(P0, 512, 608)
         either(nf, po, lambda q, ap: q.tensor_scalar(ap(nf), ap(po), -1.0, ap(pc("l64")), A.mult, A.add),
                lambda q, ap: q.activation(ap(nf), ap(po), F.Identity, bias=ap(pc("l64")), scale=-1.0), [pc("l64")])
-        codes = lambda c: [(V(P1, c + 192 * e + b, c + 192 * e + 192, 2), M("X%d" % (2 + 4 * sb + 2 * e + b)), V("wish", 96 * sb, 96 * sb + 96)) for e in range(2) for b in range(2) for sb in range(2)]
-        mm([(V(P1, 512 + 192 * e + b, 704 + 192 * e, 2), M("X%d" % (10 + 2 * e + b)), nf) for e in range(2) for b in range(2)], final=False)
+        codes = lambda c: [(V(P1, c + 192 * e + b, c + 192 * e + 192, 2), X(2 + 4 * sb + 2 * e + b), V("wish", 96 * sb, 96 * sb + 96)) for e in range(2) for b in range(2) for sb in range(2)]
+        mm([(V(P1, 512 + 192 * e + b, 704 + 192 * e, 2), X(10 + 2 * e + b), nf) for e in range(2) for b in range(2)], final=False)
         mm(codes(512), first=False); mm(codes(0)); cp(V("Nw", 2, 386), V(P1, 0, 384), "av")
         ts(V("fw", 0, 384), V(P1, 512, 896), -0.5, None, A.is_lt); tt(V("ok", 0, 192), V("fw", 0, 192), V("fw", 192, 384), A.mult)
         mm([(V(P0, 512, 704), M("Blk"), V("ok", 0, 192))]); mm([(V(P0, 0, 192), M("TriM"), V("ok", 0, 192))])
-        scan(V("cumb", 1, 193), V(P0, 512, 704), V("c884", 0, 192), 500.0, A.add, A.min)
-        scan(V("ws", 0, 192), V("big", 0, 192), V("cumb", 0, 192), 0.0, A.add, A.min); scan(V("we", 0, 192), V("big", 0, 192), V("cumb", 1, 193), 0.0, A.add, A.min)
-        tt(V("s2", 0, 12), V("we", 15, 192, 16), V("ws", 15, 192, 16), A.is_gt); tt(V("s2", 16, 28), V("s2", 0, 12), V("ws", 15, 192, 16), A.mult)
+        mm([(V(P1, 512, 524), Z("all", i), V("ok", i, 192, 16)) for i in range(16)]); ts(V("s2", 0, 12), V(P1, 512, 524), 0.5, None, A.is_gt)
+        scan(V("cumb", 1, 193), V(P0, 512, 704), V("Zr", 0, 192), 500.0, A.add, A.max)
+        scan(V("ws", 0, 192), V("big", 0, 192), V("cumb", 0, 192), 0.0, A.add, A.min); tt(V("s2", 16, 28), V("s2", 0, 12), V("ws", 15, 192, 16), A.mult)
         tt(V("s2", 32, 44), V("s2", 16, 28), V("pk", 96, 108), A.max); ts(V("ZL", 0, 12), V("s2", 32, 44), -308, None, A.add)
-        cp(IND("Z", 576 * t, 576 * t + 576, V("ZL", 0, 12)), V("ids", 0, 192))
-        zr = V("Z", 576 * t + 192, 576 * t + 576)
+        zero("Zr", 1536, [("Z", 192, 576)], 2500.0); cp(IND("Z", 0, 2880, V("ZL", 0, 12)), V("ids", 0, 192))
+        zr = V("Z", 192, 576)
         scan(a384("mx"), zr, zr, 0.0, A.max, A.max); scan(a384("wr"), a384("big"), a384("mx"), 0.0, A.add, A.min)
         cp(V("CL", 0, 24), V("wr", 15, 384, 16)); CL = V("CL", 0, 24)
         tt(V("num", 2, 194), V(P0, 0, 192), V("cumb", 0, 192), A.add)
@@ -515,8 +513,8 @@ def program():
             kb_, zz, o = (("Kn", "A", 32), ("Ke", "B", 832))[u]; po = V(Pn, c, c + b - a)
             mm([(po, M("I"), V(kb_, a, b))], final=False); mm([(po, Z(zz, s), V("Aux", 768 + 8 * a + s, 768 + 8 * b, 8)) for s in range(8)], first=False)
             cp(V("RR", o + a, o + b), po, "av")
-        for x in FOLD[:5]: fold(*x)
-        inner = lambda fold=fold: [fold(*x) for x in FOLD[5:]]
+        for x in FOLD[:4]: fold(*x)
+        inner = lambda fold=fold: [fold(*x) for x in FOLD[4:]]
         if last: inner()
         done = 0
         for a in range(0, Et, 384):
@@ -553,13 +551,14 @@ def program():
             a, b = V("s4", 48 * u, 48 * u + 24), V("s4", 48 * u + 24, 48 * u + 48)
             ts(a, valid, 0.5, base, A.is_gt, A.mult); tt(b, name, a, A.add); tt(a, b, V("pos", 0, 24), A.max); cp(o, a)
         o = V(P3, 0, 96)
-        mm([(o, Z("W", 0), V("RR", 1504, 1600)), (o, Z("W", 8), V("RR", 704, 800))])
-        tt(V("fl", 0, 96), o, V("slf", 0, 96), A.is_gt); plus(V("CT", 16, 112), o, pc("cb"))
-        mm([(V(P3, 512, 608), M("Blk"), V("fl", 0, 96))]); mm([(o, M("TR8"), V("fl", 0, 96))])
+        mm([(o, Z("W", 0), V("Ke", 672, 768)), (o, Z("W", 8), V("Kn", 672, 768))], final=False)
+        mm([(o, Z("C", s), V("Aux", 6144 + s, 6912, 8)) for s in range(8)], first=False)
+        tt(V("fl", 0, 96), o, V("slf", 0, 96), A.is_gt); ts(V("CT", 16, 112), o, pc("cb"), None, A.add)
+        mm([(V(P3, 512, 608), M("Blk"), V("fl", 0, 96))])
+        mm([(V(P3, 96, 102), Z("all", i), V("fl", i, 96, 16)) for i in range(16)], [(o, M("TR8"), V("fl", 0, 96))])
         scan(V("cs", 1, 97), V(P3, 512, 608), V("Zr", 0, 96), 500.0, A.add, A.max)
-        tt(V("PT", 16, 112), o, V("cs", 0, 96), A.add)
-        scan(V("w5", 0, 96), V("big", 0, 96), V("cs", 0, 96), 0.0, A.add, A.min); scan(V("w5", 96, 192), V("big", 0, 96), V("cs", 1, 97), 0.0, A.add, A.min)
-        tt(V("s5", 0, 6), V("w5", 111, 192, 16), V("w5", 15, 96, 16), A.is_gt); tt(V("s5", 8, 14), V("s5", 0, 6), V("w5", 15, 96, 16), A.mult)
+        ts(V("s5", 0, 6), V(P3, 96, 102), 0.5, None, A.is_gt); tt(V("PT", 16, 112), o, V("cs", 0, 96), A.add)
+        scan(V("w5", 0, 96), V("big", 0, 96), V("cs", 0, 96), 0.0, A.add, A.min); tt(V("s5", 8, 14), V("s5", 0, 6), V("w5", 15, 96, 16), A.mult)
         tt(V("s5", 16, 22), V("s5", 8, 14), V("pk", 120, 126), A.max); ts(V("ZS", 0, 6), V("s5", 16, 22), -404, None, A.add)
         cp(IND("Zs", 480 * t, 480 * t + 480, V("ZS", 0, 6)), V("id16", 0, 96))
         zr = V("Zs", 480 * t + 96, 480 * t + 480)
@@ -573,7 +572,7 @@ def program():
         send(4 * t, 1, V("sk", 48 * t, 48 * t + 48), V("lk", 48 * t, 48 * t + 48), LAT[0])
         cp(V("sy", 384 * t, 384 * t + 384), IND("xw", 0, 2720, V("E2", 0, 24)), "av")
         send(4 * t + 1, 1, V("sy", 384 * t, 384 * t + 384), V("ly", 384 * t, 384 * t + 384), LAT[1])
-        cp(IND("PN", 0, 3488, V("SS", 0, 24)), V("RR", 1632, 2016)); parts(cp, SPL[0], V("Go", 768, 1536), IND("PN", 768, 3488, V("Eb", 48, 96)), "av")
+        cp(IND("PN", 0, 3488, V("SS", 0, 24)), V("RR", 1632, 2016)); cp(V("Go", 768, 1536), IND("PN", 768, 3488, V("Eb", 48, 96)), "av")
         o = V(P3, 0, 48); mm([(o, Z("a0", i), V("Go", 768 + i, 1536, 16)) for i in range(16)]); cp(V("PL", 0, 48), o)
         o = V(*MIDB)
         mm([(o, Z("all", i), V("ix", 168 * i, 168 * i + 168)) for i in range(16) if 168 * i < Et + 384])
@@ -600,15 +599,17 @@ def program():
         ts(a384("pp"), a384("dd"), 0.5, None, A.is_gt); relu(a384("rs"), a384("dd")); ts(a384("pn"), a384("dd"), -0.5, None, A.is_lt)
         o = V(P3, 512, 536); mm([(o, Z("all", i), V("pp", i, 384, 16)) for i in range(16)]); ts(V("s3m", 416 * t + 384, 416 * t + 408), o, 8.5, None, A.is_ge)
         send(4 * t + 2, -1, V("s3m", 416 * t + 384, 416 * t + 408), V("l3m", 416 * t + 384, 416 * t + 408), LAT[0])
+        if last:
+            cp(mn, IND("xw", 0, 2720, V("E2", 24, 48)), "av"); send(4 * t + 3, -1, mn, V("l3m", 416 * t, 416 * t + 384), LAT[1]); mn = a384("Gn")
         o = V(P3, 0, 384); mm([(o, M("I"), yr)], final=False); mm([(o, M("I"), a384("rs"))], first=False); cp(mn, o, "av")
-        send(4 * t + 3, -1, mn, V("l3m", 416 * t, 416 * t + 384), LAT[1])
+        if not last: send(4 * t + 3, -1, mn, V("l3m", 416 * t, 416 * t + 384), LAT[1])
         o = V(P3, 512, 896); mm([(o, M("Blk"), a384("pn"))]); act(V("sn", 0, 384), o, F.Sign, pc("p85"), -1.0)
         for s in range(2):
             if s:
                 o = V(P3, 0, 384); mn = V("l3m", 416 * t, 416 * t + 384)
                 mm([(V(P3, i, 384, 16), V("BR", 128 * i, 128 * i + 128), V("l3m", 416 * t + 384, 416 * t + 408)) for i in range(16)])
                 cp(V("FR", 32, 416), o, "av"); parts(cp, SPL[0], V("Go", 768, 1536), IND("FR", 0, 416, V("PL", 0, 48)), "av")
-                if last: tt(IND("G1", 0, 3488, V("SS", 0, 24)), mn, a384("cm1"), A.mult)
+                if last: tt(a384("dd"), mn, V("sy", 384 * t, 384 * t + 384), A.max); tt(IND("G1", 0, 3488, V("SS", 0, 24)), a384("dd"), a384("cm1"), A.mult)
                 else: act(V("sn", 384, 768), o, F.Sign, pc("p85"), -1.0); tt(IND("xz", 0, 3488, V("SS", 0, 24)), mn, V("sn", 384, 768), A.mult)
             else:
                 tt(IND("xz", 0, 3488, V("SS", 24, 48)), mn, V("sn", 0, 384), A.mult)
@@ -624,7 +625,7 @@ def program():
             for s in range(2):
                 drop(s, 0, P1, 0); drop(s, 1, P1, 512); rows_out(P0, 672 * s, 672 * s + 96, 512 * s)
         else:
-            late.append(lambda drop=drop: [drop(*x) for x in ((0, 0, P3, 512), (0, 1, P3, 512), (1, 0, P3, 512), (1, 1, P3, 0))])
+            late.append(lambda drop=drop: [drop(*x) for x in ((0, 0, P3, 512), (1, 0, P3, 0), (0, 1, P3, 512), (1, 1, P3, 0))])
         if last:
             dma("s", [lambda T: (T.ylen[:, :], S(T, "G1", 800, 3488))], [V("G1", 800, 3488)], [V("out", 1, 2)], 4000.0)
             dma("a", [lambda T: (T.ynb[:, :], S(T, "O", 0, 768, slice(0, 64))), lambda T: (T.yen[:, :], S(T, "O", 0, 768, slice(64, 128)))], [V("O", 0, 768)], [V("out", 2, 3)], 3000.0)
@@ -669,7 +670,7 @@ def plan():
     for i, o in enumerate(ops):
         for j in o["dep"]: succ[j].append(i)
     pred = [list(o["dep"]) for o in ops]
-    lat = [o["lat"] for o in ops]
+    lat = [o["lat"] for o in ops]; pe = [o["engs"] == "p" for o in ops]
     how = [[(e, o.get("ca", o["cost"]) if e == "a" else o["cost"]) for e in o["engs"]] for o in ops]
 
     def place(pri, before, after, fixed, bias):
@@ -689,10 +690,9 @@ def plan():
             _, s, ec, at_, by = best
             busy[ec[0]].insert(at_, (s, s + ec[1], i)); t0[i] = s; f = fin[i] = s + ec[1] if back else s + ec[1] + lat[i]; eng[i] = ec
             if by >= 0: why[i] = -2 - by
-            f += SY
             for j in after[i]:
-                left[j] -= 1
-                if f > rdy[j]: rdy[j] = f; why[j] = i
+                left[j] -= 1; x = f if pe[i] and pe[j] else f + SY
+                if x > rdy[j]: rdy[j] = x; why[j] = i
                 if not left[j]: ready.append(j)
         return max(fin), t0, eng, pri, bias, fin, why
     pri = [0.0] * n
@@ -715,7 +715,20 @@ def plan():
                 if new[0] < cur[0] + 1000.0: cur = new
             if top is None or cur[0] < top[0]: top = cur
             p = place(cur[5], succ, pred, cur[2], zero)[5]
-    rs = np.random.RandomState(SEED); cur = top
+    far = [1.0 if o["kind"] == "c" else 1.5 for o in ops]; wake = [[(j, 0.0 if pe[i] and pe[j] else SY) for j in pred[i]] for i in range(n)]
+    slow = [1.0 if o["kind"] != "c" else 1.3 * (1.35 if any(v[4] for v in o["wr"]) else 1.2 if any(v[4] for v in o["rd"]) else 1.0) for o in ops]
+
+    def again(x):
+        free = dict.fromkeys("vapgsr", 0.0); fin = [0.0] * n; fre2 = dict(free); fi2 = [0.0] * n
+        for i in sorted(range(n), key=lambda k: x[1][k]):
+            e, c = x[2][i]; s = free[e]; u = fre2[e]
+            for j, w in wake[i]:
+                if fin[j] + w > s: s = fin[j] + w
+                if fi2[j] + w > u: u = fi2[j] + w
+            free[e] = s = s + c * slow[i]; fin[i] = s + lat[i]
+            fre2[e] = u = u + c * far[i]; fi2[i] = u + 1.7 * lat[i]
+        return (x[0] + WEIGHT * (max(fin) + max(fi2)),) + x[1:]
+    rs = np.random.RandomState(SEED); cur = top = again(top)
     for it in range(TRIES):
         i = max(range(n), key=lambda k: cur[5][k]); held = []
         while i != -1:
@@ -732,14 +745,16 @@ def plan():
                 elif len(how[y]) > 1 and rs.uniform() < 0.3: bias[y] = 1e5 if cur[2][y][0] == "v" else -1e5
                 else: p[x] = min(p[x], p[y]) - rs.uniform(0, 3000)
         else:
-            c0 = rs.uniform(0, cur[0]); w = rs.uniform(2000, 15000); z = rs.uniform(-1, 1, n) * rs.choice([300.0, 1000.0, 3000.0]) * (rs.uniform(0, 1, n) < 0.3)
+            c0 = rs.uniform(0, max(cur[5])); w = rs.uniform(2000, 15000); z = rs.uniform(-1, 1, n) * rs.choice([300.0, 1000.0, 3000.0]) * (rs.uniform(0, 1, n) < 0.3)
             p = [x + float(y) if abs(t - c0) < w else x for x, y, t in zip(p, z, cur[1])]
         new = place(p, pred, succ, None, bias)
         if rs.uniform() < 0.1: new = place(place(new[5], succ, pred, new[2], zero)[5], pred, succ, None, bias)
+        if new[0] > max(cur[5]) + 1500.0: continue
+        new = again(new)
         if new[0] <= cur[0] + HEAT * (1 - it / TRIES) * rs.exponential(): cur = new
         if cur[0] < top[0]: top = cur
     for i, o in enumerate(ops): o["t0"] = top[1][i]; o["e"] = top[2][i][0]; o["pri"] = pri[i]
-    return ops, sorted(range(n), key=lambda i: (top[1][i], i)), top[0]
+    return ops, sorted(range(n), key=lambda i: (top[1][i], i)), (max(top[5]), top[0])
 
 
 PLAN = []

import numpy as np
from concourse.mybir import AluOpType as A, ActivationFunctionType as F

F32, BF, I32, U16, H16 = "float32", "bfloat16", "int32", "uint16", "float16"
SB = dict(
    xz=(3488, BF), xw=(2720, BF), Lu=(1536, BF), RR=(2400, BF), Rs=(768, I32), NW=(768, I32), i2=(192, I32),
    EO=(384, U16), EW=(3840, F32), LA=(168, U16), LB=(168, U16), W=(384, U16), SL=(48, U16), XL=(16, U16),
    lo8=(800, BF), hi8=(800, BF), c8=(384, BF), cn=(36, H16), NM=(1152, BF), b1=(800, BF), b2=(800, BF), b3=(800, BF),
    PC=(128, F32), PI=(64, I32), CMx=(144, BF), CH=(128, BF), CO=(192, F32), MZ=(144 * 20, BF), M=(128 * 40, BF), MX=(2048, BF), PX=(256, BF), BR=(2048, BF), ZO=(192, BF),
    PAT=(240, BF), cod=(64, BF), pu=(192, BF), jk=(64, I32), SEL=(16, BF), SW=(272, H16), CX=(96, BF),
    fil=(576, BF), GD=(800, BF), G1=(6144, BF), KS=(192, F32), OWN=(192, F32), KI=(96, I32), XI=(96, I32), AI=(144, I32), e1=(48, F32), XR=(384, BF), OH=(3456, BF),
    AE=(96, H16), AO=(96, U16), ch=(36, BF), cc=(40, F32), rkw=(40, F32), cw=(36, BF), TG=(800, F32), ctr=(576 * 3, BF), tg=(768, F32), gb=(1536, F32), clr=(768, BF),
    junk=(288, BF), junk2=(96, BF), id0=(96, BF), vc=(16, F32), vd=(16, F32), vb=(6, BF), QL=(6, U16), VL=(12, U16),
    Rv=(192, BF), fv=(96, BF), UL=(48, U16), s1=(96, F32), s2=(96, F32), s3=(96, F32), pos=(48, F32), pk=(192, F32),
    Lf=(768, F32), Aw=(800, F32), Bw=(800, F32), Kn=(768, BF), Ke=(768, BF),
    G=(768, BF), EQ=(2304, BF), wish=(192, BF), nf=(96, BF), Nw=(400, BF), fw=(384, BF), ok=(192, BF), cumb=(208, F32),
    num=(208, F32), big=(384, BF), ws=(192, F32), ZL=(12, U16), Z=(2880, BF), ids=(192, BF), mx=(384, BF), wr=(384, BF), CL=(24, U16),
    im=(384, F32), oh=(384, BF), pr=(768, BF), j1=(48, I32), j2=(48, I32), j3=(48, I32), IL=(48, U16), W2=(1600, BF), J8=(768, BF), G2=(768, BF), e2=(768, BF),
    AL=(48, U16), Aux=(6912, BF), gz=(3840, F32), ga=(2688, F32), zb=(1536, BF), mk=(1536, BF), rl=(2304, BF), zn=(384, F32), ix=(2688, BF),
    own=(168, F32), mid=(168, F32), m1=(168, I32), m2=(168, F32), m3=(168, F32),
    sk=(144, U16), lk=(144, U16), sy=(1152, BF), ly=(1152, BF), s3m=(1248, BF), l3m=(1248, BF), Eb=(96, U16), E2=(48, U16), SS=(48, U16), ZS=(6, U16),
    slf=(96, F32), fl=(96, BF), CT=(112, F32), PT=(112, F32), cs=(100, F32), w5=(192, F32), s4=(96, F32), s5=(24, F32), Zs=(1440, BF), id16=(96, BF),
    mx2=(384, BF), wr2=(384, BF), oh2=(384, BF), cx=(384, H16), bb=(24, BF), Gn=(384, BF), ohc=(384, BF), nm=(384, BF), dd=(384, BF), rs=(384, BF),
    pp=(384, BF), pn=(384, BF), Go=(1536, BF), sn=(768, BF), PN=(3488, BF), FR=(416, BF), PL=(48, U16), cm1=(384, BF),
    O=(768, F32), Zr=(1536, BF), Zf=(384, F32), ZE=(192, F32), Vf=(768, F32),
)
ALIAS = dict(xw=("xz", 768), ga=("gz", 0), EW=("gz", 0), Vf=("O", 0), b1=("EQ", 0), b2=("EQ", 800), b3=("rl", 0), lo8=("Go", 0), hi8=("OH", 0),
             CO=("gb", 0), Lf=("gb", 768), tg=("gb", 0), i2=("Rs", 0))
LOC, SCRATCH = {}, {}
for _d in (F32, BF, I32, U16, H16):
    _n, _o = 0, 0
    for _k, (_w, _e) in SB.items():
        if _e != _d or _k in ALIAS: continue
        if _o + _w > 16384: _n, _o = _n + 1, 0
        LOC[_k] = ("%s%d" % (_d, _n), _o); _o += (_w + 31) // 32 * 32
        SCRATCH[LOC[_k][0]] = ("sbuf", [128, _o], _d)
for _k, (_b, _o) in ALIAS.items():
    LOC[_k] = (LOC[_b][0], LOC[_b][1] + _o)


def S(T, n, a, b, rows=slice(None)):
    return T[LOC[n][0]][rows, LOC[n][1] + a:LOC[n][1] + b]


SPL = [2, 1]
ACC = [4, 4, 0]
EARLY = [("EW", 3, 30000.0, 1e6), ("LA", 0, 10000.0, 1e6)] + [(n, k, up, 25000.0) for n, k in (("zb", 0), ("zb", 4), ("zb", 9), ("zb", 3), ("zb", 8), ("zb", 14)) for up in (5000.0, 10000.0)]
PIECE = 1200.0
BRV = 8
ABS = [0, 3, 3]
MIDB = ("P2", 0, 168)
DV = [0, 0, 0]
FOLD = [(0, 0, 384, "P1", 0), (0, 384, 768, "P1", 512), (1, 0, 96, "P0", 512), (1, 672, 768, "P0", 512), (1, 96, 384, "P1", 0), (1, 384, 672, "P1", 512)]
FIRST = [0, 0, 0]
KEYS = 5
EWV = 3
BIASES, PASSES, SEED, TRIES, SY, MOVE, LIFT, HEAT = (300.0, 700.0, 2000.0), 3, 1, 5200, 170.0, 0.5, 0.75, 300.0
for _k in range(4):
    SCRATCH["P%d" % _k] = ("psum", [128, 1024], F32)
NDMA = 48
SEMAPHORES = ["ev", "ea", "ep", "eg", "ax"] + ["d%d" % k for k in range(NDMA)] + [a + str(k) for a in "rl" for k in range(12)]
SEND, LAT = 1500.0, (3600.0, 5500.0)
CYC = 1.04
GAT, SCA, PEC, WEIGHT = 1.56, 3.8, 0.6, 0.6


def V(n, a, b, s=1, rows=None):
    return (n, a, b, s, None, rows)


def IND(n, a, b, off):
    return (n, a, b, 1, off, None)


def wid(v):
    return 16 * wid(v[4]) if v[4] else len(range(v[1], v[2], v[3]))


def two(v):
    return v[0] in SB and SB[v[0]][1] in (BF, U16, H16)


def make_ap(T, v, step):
    if v == "step": return step
    if not isinstance(v, tuple): return v
    nm, o = LOC.get(v[0], (v[0], 0)); rows = slice(*v[5]) if v[5] else slice(None)
    x = T[nm][rows, o + v[1]:o + v[2]] if v[3] == 1 else T[nm][rows, o + v[1]:o + v[2]:v[3]]
    return x.indirect(make_ap(T, v[4], step)) if v[4] else x


def program():
    ops = []

    def add(engs, fn, rd, wr, cost, kind="c", lat=0.0):
        r = []
        for v in rd:
            if isinstance(v, tuple):
                r.append(v)
                if v[4]: r.append(v[4])
        w = []
        for v in wr:
            w.append(v)
            if v[4]: r.append(v[4])
        ops.append(dict(engs=engs, fn=fn, rd=r, wr=w, cost=cost, kind=kind, lat=lat))

    def el(o, i, base):
        if o[4]: return SCA * wid(o)
        if i[4]: return GAT * wid(o)
        return base * wid(o)

    def ts(o, i, s1, s2, op0, op1=None):
        def fn(q, e, ap):
            if op1 is None: return q.tensor_scalar(ap(o), ap(i), ap(s1), None, op0)
            return q.tensor_scalar(ap(o), ap(i), ap(s1), ap(s2), op0, op1)
        add("v", fn, [i, s1, s2], [o], 60 + CYC * el(o, i, 0.5 if two(o) and two(i) else 1))

    def tt(o, a, b, op):
        base = 1 if a[0] not in SB or b[0] not in SB else (1.5 if two(o) and two(a) and two(b) else 2)
        add("v", lambda q, e, ap: q.tensor_tensor(ap(o), ap(a), ap(b), op), [a, b], [o], 60 + CYC * el(o, a, base))

    def either(o, i, fv, fa, more=(), engs="av"):
        add(engs, lambda q, e, ap: fv(q, ap) if e == "v" else fa(q, ap), [i] + list(more), [o], 60 + CYC * el(o, i, 0.5 if two(o) and two(i) else 1))
        ops[-1]["ca"] = 80 + CYC * el(o, i, 1)

    def cp(o, i, engs="v"):
        either(o, i, lambda q, ap: q.tensor_copy(ap(o), ap(i)), lambda q, ap: q.activation(ap(o), ap(i), F.Copy), engs=engs)

    def scl(o, i, c=-1.0):
        either(o, i, lambda q, ap: q.tensor_scalar(ap(o), ap(i), ap(c), None, A.mult), lambda q, ap: q.activation(ap(o), ap(i), F.Copy, scale=ap(c)), [c])

    def plus(o, i, c):
        either(o, i, lambda q, ap: q.tensor_scalar(ap(o), ap(i), ap(c), None, A.add), lambda q, ap: q.activation(ap(o), ap(i), F.Identity, bias=ap(c)), [c])

    def relu(o, i, bias=None):
        if bias is None:
            either(o, i, lambda q, ap: q.tensor_scalar(ap(o), ap(i), 0.0, None, A.max), lambda q, ap: q.activation(ap(o), ap(i), F.Relu))
        else:
            either(o, i, lambda q, ap: q.tensor_scalar(ap(o), ap(i), ap(bias), 0.0, A.add, A.max), lambda q, ap: q.activation(ap(o), ap(i), F.Relu, bias=ap(bias)), [bias])

    def pos_(o, i):
        either(o, i, lambda q, ap: q.tensor_scalar(ap(o), ap(i), 0.5, None, A.is_gt), lambda q, ap: q.activation(ap(o), ap(i), F.Sign))

    def act(o, i, f, bias=0.0, scale=1.0, acc=None):
        def fn(q, e, ap):
            if acc: return q.activation(ap(o), ap(i), f, bias=ap(bias), scale=ap(scale), accum_out=ap(acc))
            return q.activation(ap(o), ap(i), f, bias=ap(bias), scale=ap(scale))
        add("a", fn, [i, bias, scale], [o] + ([acc] if acc else []), 80 + CYC * wid(o))

    def eq(o, i, c, nc):
        def fn(q, e, ap):
            if e == "v": return q.tensor_scalar(ap(o), ap(i), ap(c), None, A.is_equal)
            ap("step")(q.activation(ap(o), ap(i), F.Abs, bias=ap(nc)))
            return q.activation(ap(o), ap(o), F.Relu, bias=ap(pc("one")), scale=-1.0)
        add("av", fn, [i, c, nc, pc("one")], [o], 60 + CYC * wid(o)); ops[-1]["ca"] = 160 + SY + 2 * CYC * wid(o)

    def parts(f, k, *vs):
        def cut(v, j):
            if v[4]: return (v[0], v[1], v[2], 1, cut(v[4], j), None)
            w = (v[2] - v[1]) // k
            return V(v[0], v[1] + j * w, v[1] + j * w + w)
        for j in range(k): f(*[cut(v, j) if isinstance(v, tuple) else v for v in vs])

    def scan(o, d0, d1, init, op0, op1):
        add("v", lambda q, e, ap: q.tensor_tensor_scan(ap(o), ap(d0), ap(d1), init, op0, op1), [d0, d1], [o],
            60 + CYC * wid(o) * (0.5 if two(o) and two(d0) and two(d1) else 1))

    def mset(o, c):
        add("v", lambda q, e, ap: q.memset(ap(o), c), [], [o], 60 + CYC * wid(o) * (0.5 if two(o) else 1))

    def iota(o, pat, base=0, cm=0):
        def fn(q, e, ap):
            if SB[o[0]][1] == I32: return q.iota(ap(o), pat, base, cm)
            return q.iota(ap(o), pat, base, cm, allow_small_or_imprecise_dtypes=True)
        add("g", fn, [], [o], 150 + 2 * CYC * wid(o))

    def select(o, i, pat, op, fill, base, cm):
        add("g", lambda q, e, ap: q.affine_select(ap(o), ap(i), pat, op, float(fill), base, cm), [i], [o], 200 + 2 * CYC * wid(o))

    def where0(o, pat, base, cm, fill):
        select(o, V("Zr", 0, wid(o)), pat, A.not_equal, fill, base, cm)

    def mm(*groups, first=True, final=True):
        al = [(o, l, r, first and n == 0, final and n == len(gr) - 1, PEC * max(min(64, wid(l)), wid(o))) for gr in groups for n, (o, l, r) in enumerate(gr)]
        k = int(sum(x[5] for x in al) // PIECE) + 1
        for j in range(k):
            run = al[j * len(al) // k:(j + 1) * len(al) // k]
            if run:
                add("p", lambda q, e, ap, run=run: [q.matmul(ap(x[0]), ap(x[1]), ap(x[2]), x[3], x[4]) for x in run][-1],
                    [x[1] for x in run] + [x[2] for x in run], [x[0] for x in run], (60 if j == 0 else 10) + sum(x[5] for x in run))

    def dma(eng, pairs, rd, wr, lat=2200.0):
        add(eng, pairs, rd, wr, (1000.0 if eng == "g" else 60.0) * len(pairs), kind="d", lat=lat)

    def plus_dma(o, i):
        dma("g", [lambda T: (S(T, o[0], o[1], o[2]), S(T, i[0], i[1], i[2]), dict(accum_op=A.add))], [o, i], [o], 3600.0)

    P0, P1, P2, P3 = "P0", "P1", "P2", "P3"
    a384 = lambda n: V(n, 0, 384)
    for q, ks in (("s", range(0, 4)), ("a", range(4, 8))):
        dma(q, [(lambda T, k=k, n=n, u=u: (S(T, "Rs", 0, 768, slice(k + u, 128, 16)), T[n][:, 48 * k:48 * k + 48])) for k in ks for n, u in (("nb", 0), ("en", 8))],
            [], [V("Rs", 0, 768)] if q == "s" else [V("Rs2", 0, 768)])
    dma("s", [lambda T: (S(T, "NW", 0, 384), T.nb[:, :])], [], [V("NW", 0, 384)]); dma("a", [lambda T: (S(T, "NW", 384, 768), T.en[:, :])], [], [V("NW", 384, 768)])
    dma("s", [lambda T: (S(T, "xw", 32, 1568), T.lens[:, :])], [], [V("xw", 32, 1568)], 3500.0)
    for a in (32, 800): scl(V("xw", a, a + 768), V("xw", a, a + 768))

    def zero(z, zw, parts, lat):
        ps = [(n, c, min(b, c + zw)) for n, a, b in parts for c in range(a, b, zw)]
        dma("s", [(lambda T, n=n, a=a, b=b: (S(T, n, a, b), S(T, z, 0, b - a))) for n, a, b in ps], [V(z, 0, zw)], [V(*p) for p in parts], lat)
    mset(V("Zf", 0, 384), 0); zero("Zf", 384, [("EW", 384, 3456)], 6000.0)
    mset(V("Zr", 0, 1536), 0); zero("Zr", 1536, [("xw", 1568, 2720), ("Zs", 0, 1440), ("PN", 768, 3488), ("FR", 0, 32), ("ix", 1920, 2688), ("GD", 0, 128), ("GD", 704, 800)], 5000.0)
    pcn = {}

    def pc(n, w=1):
        if n not in pcn:
            a = sum(x[2] - x[1] for x in pcn.values()); pcn[n] = V("PC", a, a + w)
        return pcn[n]

    def col(v, j):
        return V(v[0], v[1] + j, v[1] + j + 1)
    iota(V("PI", 0, 1), [[0, 1]], 0, 1)
    iota(V("CMx", 0, 144), [[1, 144]], -15)
    iota(V("CH", 0, 128), [[1, 16], [0, 8]])
    iota(V("PI", 8, 24), [[1, 16]])
    iota(V("pos", 0, 48), [[1, 48]])
    iota(V("lo8", 0, 800), [[0, 25], [1, 32]])
    iota(V("hi8", 0, 800), [[1, 25], [0, 32]])
    ts(V("PI", 1, 2), V("PI", 0, 1), 15, None, A.bitwise_and)
    ts(V("PI", 2, 3), V("PI", 0, 1), 7, None, A.bitwise_and)
    ts(V("PI", 3, 4), V("PI", 0, 1), 4, None, A.arith_shift_right)
    cp(pc("rlg", 3), V("PI", 1, 4))
    r, l, gr = col(pc("rlg"), 0), col(pc("rlg"), 1), col(pc("rlg"), 2)
    h, nh, wlh = pc("h"), pc("nh"), pc("wlh")
    ts(h, r, 8, None, A.is_ge); ts(nh, r, 8, None, A.is_lt); ts(wlh, h, 31, 1, A.mult, A.add)
    ts(pc("g16"), gr, 16, None, A.mult); ts(pc("g2"), gr, 2, None, A.mult)
    ts(pc("E", 16), V("PI", 8, 24), r, None, A.is_equal)
    E = lambda j: col(pc("E"), j)
    ts(pc("r48"), r, 48, None, A.mult)
    ts(V("SL", 0, 48), V("pos", 0, 48), pc("r48"), None, A.add)
    ts(V("pos", 0, 48), V("pos", 0, 48), 16, r, A.mult, A.add)
    ts(V("CMx", 0, 144), V("CMx", 0, 144), pc("g16"), None, A.subtract)
    CM0 = V("CMx", 15, 143)
    zn_, mn_ = {}, {}

    def Z(n, c=None):
        if n not in zn_: zn_[n] = 144 * len(zn_)
        a = zn_[n]
        return V("MZ", a, a + 144) if c is None else V("MZ", a + 15 - c, a + 143 - c)

    def M(n):
        if n not in mn_: mn_[n] = 128 * len(mn_)
        return V("M", mn_[n], mn_[n] + 128)

    def half(v, u):
        return V(v[0], v[1] + 64 * u, v[1] + 64 * u + 64)

    def zm(n, tg_, w):
        ts(Z(n), V("CMx", 0, 144), tg_, w, A.is_equal, A.mult)

    def diag(n, c):
        where0(M(n), [[1, 128]], 0, -1, c)
    zm("lo", l, nh); zm("hi", l, h); zm("W", l, wlh)
    ts(M("I"), CM0, r, None, A.is_equal)
    ts(V("CH", 0, 128), V("CH", 0, 128), pc("g2"), None, A.subtract)
    ts(M("t1"), V("CH", 0, 128), 0, None, A.is_ge); ts(M("t2"), V("CH", 0, 128), 2, None, A.is_lt); tt(M("Blk"), M("t1"), M("t2"), A.mult)
    ts(pc("mhh"), h, -1, None, A.mult); scl(M("NHi"), M("Blk"), pc("mhh"))
    ts(M("t1"), CM0, r, None, A.is_gt); tt(M("TriM"), M("t1"), M("Blk"), A.mult); select(M("TriM"), M("TriM"), [[1, 128]], A.not_equal, -500, 0, -1)
    ts(pc("n128"), h, -128, None, A.mult)
    mset(V("RR", 0, 32), 0); mset(V("RR", 800, 832), 0)
    SLv = V("SL", 0, 48); Rsw = IND("Rs", 0, 768, SLv)
    ts(V("b1", 0, 768), Rsw, 1.0 / 32, 128.515625, A.mult, A.add); ops[-1]["rd"].append(V("Rs2", 0, 768))
    ts(pc("b4128"), r, 0, -4128, A.mult, A.add)
    act(V("b2", 0, 768), V("b1", 0, 768), F.Relu, pc("b4128"), 32.0)
    tt(V("b3", 0, 768), Rsw, V("b2", 0, 768), A.subtract)
    for Pn, za, zb, o in ((P0, Z("lo", 0), Z("lo", 8), 32), (P1, Z("hi", 0), Z("hi", 8), 832)):
        mm(*[[(V(Pn, a, b), zb, V("b1", a, b))] for a, b in ((0, 512), (512, 768))], final=False)
        mm(*[[(V(Pn, a, b), za, V("b3", a, b))] for a, b in ((0, 512), (512, 768))], first=False)
        relu(V("RR", o, o + 768), V(Pn, 0, 768), pc("n128"))

    def wrap(o, n, a, b):
        return [(o, Z("W", 0), V(n, a, b, 2)), (o, Z("W", 8), V(n, a + 1, b, 2))]
    nbw, enw = V("NW", 0, 384), V("NW", 384, 768)
    ts(V("W", 0, 384), nbw, 32, None, A.add); ts(V("Ke", 0, 384), nbw, 0, 4, A.is_ge, A.mult)
    for i in range(BRV): ts(V("BR", 128 * i, 128 * i + 128), M("Blk"), E(i), 4096, A.mult, A.mult)
    for u in range(BRV // 4, 4): where0(V("BR", 512 * u, 512 * u + 512), [[1, 4], [16, 8], [0, 16]], 4 * u, -1, 4096)
    mm([(V(P2, 0, 36), M("I"), V("Ke", 48 * k + 6, 48 * k + 42)) for k in range(8)]); cp(V("cw", 0, 36), V(P2, 0, 36), "av")
    for u in range(2):
        mm([(V(P2, 512 * u + i, 512 * u + 288, 16), V("BR", 128 * i, 128 * i + 128), V("cw", 18 * u, 18 * u + 18)) for i in range(16)])
        act(V("GD", 128 + 288 * u, 416 + 288 * u), V(P2, 512 * u, 512 * u + 288), F.Relu, pc("ten"), -1.0 / 16384)
    diag("D96", 96); diag("D1536", 1536); diag("N1536", -1536)
    iota(V("Lf", 0, 384), [[0, 8], [16, 48]]); plus(V("Lf", 0, 384), V("Lf", 0, 384), r)
    iota(V("Lf", 384, 768), [[0, 16], [16, 24]], -192255); plus(V("Lf", 384, 768), V("Lf", 384, 768), r)
    tt(V("Kn", 0, 384), nbw, V("Lf", 0, 384), A.is_lt); cp(a384("cx"), enw); ts(V("Kn", 384, 768), enw, 1.0 / 16, 128.53125, A.mult, A.add)
    o = V(P3, 0, 384)
    mm([(o, M("D96"), a384("cx")), (o, M("N1536"), V("Kn", 384, 768)), (o, M("I"), V("Kn", 384, 768)), (o, M("D1536"), V("Ke", 0, 384)), (o, M("D1536"), V("Kn", 0, 384))])
    tt(V("tg", 384, 768), o, V("Lf", 384, 768), A.max); ts(V("EO", 0, 384), V("tg", 384, 768), 192255, None, A.add)
    mm(*[[(V(P3, a, b), Z("lo", 0), V("lo8", a, b)), (V(P3, a, b), Z("hi", 8), V("hi8", a, b))] for a, b in ((0, 512), (512, 800))])
    cp(V("RR", 1600, 2400), V(P3, 0, 800), "av")
    where0(V("SEL", 0, 16), [[0, 2], [16, 8]], 0, -1, -131072)
    where0(M("SE"), [[1, 8], [-8, 2], [16, 8]], 8, -1, 1)
    where0(M("SN"), [[1, 8], [0, 2], [16, 8]], 0, -1, 128); select(M("SN"), M("SN"), [[1, 8], [0, 2], [16, 8]], A.not_equal, 4096, 8, -1)
    iota(V("CX", 0, 48), [[0, 48]], -8); iota(V("CX", 48, 96), [[0, 4], [16, 2], [0, 6]])
    iota(V("im", 0, 384), [[1, 384]])
    ts(pc("sw"), pc("g16"), 2, 16, A.mult, A.add); ts(pc("sw"), pc("sw"), r, None, A.add); ts(V("SW", 0, 272), V("im", 0, 272), pc("sw"), None, A.is_equal)
    iota(V("OWN", 96, 192), [[0, 96]], 1000000); iota(V("cc", 0, 1), [[0, 1]], 500); iota(V("rkw", 36, 37), [[0, 1]], 999); iota(V("id0", 0, 96), [[1, 96]])
    diag("N128", -128); diag("D2", -2); diag("nI", -1)
    tt(M("Wc"), Z("W", 0), Z("W", 8), A.add); scl(M("Wk"), M("Wc"), 4096.0); scl(M("NWk"), M("Wc"), -4096.0); tt(M("W2"), Z("hi", 0), Z("W", 8), A.add)
    ts(pc("h8"), h, 8, None, A.mult); ts(pc("l8"), l, 8, None, A.mult); ts(pc("l8b"), l, 8, -16, A.mult, A.add); ts(pc("l64"), l, -8, 64, A.mult, A.add)
    ts(pc("we"), l, 0, wlh, A.is_equal, A.mult); tt(pc("ws"), l, nh, A.mult)
    ts(pc("wu"), E(9), 32, E(8), A.mult, A.add); ts(pc("wu"), pc("wu"), 8, None, A.mult)
    tt(pc("wa"), E(8), E(9), A.add); tt(pc("wb"), E(10), E(11), A.add)
    zm("all", 0, 1); zm("Y2", pc("h8"), -4); zm("s", 0, pc("ws")); zm("u", 0, pc("wu")); zm("A", pc("l8"), pc("wa")); zm("B", pc("l8b"), pc("wb"))
    ts(pc("tc"), pc("wa"), 8, None, A.mult); ts(pc("wc"), E(11), 32, E(10), A.mult, A.add); ts(pc("wc"), pc("wu"), 0.125, pc("wc"), A.mult, A.add); zm("C", pc("tc"), pc("wc"))
    zm("0", 0, E(0)); zm("ir", 0, r); zm("uh", 0, h); zm("lh", 0, nh); zm("aw", 0, wlh); zm("a0", 0, pc("we"))
    zm("2", 8, 1); tt(Z("2"), Z("2"), Z("all"), A.add); scl(Z("2"), Z("2"), -8.0)
    ts(M("t1"), V("CH", 0, 128), -99, None, A.add); tt(M("t2"), M("t1"), M("Blk"), A.mult); ts(V("CH", 0, 128), M("t2"), 99, None, A.add)
    CH = V("CH", 0, 128)
    ts(V("PI", 24, 32), V("PI", 8, 16), -1, l, A.mult, A.add); ts(V("PI", 24, 32), V("PI", 24, 32), 7, None, A.bitwise_and); cp(pc("dd", 8), V("PI", 24, 32))
    ts(pc("nw"), wlh, -1, None, A.mult); ts(pc("nwe"), pc("we"), -1, None, A.mult)
    for k in range(8): ts(M("N%d" % k), CH, col(pc("dd"), k), pc("nw"), A.is_equal, A.mult)
    ts(M("NV"), CH, 1, pc("nwe"), A.is_equal, A.mult); ts(M("NLo"), CH, 0, -1, A.is_equal, A.mult); ts(M("R0"), CH, 0, E(0), A.is_equal, A.mult)
    ts(M("t1"), CM0, l, -1, A.is_gt, A.mult); tt(M("t2"), M("t1"), M("NLo"), A.mult); ts(M("t1"), CM0, l, -100, A.is_equal, A.mult); tt(M("CF"), M("t1"), M("t2"), A.add)
    u0 = [M("U%d" % j) for j in range(8)][0][1]; zero("Zr", 1536, [("M", u0, u0 + 1024), ("W2", 768, 1600)], 3000.0)
    for u in range(2): where0(V("M", u0 + 8 + u, u0 + 1024, 16), [[1, 8], [16, 8]], 8 * u, -1, 1)
    iota(V("CO", 0, 192), [[1, 192]], -64)
    ts(pc("to"), gr, 8, l, A.mult, A.add); ts(V("ZO", 0, 192), V("CO", 0, 192), pc("to"), wlh, A.is_equal, A.mult)
    iota(V("jk", 0, 32), [[0, 4], [1, 8]]); iota(V("jk", 32, 64), [[1, 4], [1, 8]], 1)
    ts(V("jk", 32, 64), V("jk", 32, 64), 7, None, A.bitwise_and)
    ts(V("pu", 0, 64), V("jk", 0, 64), l, h, A.is_equal, A.mult); tt(V("PAT", 0, 32), V("pu", 0, 32), V("pu", 32, 64), A.add)
    o_ = 0
    for j in range(7):
        iota(V("cod", o_, o_ + 7 - j), [[1, 7 - j]], 17 * j + 1); iota(V("cod", 32 + o_, 32 + o_ + 7 - j), [[16, 7 - j]], 17 * j + 16); o_ += 7 - j
    iota(V("cod", 28, 32), [[0, 4]], -512); iota(V("cod", 60, 64), [[0, 4]], -512)
    cod = V("cod", 0, 64)
    ts(pc("r16"), r, 16, None, A.mult); ts(pc("p12"), r, 12, 1000, A.is_ge, A.mult)
    ts(V("pu", 0, 64), cod, pc("r16"), 0, A.subtract, A.is_ge); ts(V("pu", 64, 128), cod, pc("r16"), 8, A.subtract, A.is_ge)
    tt(V("PAT", 160, 224), V("pu", 0, 64), V("pu", 64, 128), A.subtract)
    tt(pc("lh"), l, h, A.add)
    for sb in range(2):
        y = pc("y%d" % sb); ts(V("PI", 40, 41), pc("lh"), 2 * sb + 1, None, A.add); ts(V("PI", 41, 42), V("PI", 40, 41), 7, None, A.bitwise_and); cp(y, V("PI", 41, 42))
        dst = V("PAT", 32 + 64 * sb, 96 + 64 * sb)
        for z, (a_, b_) in enumerate(((l, y), (y, l))):
            c0, w0 = pc("k%d%d" % (sb, z)), pc("w%d%d" % (sb, z))
            ts(c0, a_, 16, b_, A.mult, A.add)
            if sb: tt(c0, c0, pc("p12"), A.add)
            ts(w0, a_, 8, -64, A.mult, A.add)
            ts(V("pu", 0, 64), cod, c0, 1, A.subtract, A.is_ge); ts(V("pu", 64, 128), cod, c0, 8, A.subtract, A.is_ge); ts(V("pu", 128, 192), cod, c0, w0, A.is_equal, A.mult)
            tt(V("pu", 0, 64), V("pu", 0, 64), V("pu", 64, 128), A.subtract)
            if z: tt(V("pu", 0, 64), V("pu", 0, 64), dst, A.add)
            tt(dst, V("pu", 0, 64), V("pu", 128, 192), A.add)
    iota(V("PAT", 224, 240), [[0, 16]]); ts(pc("x16"), pc("r16"), 224, None, A.min); ts(V("XL", 0, 16), V("PI", 8, 24), pc("x16"), None, A.add)
    cp(V("PX", 0, 256), IND("PAT", 0, 240, V("XL", 0, 16)), "av"); zero("Zr", 1536, [("MX", 0, 2048)], 3000.0)
    dma("s", [(lambda T, g=g: (S(T, "MX", 256 * g, 256 * g + 256, slice(16 * g, 16 * g + 16)), S(T, "PX", 0, 256, slice(16 * g, 16 * g + 16)))) for g in range(8)],
        [V("PX", 0, 256)], [V("MX", 0, 2048)])
    X = lambda n: V("MX", n, 2048, 16)
    TR = M("TR8")
    select(TR, V("Zr", 0, 128), [[-16, 8], [0, 2], [-1, 8]], A.is_ge, 1, -8, 1); select(TR, TR, [[-16, 8], [0, 16]], A.is_ge, 0, -8, 1)
    select(TR, TR, [[16, 8], [0, 2], [1, 8]], A.not_equal, -500, 8, -1)
    iota(V("c8", 0, 384), [[0, 384]], 8); iota(a384("cm1"), [[0, 384]], -1); iota(V("Bw", 0, 32), [[0, 32]]); iota(V("Aw", 0, 32), [[-1024, 2], [0, 16]])
    iota(V("TG", 0, 128), [[0, 128]], -1024); iota(V("TG", 704, 800), [[0, 96]], -1024); ts(V("pk", 0, 36), V("pos", 0, 36), 128, None, A.add)
    iota(V("J8", 0, 768), [[0, 96], [8, 8]], 36); iota(V("ids", 0, 192), [[1, 192]], 2)
    iota(V("big", 0, 384), [[0, 24], [1, 16]]); ts(V("big", 0, 384), V("big", 0, 384), r, 4096, A.is_equal, A.mult)
    ts(pc("m9"), E(9), -8, None, A.mult); plus(V("W2", 768, 1600), V("W2", 768, 1600), pc("m9"))
    iota(V("cumb", 0, 1), [[0, 1]], 500); iota(V("num", 0, 2), [[0, 2]], 999); iota(V("Nw", 0, 2), [[0, 2]])
    iota(V("xw", 0, 32), [[-300, 2], [0, 16]]); iota(V("mid", 0, 168), [[0, 168]], 12582912 + 31)
    ts(pc("far"), nh, 10000, None, A.mult); iota(V("slf", 0, 96), [[1, 96]], 704); plus(V("slf", 0, 96), V("slf", 0, 96), pc("far"))
    ts(pc("cb"), h, 657, -1360, A.mult, A.add); iota(V("id16", 0, 96), [[1, 96]], 16); iota(V("cs", 0, 1), [[0, 1]], 500)
    iota(V("PT", 0, 16), [[0, 16]], 999); iota(V("CT", 0, 16), [[0, 16]]); ts(V("pk", 120, 126), V("pos", 0, 6), 404, None, A.add)
    ts(V("pk", 48, 96), V("pos", 0, 48), -512, None, A.add); ts(V("pk", 96, 108), V("pos", 0, 12), 308, None, A.add)
    ts(V("pk", 128, 152), V("pos", 0, 24), 500.5, None, A.add)
    scl(M("t1"), M("I"), E(10)); scl(M("t2"), M("I"), E(11))
    mm([(V(P3, 0, 384), M("t1"), V("lo8", 0, 384)), (V(P3, 0, 384), M("t2"), V("hi8", 0, 384))])
    for t in range(3):
        ts(pc("nm%d" % t), E(11), 49 + 12 * t, None, A.mult); plus(V("NM", 384 * t, 384 * t + 384), V(P3, 0, 384), pc("nm%d" % t))
    iota(V("Vf", 0, 768), [[1, 768]], 32)
    for k in range(16):
        eo = IND("EW", 0, 3456, V("EO", 24 * k, 24 * k + 24)); vf = V("Vf", 384 * (k % 2), 384 * (k % 2) + 384)
        either(eo, vf, lambda q, ap, eo=eo, vf=vf: q.tensor_copy(ap(eo), ap(vf)), lambda q, ap, eo=eo, vf=vf: q.activation(ap(eo), ap(vf), F.Silu))
    dma("s", [(lambda T, u=u: (S(T, "ZE", 96 * u, 96 * u + 96), S(T, "EW", 384 + 1536 * u, 1920 + 1536 * u, slice(0, 128, 16)))) for u in range(2)],
        [V("EW", 384, 3456)], [V("ZE", 0, 192)])
    for u, n_ in enumerate(("LA", "LB")): ts(V(n_, 0, 96), V("ZE", 96 * u, 96 * u + 96), 16, 0.25, A.max, A.add)
    zero("Zf", 384, [("ga", 1920, 2688)], 2500.0)

    sp = ((0, 512), (512, 576)); sq = ((0, 512), (512, 768)); late = []
    blank = lambda o: (o, V("Zr", 0, 128), V("Zr", 0, wid(o)))
    for t in range(3):
        Et = 1536 + 384 * t; last = t == 2
        n576 = lambda n: V(n, 0, 576)
        if t:
            pos_(n576("fil"), V("RR", 128, 704))
            mm(*[[(V(P1, a, b), M("N128"), V("ctr", 576 * u + a, 576 * u + b)) for u in range(t)] + [(V(P1, a, b), M("NHi"), V("fil", a, b))] for a, b in sp])
            relu(V("GD", 128, 704), V(P1, 0, 576), pc("ten"))
            inner()
        zero("Zr", 1536, [("Aux", 768, 6912)], 8000.0)
        kb = lambda u, B: V(P0, 512 * u + B, 512 * u + 384, 6)
        keys = lambda o, m_, first: mm(*[[(kb(u, B), V("RR", o + 128 * B, o + 128 * B + 128), half(M(m_), u)) for B in range(6)] for u in range(2)], first=first, final=False)
        for k in range(0 if t else 8):
            cp(V("G1", 768 * k, 768 * k + 768), IND("GD", 0, 800, V("W", 48 * k, 48 * k + 48)), "av"); c = 512 * (k // 4) + 96 * (k % 4)
            mm([(V(P0, c + B, c + 96, 6), V("G1", 768 * k + 128 * B, 768 * k + 128 * B + 128), V("SEL", 0, 16)) for B in range(6)], first=k % 4 == 0, final=False)
        keys(32, "SN", t > 0)
        if not t: keys(832, "SE", False); mm([blank(V(P0, 0, 8))], [blank(V(P0, 512, 520))], first=False)
        for B in range(6 if t else 0):
            if B == KEYS: keys(832, "SE", False)
            cp(V("G1", 1024 * B, 1024 * B + 1024), IND("GD", 0, 800, V("W", 64 * B, 64 * B + 64)), "av")
            mm(*[[(V(P0, 512 * u + 96 * k + B, 512 * u + 96 * k + 96, 6), V("G1", 1024 * B + 4 * u + k, 1024 * B + 1024, 8), V("SEL", 0, 16)) for k in range(4)] for u in range(2)],
               first=False, final=B == 5)
        mm([(V(P1, B, 96, 6), V(n_, o + 128 * B, o + 128 * B + 128), w_) for B in range(6)
            for n_, o, w_ in (("GD", 32, V("SEL", 0, 16)), ("RR", 1632, V("M", mn_["SN"], mn_["SN"] + 16)))])
        cp(V("OWN", 0, 96), V(P1, 0, 96), "av")
        for u in range(4): tt(V("KS", 0, 192), V(P0, 512 * (u // 2) + 192 * (u % 2), 512 * (u // 2) + 192 * (u % 2) + 192), V("KS" if u else "OWN", 0, 192), A.min)
        tt(V("KI", 0, 96), V("KS", 0, 96), V("KS", 96, 192), A.min)
        K1, K2 = V("KI", 0, 48), V("KI", 48, 96)
        ts(V("XI", 0, 48), K1, 11, 63, A.arith_shift_right, A.bitwise_and); ts(V("XI", 48, 96), K1, 7, 15, A.arith_shift_right, A.bitwise_and)
        tt(V("XR", 0, 96), V("XI", 0, 96), V("CX", 0, 96), A.add); ts(V("XR", 96, 192), V("XR", 0, 96), -1, None, A.add); ts(V("XR", 192, 384), V("XR", 0, 192), -2, None, A.add)
        for j in range(9): ts(V("OH", 384 * j, 384 * j + 384), a384("XR"), 4 * j, None, A.is_equal)
        hp = V(P1, 512, 548)
        mm([(hp, Z("0", i), V("GD", 128 + i, 704, 16)) for i in range(15)], final=False)
        mm([(V(P1, 512, 548, 1, (c // 12 * 32, c // 12 * 32 + 32)), V("OH", 48 + c, 3072, 96), V("OH", c, 3456, 96)) for c in range(48)] +
           [(hp, Z("0", 15), V("GD", 143, 704, 16))], first=False)
        ts(V("ch", 0, 36), hp, 11, None, A.is_equal)
        mm([(V(P1, 0, 36), M("Blk"), V("ch", 0, 36))]); mm([(V(P0, 0, 36), M("TriM"), V("ch", 0, 36))])
        scan(V("cc", 1, 37), V(P1, 0, 36), V("Zr", 0, 36), 500.0, A.add, A.max)
        tt(V("rkw", 0, 36), V(P0, 0, 36), V("cc", 0, 36), A.add)
        for c in range(6): act(V("junk", 48 * c, 48 * c + 36), V("cc", 1, 37), F.Sign, V("pk", 128 + c, 129 + c), -1.0, acc=V("vc", c, c + 1))
        ts(V("QL", 0, 6), V("vc", 0, 6), 0.5, 18, A.mult, A.add)
        tt(V("junk2", 0, 96), IND("rkw", 0, 37, V("QL", 0, 6)), V("id0", 0, 96), A.is_equal)
        ts(V("vd", 0, 6), V("vc", 0, 6), 8, 416, A.mult, A.add); ts(V("vd", 8, 14), V("vc", 0, 6), 35, None, A.is_lt); tt(V("vb", 0, 6), V("vd", 0, 6), V("vd", 8, 14), A.mult)
        mm([(V(P1, 0, 6), Z("ir", i), V("junk2", i, 96, 16)) for i in range(16)] + [(V(P1, 0, 6), M("I"), V("vb", 0, 6))])
        for u in range(2): ts(V("VL", 6 * u, 6 * u + 6), V(P1, 0, 6), 1600 * u, None, A.add)
        ts(V("AI", 0, 48), K1, 7, 1023, A.arith_shift_right, A.bitwise_and); ts(V("AI", 48, 96), K1, 127, None, A.bitwise_and); ts(V("AI", 96, 144), K2, 31, None, A.bitwise_and)
        cp(V("AE", 0, 48), V("AI", 0, 48)); ts(V("e1", 0, 48), V("AI", 48, 96), 32, -1400, A.mult, A.add); tt(V("AE", 48, 96), V("e1", 0, 48), V("AI", 96, 144), A.add)
        mm([blank(V(P2, 0, 432))], final=False)
        for g in range(8):
            mm([(V(P2, j, 432, 8, (g // 2 * 32, g // 2 * 32 + 32)), V("SW", 32 * j + 16 - g % 2 * 16, 32 * j + 48 - g % 2 * 16), V("AE", 6 * g, 6 * g + 54)) for j in range(8)] +
               [blank(V(P2, 0, 48))] * (g == 7), first=False, final=g == 7)
        cp(V("AO", 0, 48), V(P2, 0, 48)); ts(V("AO", 48, 96), V(P2, 384, 432), 1400, None, A.add)
        ts(V("cw", 0, 36), V("rkw", 0, 36), 95.5, None, A.is_lt); tt(V("cn", 0, 36), V("cw", 0, 36), V("pk", 0, 36), A.mult)
        ct = lambda a, b: V("ctr", 576 * t + a, 576 * t + b)
        for u in range(2):
            o = V(P2, 512 * u, 512 * u + 288)
            mm([(V(P2, 512 * u + i, 512 * u + 288, 16), V("BR", 128 * i, 128 * i + 128), V("cn", 18 * u, 18 * u + 18)) for i in range(16)])
            plus(V("TG", 128 + 288 * u, 416 + 288 * u), o, pc("m1k")); pos_(ct(288 * u, 288 * u + 288), o)
        if not FIRST[t]: cp(V("Rv", 0, 192), IND("RR", 0, 2400, V("VL", 0, 12)))
        for f in late: f()
        late.clear()
        if FIRST[t]: cp(V("Rv", 0, 192), IND("RR", 0, 2400, V("VL", 0, 12)))
        mm(wrap(V(P0, 0, 48), "Rv", 0, 96)); cp(V("UL", 0, 48), V(P0, 0, 48))
        ts(V("fv", 0, 96), V("Rv", 0, 96), 1, None, A.is_ge)
        for u in range(2): cp(V("G", 384 * u, 384 * u + 384), IND("RR", 0, 800, V("UL", 24 * u, 24 * u + 24)), "av")
        cp(V("Lu", 0, 768), IND("xw", 0, 2720, V("AO", 48, 96)), "av"); scl(V("Lu", 768, 1536), V("Lu", 0, 768))
        parts(cp, SPL[0], V("Aw", 32, 800), IND("TG", 0, 800, V("AO", 0, 48)), "av")
        relu(V("Bw", 32, 800), V("Aw", 32, 800))
        for u in range(2):
            a, b = 384 * u, 384 * u + 384; o = V(P2, 512 * u, 512 * u + 384)
            mm([(o, M("Wk"), V("RR", 32 + a, 32 + b)), (o, M("N128"), a384("c8"))]); tt(V("clr", a, b), o, V("Aw", 32 + a, 32 + b), A.is_equal)
        plus_dma(V("Aw", 32, 800), V("Lu", 0, 768)); plus_dma(V("Bw", 32, 800), V("Lu", 768, 1536))
        for kb_, o_ in (("Kn", 32), ("Ke", 832)):
            for u in range(2):
                a, b = 384 * u, 384 * u + 384; o = V(P2, 512 * u, 512 * u + 384)
                mm([(o, M("I"), V("RR", o_ + a, o_ + b)), (V(P2, 512 * u + 96 - 96 * u, 512 * u + 384 - 96 * u), M("N128"), ct(288 * u, 288 * u + 288)), (o, M("N128"), V("clr", a, b))])
                relu(V(kb_, a, b), o)
        for n_, (it, a) in enumerate([(it, a) for a in (0, 384) for it in (0, 1, 2)]):
            Pn, c = (P1, P0)[n_ // 2 % 2], n_ % 2 * 512; rv = V("Rv", a // 8 + 96 * (it == 2), a // 8 + 48 + 96 * (it == 2))
            mm([(V(Pn, c + j, c + 384, 8), M("NV") if it == 2 else M("N%d" % ((j + 2 * it + 1) % 8)), rv) for j in range(8)], final=False)
            mm([(V(Pn, c, c + 384), M("W2" if it == 2 else "Wc"), V("G", a, a + 384))], first=False)
            eq(V("EQ", 768 * it + a, 768 * it + a + 384), V(Pn, c, c + 384), 0, 0.0)
        for b in range(2):
            mm([(V(P0, 96 * b, 96 * b + 96), X(b), V("fv", 0, 96))] + [(V(P0, 96 * b, 96 * b + 96), Z("Y2", j), V("EQ", 768 * b + j, 768 * b + 768, 8)) for j in range(8)])
        relu(V("wish", 0, 192), V(P0, 0, 192), pc("m1"))
        mm([(V(P0, 512, 608), Z("all", j), V("EQ", 1536 + j, 2304, 8)) for j in range(8)])
        nf, po = V("nf", 0, 96), V(P0, 512, 608)
        either(nf, po, lambda q, ap: q.tensor_scalar(ap(nf), ap(po), -1.0, ap(pc("l64")), A.mult, A.add),
               lambda q, ap: q.activation(ap(nf), ap(po), F.Identity, bias=ap(pc("l64")), scale=-1.0), [pc("l64")])
        codes = lambda c: [(V(P1, c + 192 * e + b, c + 192 * e + 192, 2), X(2 + 4 * sb + 2 * e + b), V("wish", 96 * sb, 96 * sb + 96)) for e in range(2) for b in range(2) for sb in range(2)]
        mm([(V(P1, 512 + 192 * e + b, 704 + 192 * e, 2), X(10 + 2 * e + b), nf) for e in range(2) for b in range(2)], final=False)
        mm(codes(512), first=False); mm(codes(0)); cp(V("Nw", 2, 386), V(P1, 0, 384), "av")
        ts(V("fw", 0, 384), V(P1, 512, 896), -0.5, None, A.is_lt); tt(V("ok", 0, 192), V("fw", 0, 192), V("fw", 192, 384), A.mult)
        mm([(V(P0, 512, 704), M("Blk"), V("ok", 0, 192))]); mm([(V(P0, 0, 192), M("TriM"), V("ok", 0, 192))])
        mm([(V(P1, 512, 524), Z("all", i), V("ok", i, 192, 16)) for i in range(16)]); ts(V("s2", 0, 12), V(P1, 512, 524), 0.5, None, A.is_gt)
        scan(V("cumb", 1, 193), V(P0, 512, 704), V("Zr", 0, 192), 500.0, A.add, A.max)
        scan(V("ws", 0, 192), V("big", 0, 192), V("cumb", 0, 192), 0.0, A.add, A.min); tt(V("s2", 16, 28), V("s2", 0, 12), V("ws", 15, 192, 16), A.mult)
        tt(V("s2", 32, 44), V("s2", 16, 28), V("pk", 96, 108), A.max); ts(V("ZL", 0, 12), V("s2", 32, 44), -308, None, A.add)
        zero("Zr", 1536, [("Z", 192, 576)], 2500.0); cp(IND("Z", 0, 2880, V("ZL", 0, 12)), V("ids", 0, 192))
        zr = V("Z", 192, 576)
        scan(a384("mx"), zr, zr, 0.0, A.max, A.max); scan(a384("wr"), a384("big"), a384("mx"), 0.0, A.add, A.min)
        cp(V("CL", 0, 24), V("wr", 15, 384, 16)); CL = V("CL", 0, 24)
        tt(V("num", 2, 194), V(P0, 0, 192), V("cumb", 0, 192), A.add)
        tt(a384("oh"), IND("num", 0, 194, CL), a384("im"), A.is_equal)
        for e in range(2):
            tt(V("pr", 384 * e, 384 * e + 384), IND("Nw", 192 * e, 192 * e + 194, CL), a384("oh"), A.mult)
            mm([(V(P1, 512 * e, 512 * e + 24), Z("all", i), V("pr", 384 * e + i, 384 * e + 384, 16)) for i in range(16)])
        cp(V("j1", 0, 24), V("wr", 15, 384, 16)); ts(V("j1", 24, 48), V("j1", 0, 24), 510, None, A.bitwise_and)
        ts(V("s3", 0, 24), V("j1", 24, 48), 4, -8, A.mult, A.add); ts(V("s3", 24, 48), V("pk", 128, 152), V("cumb", 192, 193), 800, A.is_gt, A.mult)
        tt(V("s3", 48, 72), V("s3", 0, 24), V("s3", 24, 48), A.add)
        mm(*[[(V(P3, a, b), M("R0"), V("J8", a, b))] + [(V(P3, a + j, b, 8), M("U%d" % j), V("Rv", a // 8, b // 8)) for j in range(8)] for a, b in sq], final=False)
        mm(*[[(V(P3, a, b), M("CF"), V("EQ", 1536 + a, 1536 + b))] for a, b in sq], first=False)
        cp(V("W2", 0, 768), V(P3, 0, 768), "av")
        for e in range(2):
            w = (24 * e, 24 * e + 24)
            ts(V("j2", *w), V(P1, 512 * e, 512 * e + 24), 0.125, 7.625, A.mult, A.add); tt(V("s1", 48 + w[0], 48 + w[1]), V("s3", 48, 72), V("j2", *w), A.add); cp(V("IL", *w), V("s1", 48 + w[0], 48 + w[1]))
            ge = V("G2", 384 * e, 384 * e + 384); pe = V(P0, 512 * e, 512 * e + 384)
            cp(ge, IND("W2", 0, 1600, V("IL", *w)), "av")
            mm([(pe, M("NLo"), V("pr", 384 * e, 384 * e + 384))], final=False); mm([(pe, Z("lo", 0), ge)], first=False)
            eq(V("e2", 384 * e, 384 * e + 384), pe, 0, 0.0)
        o = V(P1, 0, 48)
        mm([(o, Z("u", i), V("G2", i, 768, 16)) for i in range(16)], final=False); mm([(o, Z("s", i), V("e2", i, 768, 16)) for i in range(16)], first=False)
        tt(V("s1", 0, 48), o, V("pk", 48, 96), A.max); ts(V("AL", 0, 48), V("s1", 0, 48), 512, None, A.add)
        for e in range(2):
            tt(IND("Aux", 0, 6912, V("AL", 24 * e, 24 * e + 24)), V("G2", 384 - 384 * e, 768 - 384 * e), V("NM", 384 * t, 384 * t + 384), A.add)
        ts(V("j3", 0, 48), o, 0.125, -0.4375, A.mult, A.add)
        nl = Et // 16
        cp(V("LA", nl, nl + 24), V("j3", 0, 24)); cp(V("LB", nl, nl + 24), V("j3", 24, 48))
        def fold(u, a, b, Pn, c):
            kb_, zz, o = (("Kn", "A", 32), ("Ke", "B", 832))[u]; po = V(Pn, c, c + b - a)
            mm([(po, M("I"), V(kb_, a, b))], final=False); mm([(po, Z(zz, s), V("Aux", 768 + 8 * a + s, 768 + 8 * b, 8)) for s in range(8)], first=False)
            cp(V("RR", o + a, o + b), po, "av")
        for x in FOLD[:4]: fold(*x)
        inner = lambda fold=fold: [fold(*x) for x in FOLD[4:]]
        if last: inner()
        done = 0
        for a in range(0, Et, 384):
            b = a + 384; z = a % 1536; zb, mk, rr = V("zb", z, z + 384), V("mk", z, z + 384), V("rl", a, b); xs = V("xw", 32 + a, 32 + b)
            scl(V("ga", a, b), IND("Aw", 0, 800, V("LA", a // 16, b // 16)))
            o = V(P2 if not last or a // 768 % 2 == 0 else P3, a // 384 % 2 * 512, a // 384 % 2 * 512 + 384)
            if a // 384 < DV[t]:
                gb = V("gb", a, b); cp(gb, IND("Bw", 0, 800, V("LB", a // 16, b // 16)), "av"); plus_dma(gb, V("ga", a, b))
                act(zb, gb, F.Abs); mm([(o, M("nI"), xs), (o, M("nI"), zb)])
            else:
                tt(zb, IND("Bw", 0, 800, V("LB", a // 16, b // 16)), V("ga", a, b), A.add)
                if a // 384 < ABS[t]: act(mk, zb, F.Abs); mm([(o, M("nI"), xs), (o, M("nI"), mk)])
                else: relu(mk, zb); mm([(o, M("nI"), xs), (o, M("I"), zb), (o, M("D2"), mk)])
            relu(rr, o); pos_(V("ix", a, b), rr)
            if a >= 384 * ACC[t]:
                mm([(o, M("I"), xs), (o, M("I"), rr)]); cp(xs, o, "av")
            elif b % 768 == 0 or b == 384 * ACC[t]:
                plus_dma(V("xw", 32 + done, 32 + b), V("rl", done, b)); done = b
        scl(V("ga", Et, Et + 384), IND("Aw", 0, 800, V("LA", nl, nl + 24)))
        tt(a384("zn"), IND("Bw", 0, 800, V("LB", nl, nl + 24)), V("ga", Et, Et + 384), A.add)
        ts(V("xw", 32 + Et, 416 + Et), a384("zn"), -1, -255, A.mult, A.max)
        pos_(V("ix", Et, Et + 384), a384("zn"))
        dma("s", [lambda T: (S(T, "own", 0, 168), S(T, "ga", 0, 2688, slice(0, 128, 16)))], [V("ga", 0, 2688)], [V("own", 0, 168)])
        if not last:
            mm(wrap(V(P0, 0, 384), "RR", 32, 800)); cp(V("W", 0, 384), V(P0, 0, 384))
        mm(*[wrap(V(P2, 48 * s, 48 * s + 48), "RR", 832 + 672 * s, 928 + 672 * s) for s in range(2)])
        cp(V("Eb", 0, 96), V(P2, 0, 96))

        def send(k, dr, src, dst, lat):
            add("g", (k, dr, src, dst), [src], [V("net", k, k + 1)], SEND if k else 2 * SEND, kind="send")
            add("r", (k, dr, src, dst), [V("net", k, k + 1)], [dst], 0.0, kind="recv", lat=lat)

        def spare(o, valid, name, base, u):
            a, b = V("s4", 48 * u, 48 * u + 24), V("s4", 48 * u + 24, 48 * u + 48)
            ts(a, valid, 0.5, base, A.is_gt, A.mult); tt(b, name, a, A.add); tt(a, b, V("pos", 0, 24), A.max); cp(o, a)
        o = V(P3, 0, 96)
        mm([(o, Z("W", 0), V("Ke", 672, 768)), (o, Z("W", 8), V("Kn", 672, 768))], final=False)
        mm([(o, Z("C", s), V("Aux", 6144 + s, 6912, 8)) for s in range(8)], first=False)
        tt(V("fl", 0, 96), o, V("slf", 0, 96), A.is_gt); ts(V("CT", 16, 112), o, pc("cb"), None, A.add)
        mm([(V(P3, 512, 608), M("Blk"), V("fl", 0, 96))])
        mm([(V(P3, 96, 102), Z("all", i), V("fl", i, 96, 16)) for i in range(16)], [(o, M("TR8"), V("fl", 0, 96))])
        scan(V("cs", 1, 97), V(P3, 512, 608), V("Zr", 0, 96), 500.0, A.add, A.max)
        ts(V("s5", 0, 6), V(P3, 96, 102), 0.5, None, A.is_gt); tt(V("PT", 16, 112), o, V("cs", 0, 96), A.add)
        scan(V("w5", 0, 96), V("big", 0, 96), V("cs", 0, 96), 0.0, A.add, A.min); tt(V("s5", 8, 14), V("s5", 0, 6), V("w5", 15, 96, 16), A.mult)
        tt(V("s5", 16, 22), V("s5", 8, 14), V("pk", 120, 126), A.max); ts(V("ZS", 0, 6), V("s5", 16, 22), -404, None, A.add)
        cp(IND("Zs", 480 * t, 480 * t + 480, V("ZS", 0, 6)), V("id16", 0, 96))
        zr = V("Zs", 480 * t + 96, 480 * t + 480)
        scan(a384("mx2"), zr, zr, 0.0, A.max, A.max); scan(a384("wr2"), a384("big"), a384("mx2"), 0.0, A.add, A.min)
        ka, kf = V("sk", 48 * t, 48 * t + 24), V("sk", 48 * t + 24, 48 * t + 48)
        cp(ka, V("wr2", 15, 384, 16))
        tt(a384("oh2"), IND("PT", 0, 112, ka), a384("im"), A.is_equal); tt(a384("cx"), IND("CT", 0, 112, ka), a384("oh2"), A.mult)
        pn_, pf_ = V(P3, 0, 24), V(P3, 512, 536)
        mm([(pf_, Z("uh", i), V("cx", i, 384, 16)) for i in range(16)]); mm([(pn_, Z("lh", i), V("cx", i, 384, 16)) for i in range(16)])
        cp(kf, pf_); ts(V("E2", 0, 24), pn_, 1360, None, A.add); spare(V("SS", 0, 24), kf, pn_, 2128, 0)
        send(4 * t, 1, V("sk", 48 * t, 48 * t + 48), V("lk", 48 * t, 48 * t + 48), LAT[0])
        cp(V("sy", 384 * t, 384 * t + 384), IND("xw", 0, 2720, V("E2", 0, 24)), "av")
        send(4 * t + 1, 1, V("sy", 384 * t, 384 * t + 384), V("ly", 384 * t, 384 * t + 384), LAT[1])
        cp(IND("PN", 0, 3488, V("SS", 0, 24)), V("RR", 1632, 2016)); cp(V("Go", 768, 1536), IND("PN", 768, 3488, V("Eb", 48, 96)), "av")
        o = V(P3, 0, 48); mm([(o, Z("a0", i), V("Go", 768 + i, 1536, 16)) for i in range(16)]); cp(V("PL", 0, 48), o)
        o = V(*MIDB)
        mm([(o, Z("all", i), V("ix", 168 * i, 168 * i + 168)) for i in range(16) if 168 * i < Et + 384])
        act(V("m3", 0, 168), V("own", 0, 168), F.Identity, pc("md%d" % t), -1.0 / 4096)
        ts(o, o, 8.5, None, A.is_ge); tt(V("m2", 0, 168), o, V("m3", 0, 168), A.mult); tt(V("mid", 0, 168), V("mid", 0, 168), V("m2", 0, 168), A.max)
        if last:
            ts(V("m1", 0, 168), V("mid", 0, 168), -12582912, None, A.add); ts(V("m1", 0, 168), V("m1", 0, 168), 1023, None, A.bitwise_and)
            ts(V("m3", 0, 168), V("m1", 0, 168), -32, None, A.add)
            dma("s", [lambda T: (T.ymid[:, :], S(T, "m3", 0, 168))], [V("m3", 0, 168)], [V("out", 0, 1)])

        def rows_out(Pn, a, b, pa, more=()):
            o = V(Pn, pa, pa + b - a)
            mm([(o, V("ZO", 64, 192), V("RR", 32 + a, 32 + b)), (o, V("ZO", 0, 128), V("RR", 832 + a, 832 + b))])
            ts(V("O", a, b), o, -32, -1, A.add, A.max)
        if last: rows_out(P0, 96, 384, 0); rows_out(P0, 384, 672, 512)
        la = V("lk", 48 * t, 48 * t + 24); yr = V("ly", 384 * t, 384 * t + 384); mn = V("s3m", 416 * t, 416 * t + 384); o = V(P2, 512, 896)
        cp(V("bb", 0, 24), V("lk", 48 * t + 24, 48 * t + 48)); cp(a384("Gn"), IND("RR", 16, 128, la), "av")
        mm([(V(P2, 512 + i, 896, 16), V("BR", 128 * i, 128 * i + 128), V("bb", 0, 24)) for i in range(16)], final=False); mm([(o, M("NWk"), a384("Gn"))], first=False)
        eq(a384("ohc"), o, -4096.0 * 31, pc("c31")); tt(a384("nm"), IND("RR", 816, 928, la), a384("ohc"), A.mult)
        o = V(P2, 512, 536)
        mm([(o, Z("aw", i), V("nm", i, 384, 16)) for i in range(16)])
        ts(V("E2", 24, 48), o, 16, None, A.max); spare(V("SS", 24, 48), o, o, 768, 1)
        tt(a384("dd"), IND("xw", 0, 2720, V("E2", 24, 48)), yr, A.subtract)
        ts(a384("pp"), a384("dd"), 0.5, None, A.is_gt); relu(a384("rs"), a384("dd")); ts(a384("pn"), a384("dd"), -0.5, None, A.is_lt)
        o = V(P3, 512, 536); mm([(o, Z("all", i), V("pp", i, 384, 16)) for i in range(16)]); ts(V("s3m", 416 * t + 384, 416 * t + 408), o, 8.5, None, A.is_ge)
        send(4 * t + 2, -1, V("s3m", 416 * t + 384, 416 * t + 408), V("l3m", 416 * t + 384, 416 * t + 408), LAT[0])
        if last:
            cp(mn, IND("xw", 0, 2720, V("E2", 24, 48)), "av"); send(4 * t + 3, -1, mn, V("l3m", 416 * t, 416 * t + 384), LAT[1]); mn = a384("Gn")
        o = V(P3, 0, 384); mm([(o, M("I"), yr)], final=False); mm([(o, M("I"), a384("rs"))], first=False); cp(mn, o, "av")
        if not last: send(4 * t + 3, -1, mn, V("l3m", 416 * t, 416 * t + 384), LAT[1])
        o = V(P3, 512, 896); mm([(o, M("Blk"), a384("pn"))]); act(V("sn", 0, 384), o, F.Sign, pc("p85"), -1.0)
        for s in range(2):
            if s:
                o = V(P3, 0, 384); mn = V("l3m", 416 * t, 416 * t + 384)
                mm([(V(P3, i, 384, 16), V("BR", 128 * i, 128 * i + 128), V("l3m", 416 * t + 384, 416 * t + 408)) for i in range(16)])
                cp(V("FR", 32, 416), o, "av"); parts(cp, SPL[0], V("Go", 768, 1536), IND("FR", 0, 416, V("PL", 0, 48)), "av")
                if last: tt(a384("dd"), mn, V("sy", 384 * t, 384 * t + 384), A.max); tt(IND("G1", 0, 3488, V("SS", 0, 24)), a384("dd"), a384("cm1"), A.mult)
                else: act(V("sn", 384, 768), o, F.Sign, pc("p85"), -1.0); tt(IND("xz", 0, 3488, V("SS", 0, 24)), mn, V("sn", 384, 768), A.mult)
            else:
                tt(IND("xz", 0, 3488, V("SS", 24, 48)), mn, V("sn", 0, 384), A.mult)
                parts(relu, SPL[0], V("Go", 0, 768), IND("xw", 0, 2720, V("Eb", 0, 48)))
                if last:
                    for a in range(0, 2688, 672): act(V("G1", 800 + a, 1472 + a), V("xw", 32 + a, 704 + a), F.Abs)


        def drop(s, u, Pn, c):
            o = V(Pn, c, c + 96); b = 32 + 800 * u + 672 * s
            mm([(o, M("I"), V("RR", b, b + 96))] + [(o, Z("2", k), V("Go", 768 * s + k, 768 * s + 768, 8)) for k in range(8)]); relu(V("RR", b, b + 96), o)
        if last:
            for s in range(2):
                drop(s, 0, P1, 0); drop(s, 1, P1, 512); rows_out(P0, 672 * s, 672 * s + 96, 512 * s)
        else:
            late.append(lambda drop=drop: [drop(*x) for x in ((0, 0, P3, 512), (1, 0, P3, 0), (0, 1, P3, 512), (1, 1, P3, 0))])
        if last:
            dma("s", [lambda T: (T.ylen[:, :], S(T, "G1", 800, 3488))], [V("G1", 800, 3488)], [V("out", 1, 2)], 4000.0)
            dma("a", [lambda T: (T.ynb[:, :], S(T, "O", 0, 768, slice(0, 64))), lambda T: (T.yen[:, :], S(T, "O", 0, 768, slice(64, 128)))], [V("O", 0, 768)], [V("out", 2, 3)], 3000.0)
    pre = len(ops)
    mset(pc("p85"), 8.5)
    for n_, c_ in (("ten", 10), ("m1k", -1024), ("c31", 4096 * 31), ("one", 1), ("m1", -1),
                   ("md0", 12582912 + 1024), ("md1", 12582912 + 2048), ("md2", 12582912 + 3072)): iota(pc(n_), [[0, 1]], c_)
    return ops[pre:] + ops[:pre]


def span(v):
    a, b = v[1], v[2]
    if v[0] in ("P0", "P1", "P2", "P3"):
        return v[0], a // 512 * 512, (b - 1) // 512 * 512 + 512
    if v[0] in LOC:
        return LOC[v[0]][0], a + LOC[v[0]][1], b + LOC[v[0]][1]
    return v[0], a, b


def depend():
    ops = program(); hist = {}
    for i, o in enumerate(ops):
        dep = {}; uses = set([(span(v), False, v[0] in SB) for v in o["rd"]] + [(span(v), True, v[0] in SB) for v in o["wr"]])
        for (nm, a, b), w, sb in uses:
            ps = not sb and nm[0] == "P"
            for (j, c, d, ww) in hist.get(nm, []):
                if d <= a or b <= c: continue
                if ww or w: dep[j] = True
                elif ps: dep[j] = dep.get(j, False)
        for v in o["wr"]:
            nm, a, b = span(v)
            if (not v[4] and v[3] == 1 and v[0] in SB) or nm[0] == "P":
                hist[nm] = [x for x in hist.get(nm, []) if not (a <= x[1] and x[2] <= b)]
        for (nm, a, b), w, sb in sorted(uses): hist.setdefault(nm, []).append((i, a, b, w))
        o["dep"] = dep
    return ops


def plan():
    ops = depend(); n = len(ops)
    succ = [[] for _ in ops]
    for i, o in enumerate(ops):
        for j in o["dep"]: succ[j].append(i)
    pred = [list(o["dep"]) for o in ops]
    lat = [o["lat"] for o in ops]; pe = [o["engs"] == "p" for o in ops]
    how = [[(e, o.get("ca", o["cost"]) if e == "a" else o["cost"]) for e in o["engs"]] for o in ops]

    def place(pri, before, after, fixed, bias):
        busy = {e: [] for e in "vapgsr"}; t0 = [0.0] * n; fin = [0.0] * n; eng = [None] * n; why = [-1] * n; rdy = [0.0] * n
        left = [len(x) for x in before]; ready = [i for i in range(n) if not left[i]]; back = before is succ
        while ready:
            i = max(ready, key=lambda k: pri[k]); ready.remove(i)
            rt = rdy[i] + lat[i] if back else rdy[i]; best = None
            for ec in ([fixed[i]] if fixed else how[i]):
                s = rt; c = ec[1]; bz = busy[ec[0]]; at_ = m = len(bz); by = -1
                while at_ and bz[at_ - 1][1] > s: at_ -= 1
                while at_ < m and s + c > bz[at_][0]:
                    if bz[at_][1] > s: s = bz[at_][1]; by = bz[at_][2]
                    at_ += 1
                key = s + c + bias[i] if ec[0] == "v" else s + c
                if best is None or key < best[0]: best = (key, s, ec, at_, by)
            _, s, ec, at_, by = best
            busy[ec[0]].insert(at_, (s, s + ec[1], i)); t0[i] = s; f = fin[i] = s + ec[1] if back else s + ec[1] + lat[i]; eng[i] = ec
            if by >= 0: why[i] = -2 - by
            for j in after[i]:
                left[j] -= 1; x = f if pe[i] and pe[j] else f + SY
                if x > rdy[j]: rdy[j] = x; why[j] = i
                if not left[j]: ready.append(j)
        return max(fin), t0, eng, pri, bias, fin, why
    pri = [0.0] * n
    for i in range(n - 1, -1, -1):
        pri[i] = ops[i]["cost"] + lat[i] + SY + max([pri[j] for j in succ[i]] + [0.0])
    def lift(p, x, up, t0, since):
        todo = [x]; got = {x}
        while todo:
            j = todo.pop(); p[j] += up
            for k in pred[j]:
                if k not in got and t0[k] > since: got.add(k); todo.append(k)
    top = None; zero = [0.0] * n
    for bias in BIASES:
        p = pri
        for _ in range(PASSES):
            cur = place(p, pred, succ, None, [bias] * n)
            for name, nth, up, span_ in EARLY:
                p = list(cur[3]); x = [i for i, o in enumerate(ops) if o["wr"][0][0] == name][nth]; lift(p, x, up, cur[1], cur[1][x] - span_)
                new = place(p, pred, succ, None, [bias] * n)
                if new[0] < cur[0] + 1000.0: cur = new
            if top is None or cur[0] < top[0]: top = cur
            p = place(cur[5], succ, pred, cur[2], zero)[5]
    far = [1.0 if o["kind"] == "c" else 1.5 for o in ops]; wake = [[(j, 0.0 if pe[i] and pe[j] else SY) for j in pred[i]] for i in range(n)]
    slow = [1.0 if o["kind"] != "c" else 1.3 * (1.35 if any(v[4] for v in o["wr"]) else 1.2 if any(v[4] for v in o["rd"]) else 1.0) for o in ops]

    def again(x):
        free = dict.fromkeys("vapgsr", 0.0); fin = [0.0] * n; fre2 = dict(free); fi2 = [0.0] * n
        for i in sorted(range(n), key=lambda k: x[1][k]):
            e, c = x[2][i]; s = free[e]; u = fre2[e]
            for j, w in wake[i]:
                if fin[j] + w > s: s = fin[j] + w
                if fi2[j] + w > u: u = fi2[j] + w
            free[e] = s = s + c * slow[i]; fin[i] = s + lat[i]
            fre2[e] = u = u + c * far[i]; fi2[i] = u + 1.7 * lat[i]
        return (x[0] + WEIGHT * (max(fin) + max(fi2)),) + x[1:]
    rs = np.random.RandomState(SEED); cur = top = again(top)
    for it in range(TRIES):
        i = max(range(n), key=lambda k: cur[5][k]); held = []
        while i != -1:
            j = cur[6][i]
            if j < -1: j = -2 - j; held.append((j, i))
            i = j
        p = list(cur[3]); bias = list(cur[4])
        if held and rs.uniform() < LIFT:
            x = held[rs.randint(len(held))][rs.randint(2)]; lift(p, x, rs.uniform(500, 8000), cur[1], cur[1][x] - rs.uniform(3000, 30000))
        elif held and rs.uniform() < MOVE:
            for _ in range(rs.randint(1, 4)):
                x, y = held[rs.randint(len(held))]
                if len(how[x]) > 1 and rs.uniform() < 0.5: bias[x] = 1e5 if cur[2][x][0] == "v" else -1e5
                elif len(how[y]) > 1 and rs.uniform() < 0.3: bias[y] = 1e5 if cur[2][y][0] == "v" else -1e5
                else: p[x] = min(p[x], p[y]) - rs.uniform(0, 3000)
        else:
            c0 = rs.uniform(0, max(cur[5])); w = rs.uniform(2000, 15000); z = rs.uniform(-1, 1, n) * rs.choice([300.0, 1000.0, 3000.0]) * (rs.uniform(0, 1, n) < 0.3)
            p = [x + float(y) if abs(t - c0) < w else x for x, y, t in zip(p, z, cur[1])]
        new = place(p, pred, succ, None, bias)
        if rs.uniform() < 0.1: new = place(place(new[5], succ, pred, new[2], zero)[5], pred, succ, None, bias)
        if new[0] > max(cur[5]) + 1500.0: continue
        new = again(new)
        if new[0] <= cur[0] + HEAT * (1 - it / TRIES) * rs.exponential(): cur = new
        if cur[0] < top[0]: top = cur
    for i, o in enumerate(ops): o["t0"] = top[1][i]; o["e"] = top[2][i][0]; o["pri"] = pri[i]
    return ops, sorted(range(n), key=lambda i: (top[1][i], i)), (max(top[5]), top[0])


PLAN = []


def rank_program(g, core, T, topo):
    rank = T.rank_of(core)
    if rank is None:
        return
    if not PLAN: PLAN.append(plan())
    ops, order, _ = PLAN[0]
    Q = dict(v=g.vector, a=g.scalar, p=g.tensor, g=g, s=g.sync)

    steps = [0]

    def step(ins):
        steps[0] += 1; ins.then_inc(T.sem.ax, 1); g.scalar.wait_ge(T.sem.ax, steps[0])

    ap = lambda v: make_ap(T, v, step)
    at = {i: k for k, i in enumerate(order)}; seen = {e: {} for e in Q}; waits = {}; need = set()
    for i in order:
        o = ops[i]; e = o["e"]; waits[i] = []
        if e == "r": continue
        best = {}
        for j, hard in o["dep"].items():
            d = ops[j]; key = d["e"] if d["kind"] == "c" else j
            if d["kind"] == "c" and d["e"] == e and (e == "p" or not hard): continue
            if key not in best or at[j] > at[best[key]]: best[key] = j
        for key, j in best.items():
            if seen[e].get(key, -1) >= at[j]: continue
            seen[e][key] = at[j]; waits[i].append(j); need.add(j)
    token = {}; cnt = {e: 0 for e in "vapg"}; nd = 0; tail = []
    n = len(T.cores)
    for i in order:
        o = ops[i]; e = o["e"]
        if o["kind"] == "recv":
            token[i] = (T.sem["r%d" % o["fn"][0]], len(topo.engines(T.cores[(rank - o["fn"][1]) % n], core))); continue
        q = Q[e]
        for j in waits[i]: q.wait_ge(*token[j])
        if o["kind"] == "c":
            ins = o["fn"](q, e, ap)
            if i in need:
                cnt[e] += 1; ins.then_inc(T.sem["e" + e], 1); token[i] = (T.sem["e" + e], cnt[e])
        elif o["kind"] == "d":
            sem = T.sem["d%d" % nd]; nd += 1
            for f in o["fn"]:
                z = f(T); q.dma_start(z[0], z[1], **(z[2] if len(z) > 2 else {})).then_inc(sem, 16)
            token[i] = (sem, 16 * len(o["fn"]))
            if i not in need: tail.append(token[i])
        else:
            m, dr, src, dst = o["fn"]; d = T.cores[(rank + dr) % n]; rid, pid = topo.addr(d, core)
            g.remote_dma(ap(dst), ap(src), T.sem["r%d" % m], T.sem["l%d" % m], pid, rid, topo.mask(core, d))
            tail.append((T.sem["l%d" % m], len(topo.engines(core, d))))
    for tk in tail: g.wait_ge(*tk)
